import numpy as np, ml_dtypes
CORES = [40,41,42,43,44,45,46,47]
N = 8
BF = ml_dtypes.bfloat16
E, V, L, ST, OF, BL, RO, M = 3072, 512, 256, 12, 5, 8, 3, 12
NONE = E - 1; B = L // BL; KM = 31 * 16 * (63 + M)
def ring(rng, pm, n, dl, dense):
    x = np.repeat(np.arange(n), 8); z = (x + np.tile(dl, n)) % n
    first = (x < dense * n) & (rng.random(8 * n) < 0.97)
    o = rng.permutation(np.argsort(rng.random(8 * n) - first)[:E - 1])
    return pm[x[o]], pm[z[o]]
def fill_rows(rng, a, b):
    h = np.concatenate([a, b]); ids = np.concatenate([np.arange(E - 1), np.arange(E - 1)])
    o = rng.permutation(2 * (E - 1)); h = h[o]; ids = ids[o]
    o = np.argsort(h, kind="stable"); h = h[o]; ids = ids[o]
    place = np.arange(2 * (E - 1)) - np.searchsorted(h, h)
    k = np.argsort(rng.random((V, 16)), axis=1)[h, place]
    out = np.full((16, V), NONE); out[k, h] = ids
    return out
def pack(rng, y, a, b, th):
    en = np.zeros((N, 8, E), np.int32); en[:, :, :E - 1] = 1024 * np.minimum(a, b) + np.maximum(a, b)
    ne = np.stack([np.concatenate([fill_rows(rng, a[r, g], b[r, g]) for g in range(8)]) for r in range(N)]).astype(np.int32)
    return {"y0": y.reshape(N, 128, E).astype(np.float32).astype(BF), "ends0": en, "ne0": ne, "th": np.ascontiguousarray(np.reshape(th, (N, 8, 1))).astype(np.int32)}
def levels(rng):
    return np.clip(rng.integers(0, 64, (N, 8, 1, E)) + rng.integers(-12, 13, (N, 8, 16, E)), 0, 63)
def blank():
    return np.zeros((N, 8, E - 1), np.int64), np.zeros((N, 8, E - 1), np.int64)
def numbers(rng, at, forced):
    num = np.full(E - 1, -1); num[at] = forced
    num[num < 0] = rng.permutation(np.setdiff1d(np.arange(E - 1), forced))
    return num
def setup_inputs(rng):
    a, b = blank()
    for g in range(8):
        pm = rng.permutation(V)
        for r in range(N): a[r, g], b[r, g] = ring(rng, np.roll(pm, rng.integers(0, V)), V, rng.integers(1, 10, 8), 0.2)
    return pack(rng, levels(rng), a, b, rng.integers(300, 1801, (N, 8)))
def setup_inputs_spread(rng):
    a, b = blank()
    for g in range(8):
        pm = rng.permutation(V)
        for r in range(N): a[r, g], b[r, g] = ring(rng, pm, int(rng.integers((E + 6) // 8 + 8, V + 1)), rng.integers(1, int(rng.integers(4, 16)), 8), 0.5 * rng.random())
    y = np.minimum((np.exp2(6 * rng.random((N, 8, 1, E))) * rng.random((N, 8, 16, E))).astype(np.int64), 63)
    return pack(rng, y, a, b, np.minimum(np.exp2(15.2 * rng.random((N, 8))).astype(np.int64) - 1, KM))
def setup_inputs_corners(rng):
    a, b = blank(); sh = int(rng.integers(0, 4)); flat = rng.permutation(8)[:3]
    y = levels(rng); y = np.where(rng.random((N, 8, 1, E)) < 0.4, 63 * rng.integers(0, 2, (N, 8, 1, E)), y)
    th = rng.choice(np.array([0, 1, 16 * M, 640, 1280, KM]), (N, 8))
    for g in range(8):
        pm = rng.permutation(V); one = int(rng.choice(np.array([0, 63, 20])))
        if g == flat[0]: one = 63
        for r in range(N):
            k = (g + r + sh) % 4; n = V; dl = rng.permutation(8) + 1; dense = 0.3
            if k == 0: n = min(V, (E + 6) // 8 + int(rng.choice(np.array([0, 2, 6]))))
            if k == 1: dl = np.array([1, 1, 1, 1, 2, 2, 2, 2])
            if k == 3: dl = np.array([1, 1, 1, 1, 1, 1, 1, 1]); dense = 0.1
            a[r, g], b[r, g] = ring(rng, pm, n, dl, dense)
            if g in flat: y[r, g] = one; th[r, g] = 16 * M * int(rng.integers(0, 12))
    return pack(rng, y, a, b, th)
def setup_inputs_crowd(rng):
    a, b = blank(); sh = int(rng.integers(0, 4)); y = rng.integers(1, 64, (N, 8, 16, E)); th = rng.choice(np.array([0, 1, 300]), (N, 8))
    off = np.arange(E - 1); off = off[(off % ST > 0) & (off % ST != OF)]
    for g in range(8):
        kind = (g + sh) % 4; c0 = np.arange(g % 2, V, 2); c1 = np.arange(1 - g % 2, V, 2)
        tri = rng.permutation(c0[B:])[:3]; lo = int(rng.integers(0, 11)); came = (B, B - 1, 1, 2)[kind] & (B - 1)
        for r in range(N):
            u = rng.permutation(c0[:B]); p = rng.permutation(np.setdiff1d(c0[B:], tri))[:B]; v = rng.permutation(c1[V // 2 - B:])
            o = rng.permutation(c1[:V // 2 - B])
            if g % 2 == 1: o = np.concatenate([np.zeros(1, np.int64), o[o != 0]])
            s = np.array(o[:B]); w = o[B:2 * B]; j = int(rng.integers(1, B))
            if kind == 1: s[j] = s[j - 1]
            if kind >= 2:
                lu, ls = int(u[B - 1]), int(s[B - 1]); u = u[np.arange(B) // 14]; s[:] = s[0]
                if kind == 3: u[j] = lu; s[j] = ls
            k = np.unique(u, return_index=True)[1]; n3 = 2 * B + len(k)
            fa = np.concatenate([u, p, u[k], np.repeat(tri, 8)]); fb = np.concatenate([v, w, s[k], np.repeat(np.roll(tri, -1), 8)])
            cap = 16 - np.bincount(np.concatenate([fa, fb]), minlength=V); cap[v] -= 1; cap[np.unique(s)] -= 1
            more = E - 1 - len(fa)
            ea = np.concatenate([fa, rng.permutation(np.repeat(c0, cap[c0]))[:more]]); eb = np.concatenate([fb, rng.permutation(np.repeat(c1, cap[c1]))[:more]])
            block = ST * (BL * int(rng.integers(0, B)) + np.arange(BL)) + OF
            forced = np.concatenate([ST * BL * np.arange(B), ST * (BL * np.arange(B) + BL - 1), block, rng.permutation(off)[:24 - BL]])
            num = numbers(rng, np.concatenate([np.arange(2 * B), n3 + np.arange(24)]), forced)
            a[r, g][num] = ea; b[r, g][num] = eb
            y[r, g][:, num[2 * B:n3]] = 0
            up = int(rng.integers(8, 51)); y[r, g][:, num[n3:n3 + 24]] = lo; y[r, g][:, block] = lo + up
            if kind == 1 or r % 2 == 1:
                over = 0 if kind == 0 else 1 if r == 1 else int(rng.choice(np.array([0, 1, 8])))
                th[r, g] = 256 * (up + M) + over - 8 * came
    return pack(rng, y, a, b, th)
def setup_inputs_ends(rng):
    a, b = blank(); y = 63 * rng.integers(0, 2, (N, 8, 16, E)); Q = V // 4; R = E - 1 - 18 * Q
    forced = [0, ST, ST * (L - 2), ST * (L - 1)]
    for t in range(1, RO): forced += [OF * t, ST * (L - 1) + OF * t]
    forced = np.array(forced); FO = len(forced)
    th = (np.arange(N)[:, None] + np.arange(8)[None, :] + N + 1) % 2; th[:, :4] = rng.integers(0, 2, (N, 4))
    for g in range(8):
        pm = rng.permutation(np.arange(2, V - 2)); rest = pm[4:].reshape(-1, 4)
        quad = np.concatenate([np.array([[pm[0], V - 2, V - 1, pm[1]], [0, pm[2], 1, pm[3]]]), np.concatenate([np.sort(rest[:, :2], axis=1), rest[:, 2:]], axis=1)])
        u, v, s, w = rng.permutation(quad).T
        calm = (np.arange(Q) // N < FO) | (rng.random(Q) < 0.5)
        for r in range(N):
            home = np.arange(Q) % N == r
            qa = np.stack([u] * 16 + [v] * 2, axis=1).reshape(-1); qb = np.stack([np.where(home, v, w)] + [s] * 8 + [w] * 7 + [s, w], axis=1).reshape(-1)
            ea = np.concatenate([qa, rng.permutation(np.repeat(v[0::2], 13))[:R]]); eb = np.concatenate([qb, rng.permutation(np.repeat(v[1::2], 13))[:R]])
            num = numbers(rng, 18 * np.flatnonzero(home)[:FO], forced)
            a[r, g][num] = ea; b[r, g][num] = eb; yy = y[r, g]
            yy[:, num[(18 * np.flatnonzero(calm)[:, None] + np.arange(18)).reshape(-1)]] = 0
            yy[:, num[18 * np.flatnonzero(calm & home)]] = 63
            yy[:, num[18 * Q:]] = 63 * rng.integers(0, 2, R)[None, :]
    return pack(rng, y, a, b, KM * th)
def setup_inputs_again(rng):
    a, b = blank(); y = levels(rng); th = rng.integers(300, 3001, (N, 8)); sh = int(rng.integers(0, 2)); tr = V // 6; h = (V - 6 * B) // 2
    i = np.arange(L); mid = i[(i % BL > 0) & (i % BL < BL - 1)]; m = len(mid); at = ST * BL * np.arange(B); la = ST * (BL - 1)
    forced = np.concatenate([at, at + la, at + OF, at + la + OF, ST * mid + OF])
    folds = np.array([[15, 1, 1], [13, 2, 2], [11, 4, 4], [9, 6, 6]])
    for g in range(8):
        pm = rng.permutation(V); low = rng.permutation(2 * B); high = V - 2 * B + rng.permutation(2 * B); rest = 2 * B + rng.permutation(V - 4 * B)
        for r in range(N):
            if (g + sh) % 2 == 0:
                u, uu = rng.permutation(low[:B]), rng.permutation(low[B:]); v, vv = rng.permutation(high[:B]), rng.permutation(high[B:])
                s, ss = rng.permutation(rest[:B]), rng.permutation(rest[B:2 * B])
                c0 = np.concatenate([u, vv, ss, rest[2 * B:2 * B + h]]); free = np.concatenate([uu, rest[2 * B + h:]]); moved = np.concatenate([v, s])
                fa = np.concatenate([u, u, vv, ss]); fb = np.concatenate([v, s, uu, uu])
                cap = np.full(V, 16); cap[np.concatenate([v, s, vv, ss])] = 15; cap = cap - np.bincount(np.concatenate([fa, fb]), minlength=V)
                x = rng.permutation(np.repeat(c0, cap[c0])); z = rng.permutation(np.repeat(free, cap[free]))
                z = np.concatenate([z[:m], rng.permutation(np.concatenate([z[m:], np.repeat(moved, cap[moved])]))])
                more = E - 1 - 4 * B; num = numbers(rng, np.arange(4 * B + m), forced)
                a[r, g][num] = np.concatenate([fa, x[:more]]); b[r, g][num] = np.concatenate([fb, z[:more]])
                y[r, g] = rng.integers(16, 64, (16, E))
                y[r, g][:, np.concatenate([num[B:2 * B], num[3 * B:4 * B]])] = rng.integers(0, 12, (16, 2 * B))
                th[r, g] = 0 if r < 2 else int(rng.integers(0, 2))
            else:
                c = folds[rng.integers(0, 4, tr)]; tri = np.take_along_axis(pm[:3 * tr].reshape(tr, 3), np.argsort(rng.random((tr, 3)), axis=1), 1)
                qa = np.concatenate([np.repeat(tri[:, j], c[:, j]) for j in range(3)]); qb = np.concatenate([np.repeat(tri[:, (j + 1) % 3], c[:, j]) for j in range(3)])
                n = V - 3 * tr; o = rng.permutation(8 * n)[:E - 1 - len(qa)]; dl = rng.integers(1, 10, 8); ot = pm[3 * tr:]
                ea = np.concatenate([qa, ot[o // 8]]); eb = np.concatenate([qb, ot[(o // 8 + dl[o % 8]) % n]])
                num = rng.permutation(E - 1)
                a[r, g][num] = ea; b[r, g][num] = eb
    return pack(rng, y, a, b, th)
def check_inputs(d):
    bad = []
    for k, lo, hi in (("y0", 0, 63), ("ends0", 0, 1024 * (V - 2) + V - 1), ("ne0", 0, NONE), ("th", 0, KM)):
        x = np.asarray(d[k]).astype(np.float64)
        if not (np.min(x) >= lo and np.max(x) <= hi): bad.append("range of " + k)
        elif np.any(x != np.floor(x)): bad.append("whole numbers in " + k)
    if bad: return bad
    en = np.asarray(d["ends0"]).astype(np.int64); u = en >> 10; w = en & 1023; ne = np.asarray(d["ne0"]).astype(np.int64).reshape(N, 8, 16, V)
    if np.any(en[:, :, NONE] != 0): bad.append("ends0 of no edge")
    if np.any(u[:, :, :NONE] >= w[:, :, :NONE]) or np.any(w >= V): bad.append("ends of an edge")
    node = np.zeros((16, 1), np.int64) + np.arange(V)[None, :]
    for r in range(N):
        for g in range(8):
            m = ne[r, g] != NONE; e = ne[r, g][m]; c = node[m]; lo = c == u[r, g][e]; hi = c == w[r, g][e]
            if not np.all(lo | hi) or np.any(np.bincount(e[lo], minlength=E)[:NONE] != 1) or np.any(np.bincount(e[hi], minlength=E)[:NONE] != 1):
                bad.append("lists of rank %d, graph %d" % (r, g))
    return bad
def score(yx, nx, ux, wx, u, v, ye):
    a = np.take_along_axis(nx, u[:, None, :], 2); b = np.take_along_axis(nx, v[:, None, :], 2); both = ux + wx
    s = np.where(a == NONE, -1, np.take_along_axis(both, a.reshape(8, -1), 1).reshape(a.shape) - u[:, None, :])
    f = np.where(b == NONE, -2, np.take_along_axis(both, b.reshape(8, -1), 1).reshape(b.shape) - v[:, None, :])
    c = np.max(np.where(s[:, :, None, :] == f[:, None, :, :], b[:, None, :, :], -1), axis=2)
    ya = np.take_along_axis(yx, a.reshape(8, 1, -1), 2).reshape(8, 16, 16, L); yc = np.take_along_axis(yx, np.maximum(c, 0).reshape(8, 1, -1), 2).reshape(8, 16, 16, L)
    gain = np.sum(np.maximum(ye[:, :, None, :] + M - np.maximum(ya, yc), 0), axis=1)
    return np.sum(np.where(c >= 0, gain, 0), axis=1), a, s, c >= 0, np.sum(ya, axis=1)
def reference(y0, ends0, ne0, th):
    y = y0.astype(np.float32).astype(np.int32).reshape(N, 8, 16, E); en = ends0.astype(np.int64); u = en >> 10; w = en & 1023
    ne = np.array(ne0, np.int64).reshape(N, 8, 16, V); thr = th.astype(np.int64)[:, :, 0]; moves = np.zeros((N, 8), np.int64)
    low = np.tril(np.ones((B, B), bool), -1)[None]
    for t in range(RO):
        lane = ST * np.arange(L) + OF * t
        yn, un, wn, nn, mn = np.array(y), np.array(u), np.array(w), np.array(ne), np.array(moves)
        for r in range(N):
            q = (r + 1 + t) % N; lu, lv, ye = u[r][:, lane], w[r][:, lane], y[r][:, :, lane]
            kap, a, s, closed, tot = score(y[r], ne[r], u[r], w[r], lu, lv, ye)
            kap = kap + score(y[q], ne[q], u[q], w[q], lu, lv, ye)[0]
            up = kap >= (thr[r] + 8 * (moves[r] & (B - 1)))[:, None]
            yn[r][:, :, lane] = np.clip(ye + np.where(up, 1, -1)[:, None, :], 0, 63)
            kb = kap.reshape(8, B, BL); at = BL * np.arange(B)[None, :]
            el = at + np.argmin(kb, axis=2); d = lane[at + BL - 1 - np.argmax(kb[:, :, ::-1], axis=2)]; e = lane[el]
            a, s, closed, tot = [np.take_along_axis(x, el[:, None, :], 2) for x in (a, s, closed, tot)]
            v = np.take_along_axis(w[r], e, 1); p1 = np.take_along_axis(u[r], d, 1); p2 = np.take_along_axis(w[r], d, 1)
            ok = (a != NONE) & ~closed & (s != v[:, None, :]); has = np.any(ok, axis=1)
            k = np.argmin(np.where(ok, tot, 10 ** 6), axis=1)[:, None, :]
            s = np.maximum(np.take_along_axis(s, k, 1)[:, 0], 0); a = np.take_along_axis(a, k, 1)[:, 0]
            four = np.stack([s, v, p1, p2], axis=2)
            hit = np.any(four[:, :, None, :, None] == four[:, None, :, None, :], axis=(3, 4))
            clash = np.any(hit & has[:, None, :] & low, axis=2)
            fs = np.take_along_axis(ne[r], s[:, None, :], 2) == NONE; fv = np.take_along_axis(ne[r], v[:, None, :], 2) == NONE
            go = has & ~clash & np.any(fs, axis=1) & np.any(fv, axis=1)
            ks, kv = np.argmax(fs, axis=1), np.argmax(fv, axis=1)
            for g in range(8):
                i = np.flatnonzero(go[g]); dd, ss, vv = d[g, i], s[g, i], v[g, i]
                nn[r, g] = np.where(np.isin(nn[r, g], dd), NONE, nn[r, g])
                nn[r, g][ks[g, i], ss] = dd; nn[r, g][kv[g, i], vv] = dd
                un[r, g, dd] = np.minimum(ss, vv); wn[r, g, dd] = np.maximum(ss, vv)
                yn[r, g][:, dd] = (y[r, g][:, a[g, i]] + y[r, g][:, e[g, i]]) >> 1
                mn[r, g] += len(i)
        y, u, w, ne, moves = yn, un, wn, nn, mn
    return {"y1": y.reshape(N, 128, E).astype(np.float32).astype(BF), "ends1": (1024 * u + w).astype(np.float32), "ne1": ne.reshape(N, 128, V).astype(np.float32)}

@@ -1,0 +1,654 @@
+from concourse.bass import DstId, RemoteDMATransfer
+from concourse.mybir import AluOpType, AxisListType, ActivationFunctionType
+
+A = AluOpType
+AF = ActivationFunctionType
+N, RO = 8, 3
+L = 128
+CH = [(0, 64), (64, 128), (128, 256), (256, 384), (384, 448), (448, 512)]
+PRE = [(0, 64), (64, 256), (256, 512)]
+PLAN = ("O0 P0 Q0 D01 P1 P2 Q1 D00 A01 O2 A00 O1 Y00v D10 D11 S0 Y21a A10 D20 Q2 X0 A11 D22 D23 A20 Z00 Y10a A23 D21 S1 A22 R00v Z01 D33 D30 "
+        "A21 D31 X1 Y20a U00 A33 A30 Z10 D32 S2 R01v Z11 A31 Y30a A32 R10a U01 D51 R11a D41 Y31a X2 Y50a Z20 Z22 R20a S3 D50 A51 A50 U10 U11 "
+        "T3 R22v Z21 R21a U20 D40 A41 Z23 A40 X3 U21 U22 R23a Z30 S5 Z31 R30a Y40a R31a S4 U23 Z32 U30 X5 R32a T5 T4 X4 Z33 U31 R33a U32 Z50 "
+        "Z40 R40v U33 R50a Z41 Z51 R51a U50 U40 R41v U41 U51")
+GPLAN = "vavavava"
+ND, NZ = 3, 2
+CEN = 256.0 * 18600
+BIGK = 10485760.0
+KEYMAX = 4800000.0
+BD = 8192.0
+LIM = 12000000.0
+SC2 = 1048576.0
+CC2 = 126976.0
+
+F32, BF, I32, U16, F16 = "float32", "bfloat16", "int32", "uint16", "float16"
+SB = {
+    "YW": (3136, BF), "W": (3088, BF), "ENR": (3136, F32), "SVC": (8, BF),
+    "EB": (192, I32), "EBF": (192, F32), "EI": (384, I32), "PC": (384, BF),
+    "NEI": (512, I32), "NEO": (512, U16), "NE": (640, F32), "FAR": (640, F32), "NOUT": (640, F32),
+    "G": (8192, BF), "RM": (16, F32), "SEL": (2048, BF), "SELH": (2048, F16), "RST": (16 * L, BF),
+    "OWN": (3 * 288, BF), "LAND": (3 * 288, BF), "UVO": (3 * 64, U16), "WL": (768, BF), "UV": (3 * 512, BF),
+    "KOUT": (3 * 256, F32), "KIN": (3 * 256, F32),
+    "AO": (512, U16), "CO": (512, U16), "SS": (512, BF), "X1": (512, BF), "X2": (512, F16),
+    "AB": (2 * 16 * L, F32), "MN": (2 * 16 * L, F32), "YA": (8192, BF), "MM": (8192, BF), "RR": (4 * 512, BF),
+    "PEN": (256, BF), "F2": (256, BF), "K2": (256, F32), "KEY": (256, F32), "SC": (512, F32),
+    "SG": (256, BF), "T2": (256, BF),
+    "IOT": (144, F32), "C3": (64, F32), "QG": (128, BF), "T16": (192, F32), "LI": (48, F32), "LID": (256, F32),
+    "BBI": (128, BF), "BB": (128, BF), "CX": (512, BF), "JJ": (256, BF), "BE": (144, BF),
+    "I1": (128, BF), "IN1": (128, BF), "IN8": (128, BF), "IBG": (128, BF), "I16": (128, BF),
+    "O1": (128, BF), "O256": (128, BF), "ONB": (128, BF), "OKW": (128, BF), "TRI": (128, BF),
+    "MMN": (128, BF), "MMX": (128, BF), "E1": (192, BF), "E2": (192, BF), "MD": (192, BF),
+    "PI": (8, I32), "CF": (32, F32), "LOFF": (48, U16), "POFF": (16, U16), "DUM": (10, F32), "C256": (4, F32),
+    "THI": (8, I32), "THF": (8, F32), "THB": (8, F32), "THM": (8, F32), "AC": (16, F32), "AI": (8, I32),
+    "Q": (16, I32), "OFF": (10, U16), "KE": (32, F32), "TT": (48, F32), "MV": (2, F32), "EQ": (32, BF), "SL": (32, BF),
+    "SE": (32, BF), "SX": (32, BF), "VP": (96, BF), "PS": (32, BF), "YE": (32, BF), "DD": (128, F32),
+    "WR": (192, F32), "WB": (8, F32), "NO": (10, U16), "AX": (1024, BF), "CM": (1024, BF),
+    "CN": (128, F32), "CR": (128, F32), "EM": (64, BF), "KP": (128, F32), "FM": (64, F32), "OT": (64, F32),
+    "M1": (64, F32), "M2": (64, F32), "N1": (128, F32), "N2": (128, F32),
+    "W2": (64, F32), "OK": (8, F32), "XF": (10, F32), "XP": (10, F32), "XM": (10, F32), "XN": (10, F32), "SO": (10, U16),
+    "YS": (32, F32), "YI": (32, I32), "LH": (96, F32), "GO": (2, BF),
+}
+SCRATCH = {k: ("sbuf", [128, w], d) for k, (w, d) in SB.items()}
+for _i in range(8):
+    SCRATCH["p%d" % _i] = ("psum", [128, 512], F32)
+SEMAPHORES = ["sv", "sa", "sp", "sg", "sent"] + ["d%d" % i for i in range(16)] + ["ln%d" % t for t in range(RO)] \
+    + ["kin%d" % i for i in range(RO * 4)]
+
+CYC, PCYC, GATH, SCAT, WAKE = 1.0, 0.5, 1.6, 3.5, 120.0
+
+
+def rank_program(g, core, T, topo):
+    rank = T.rank_of(core)
+    if rank is None:
+        return
+    ops = []
+    last_w, readers, bank_last = {}, {}, {}
+    masks = {}
+    boost, chain, tail = [0.0], [False], {}
+
+    def S(name, a=None, b=None, s=None, part=None):
+        w = 512 if name not in SB else SB[name][0]
+        a = 0 if a is None else a
+        b = w if b is None else b
+        key = (a, b, s)
+        if key not in masks:
+            masks[key] = ((1 << (b - a)) - 1) << a if s is None else sum(1 << c for c in range(a, b, s))
+        cols = slice(a, b) if s is None else slice(a, b, s)
+        t = T[name]
+        return {"ap": t[:, cols] if part is None else t[part, cols], "acc": [(name, masks[key])],
+                "n": len(range(a, b, s or 1)), "dt": F32 if name not in SB else SB[name][1], "ps": name not in SB, "ind": False}
+
+    def IND(win, off):
+        return {"ap": win["ap"].indirect(off["ap"]), "acc": win["acc"], "off": off["acc"], "n": 16 * off["n"],
+                "dt": win["dt"], "ps": False, "ind": True}
+
+    def add(eng, fn, outs, ins, cost, kind="c", sem=None, val=0, busy=None):
+        i = len(ops)
+        hard, soft = set(), set()
+        rd = [x for v in ins if isinstance(v, dict) for x in v["acc"] + v.get("off", [])]
+        rd += [x for v in outs for x in v.get("off", [])]
+        wr = [x for v in outs for x in v["acc"]]
+        for name, m in rd + wr:
+            if name not in SB:
+                j = bank_last.get(name)
+                if j is not None and j != i:
+                    (soft if ops[j]["eng"] == eng else hard).add(j)
+                bank_last[name] = i
+        for name, m in rd:
+            hard.update(j for j, mm in last_w.get(name, []) if mm & m)
+        for name, m in wr:
+            for j, mm in last_w.get(name, []) + readers.get(name, []):
+                if mm & m and j != i:
+                    (soft if eng == "p" and ops[j]["eng"] == "p" else hard).add(j)
+        for name, m in rd:
+            readers.setdefault(name, []).append((i, m))
+        for name, m in wr:
+            last_w[name] = [(j, mm & ~m) for j, mm in last_w.get(name, []) if mm & ~m] + [(i, m)]
+            readers[name] = [(j, mm & ~m) for j, mm in readers.get(name, []) if mm & ~m or j == i]
+        ops.append({"eng": eng, "fn": fn, "hard": hard, "soft": soft - hard, "cost": cost, "kind": kind, "tag": wr[0][0] if wr else "", "sem": sem, "val": val,
+                    "busy": cost if busy is None else busy, "boost": boost[0]})
+        if chain[0]:
+            if eng in tail and tail[eng] not in hard:
+                ops[i]["soft"].add(tail[eng])
+            tail[eng] = i
+        return i
+
+    def val(x):
+        return x["ap"] if isinstance(x, dict) else x
+
+    def vcost(out, ins, two=False, fast=True):
+        n = max(v["n"] for v in ins + [out])
+        if out["ind"]:
+            return 50 + out["n"] * SCAT * CYC
+        if any(v["ind"] for v in ins):
+            return 50 + out["n"] * GATH * CYC
+        n = out["n"] if len(ins) == 0 else ins[0]["n"]
+        f = 0.5 if fast and all(v["dt"] in (BF, F16, U16) for v in ins + [out]) else 1.0
+        if two and not any(v["ps"] for v in ins):
+            f *= 2
+        return 30 + max(64, n * f) * CYC
+
+    def ts(out, in0, s1, s2, op0, op1=None):
+        def fn():
+            if op1 is None:
+                return g.vector.tensor_scalar(out["ap"], in0["ap"], val(s1), None, op0)
+            return g.vector.tensor_scalar(out["ap"], in0["ap"], val(s1), val(s2), op0, op1)
+        return add("v", fn, [out], [in0, s1, s2], vcost(out, [in0]))
+
+    def tt(out, in0, in1, op):
+        return add("v", lambda: g.vector.tensor_tensor(out["ap"], in0["ap"], in1["ap"], op), [out], [in0, in1], vcost(out, [in0, in1], True))
+
+    def cp(out, in0):
+        return add("v", lambda: g.vector.tensor_copy(out["ap"], in0["ap"]), [out], [in0], vcost(out, [in0]))
+
+    def ms(out, c):
+        return add("v", lambda: g.vector.memset(out["ap"], c), [out], [], vcost(out, []))
+
+    def scan(out, d0, d1, init, op0, op1):
+        return add("v", lambda: g.vector.tensor_tensor_scan(out["ap"], d0["ap"], d1["ap"], val(init), op0, op1), [out], [d0, d1, init], vcost(out, [d0, d1]))
+
+    def red(out, in0, op):
+        return add("v", lambda: g.vector.tensor_reduce(out["ap"], in0["ap"], AxisListType.X, op), [out], [in0], vcost(out, [in0], False, False))
+
+    def tr(out, in0):
+        return add("v", lambda: g.vector.transpose(out["ap"], in0["ap"]), [out], [in0], vcost(out, [in0]))
+
+    def act(out, in0, f, bias=0.0, scale=1.0):
+        return add("a", lambda: g.scalar.activation(out["ap"], in0["ap"], f, bias=val(bias), scale=val(scale)), [out], [in0, bias, scale],
+                   65 + max(64, in0["n"] * (GATH if in0["ind"] else 1)) * CYC)
+
+    def mm(items):
+        def fn():
+            r = None
+            for o, l, x, st, sp in items:
+                r = g.tensor.matmul(o["ap"], l["ap"], x["ap"], st, sp)
+            return r
+        return add("p", fn, [it[0] for it in items], [it[1] for it in items] + [it[2] for it in items],
+                   40 + sum(max(64, it[2]["n"]) for it in items) * PCYC)
+
+    def iota(out, pat, base, cm):
+        def fn():
+            if out["dt"] == I32:
+                return g.iota(out["ap"], pat, base, cm)
+            return g.iota(out["ap"], pat, base, cm, allow_small_or_imprecise_dtypes=True)
+        return add("g", fn, [out], [], 130 + 2 * out["n"] * CYC)
+
+    def pick(out, in0, op, fill):
+        return add("g", lambda: g.affine_select(out["ap"], in0["ap"], [[1, 128]], op, fill, 0, -1), [out], [in0], 170 + 256 * CYC)
+
+    ndma = [0]
+
+    def dma(eng, out, in0, cost, slow=False):
+        sem = "d%d" % ndma[0]
+        ndma[0] += 1
+        q = {"s": g.sync, "a": g.scalar, "g": g}[eng]
+
+        def fn():
+            if slow:
+                return q.dma_start(val(out), val(in0), allow_slow_non_contiguous=True)
+            return q.dma_start(val(out), val(in0))
+        return add(eng, fn, [out] if isinstance(out, dict) else [], [in0], cost, "dma", sem, 16, 1000 if eng == "g" else 100)
+
+    def col(name, c):
+        return S(name, c, c + 1)
+
+    dma("s", S("EB"), T.ends0[:], 2200)
+    dma("a", S("NEI"), T.ne0[:], 2500)
+    dma("s", S("YW", 16, 3088), T.y0[:], 4500)
+    chain[0] = True
+    iota(col("PI", 0), [[0, 1]], 0, 1)
+    iota(S("QG"), [[1, 8], [0, 16]], 0, 0)
+    iota(S("T16"), [[0, 12], [1, 16]], 0, 0)
+    iota(S("LI"), [[5, 3], [12, 16]], 16, 0)
+    iota(S("IOT"), [[1, 144]], 0, 0)
+    iota(S("CX"), [[1, 512]], -256, 0)
+    iota(S("JJ"), [[1, 256]], 0, 0)
+    chain[0] = False
+    RF, GF = col("CF", 0), col("CF", 1)
+    R15, R192, R16, G16, R1, R1W, INI, INX, NBC, KB, COF, CBI, CKA, CYO, OFD = [col("CF", c) for c in range(2, 17)]
+    boost[0] = 2e6
+    chain[0] = True
+    ms(S("W", 0, 768), 0.0)
+    ts(col("PI", 1), col("PI", 0), 15, None, A.bitwise_and)
+    ts(col("PI", 2), col("PI", 0), 4, None, A.logical_shift_right)
+    ms(S("YW", 0, 16), 255.0)
+    cp(S("CF", 0, 2), S("PI", 1, 3))
+    ms(S("YW", 3088, 3136), 0.0)
+    ts(S("O1"), S("QG"), GF, None, A.is_equal)
+    ts(S("RM"), S("T16", 0, 16), RF, 8192.0, A.is_equal, A.mult)
+    ts(col("CF", 20), RF, 15.0, 2304.0, A.is_equal, A.mult)
+    ts(R192, RF, 192.0, None, A.mult)
+    ms(S("W", 768, 3088), 0.0)
+    ts(S("EI", 0, 192), S("EB"), 10, None, A.logical_shift_right)
+    ts(S("EI", 192, 384), S("EB"), 1023, None, A.bitwise_and)
+    ts(S("PC", 0, 191), S("EI", 0, 191), -256.0, None, A.add)
+    ts(col("PC", 191), col("EI", 191), -256.0, col("CF", 20), A.add, A.add)
+    ts(S("PC", 192, 384), S("EI", 192, 384), -256.0, None, A.add)
+    ts(S("LOFF"), S("LI"), R192, None, A.add)
+    ts(S("NEO"), S("NEI"), 16.0, None, A.add)
+    ts(G16, GF, 16.0, 15.0, A.mult, A.add)
+    ts(S("BE"), S("IOT", 0, 144), G16, 8192.0, A.is_equal, A.mult)
+    ts(S("NE", 0, 512), S("NEI"), -3071.0, None, A.add)
+    ms(S("NE", 512, 640), 0.0)
+    ms(S("FAR", 512, 640), 0.0)
+    chain[0] = False
+    boost[0] = 1e6
+    for m in range(16):
+        act(S("SEL", 128 * m, 128 * m + 128), S("O1"), AF.Identity, scale=col("RM", m))
+    ts(S("SELH", 0, 1024), S("SEL", 0, 1024), 1.0 / 8192, None, A.mult)
+    ts(S("SELH", 1024, 2048), S("SEL", 1024, 2048), 1.0 / 8192, None, A.mult)
+    boost[0] = 0.0
+    ts(R15, RF, 15.0, None, A.is_equal)
+    ts(R16, RF, 16.0, None, A.mult)
+    ts(R1, RF, 1.0, None, A.add)
+    ts(R1W, R15, -16.0, R1, A.mult, A.add)
+    ts(INI, R15, BIGK, KEYMAX - BIGK, A.mult, A.add)
+    ts(INX, R15, -BIGK, BIGK - KEYMAX, A.mult, A.add)
+    ts(KB, RF, 512.0, None, A.mult)
+    ts(COF, R15, BD, 1280.0 - BD, A.mult, A.add)
+    ts(CBI, R15, -BD * SC2, (BD + 0.125) * SC2, A.mult, A.add)
+    ts(CKA, R15, BD, -BD, A.mult, A.add)
+    for t in range(RO):
+        ts(col("CF", 17 + t), RF, -191.25, 4080.0 - 5 * t, A.mult, A.add)
+    ts(OFD, R15, -BD, BD + 0.5, A.mult, A.add)
+    ts(S("POFF"), S("IOT", 0, 16), R16, None, A.add)
+    ts(S("XM", 0, 8), S("IOT", 0, 128, 16), RF, 512.0, A.add, A.add)
+    ts(S("XM", 8, 10), S("IOT", 0, 32, 16), RF, 3088.0, A.add, A.add)
+    ts(S("DUM"), S("XM"), -1.0, CC2, A.mult, A.add)
+    ms(S("C256"), 1.0 / 256)
+    for nm, c in (("O256", 256.0), ("ONB", -1024.0), ("OKW", RF)):
+        ts(S(nm), S("QG"), GF, c, A.is_equal, A.mult)
+    chain[0] = True
+    pick(S("I1"), S("O1"), A.is_equal, 0.0)
+    for nm, c in (("IN8", -8192.0), ("IN1", -1.0)):
+        pick(S(nm), S("I1"), A.not_equal, c)
+    chain[0] = False
+    ts(S("E1", 0, 128), S("T16", 0, 128), RF, BIGK, A.is_equal, A.mult)
+    ts(S("E2", 0, 128), S("T16", 0, 128), R1W, BIGK, A.is_equal, A.mult)
+    tt(S("MMN"), S("E1", 0, 128), S("E2", 0, 128), A.subtract)
+    tt(S("MMX"), S("E2", 0, 128), S("E1", 0, 128), A.subtract)
+    ts(S("E1"), S("T16"), RF, -3 * BD, A.is_equal, A.mult)
+    ts(S("E2"), S("T16"), R1, BD, A.is_equal, A.mult)
+    tt(S("MD"), S("E1"), S("E2"), A.add)
+    boost[0] = 2e6
+    dma("s", S("W", 16, 3088, part=slice(0, 128, 16)), S("PC", 0, 192), 2200)
+    j = dma("a", S("W", 16, 3088, part=slice(1, 128, 16)), S("PC", 192, 384), 2200)
+    ops[j]["hard"].discard(j - 1)
+    ops[j]["hard"].update(ops[j - 1]["hard"])
+    last_w["W"].append((j - 1, last_w["W"][-1][1]))
+    for t in range(RO):
+        act(S("OWN", 288 * t, 288 * t + 256), IND(S("YW"), S("LOFF", 16 * t, 16 * t + 16)), AF.Identity)
+        for s in range(2):
+            act(S("OWN", 288 * t + 256 + 16 * s, 288 * t + 272 + 16 * s), S("PC", 192 * s + 5 * t, 192 * s + 192, 12), AF.Identity)
+    boost[0] = 0.0
+    for t in range(RO):
+        ts(S("UVO", 64 * t + 32, 64 * t + 64), S("OWN", 288 * t + 256, 288 * t + 288), 256.0, None, A.add)
+    cp(col("SVC", 0), col("YW", 3087))
+    ms(col("YW", 3087), 255.0)
+    boost[0] = 0.5e6
+    for c in range(8):
+        o, src = S("G", 1024 * c, 1024 * c + 1024), IND(S("W"), S("NEO", 64 * c, 64 * c + 64))
+        if GPLAN[c] == "v":
+            cp(o, src)
+        else:
+            act(o, src, AF.Identity)
+        pb = S("p%d" % (c // 2), 64 * (c % 2), 64 * (c % 2) + 64)
+        mm([(pb, S("IN8"), S("CX", 64 * c, 64 * c + 64), True, False)]
+           + [(pb, S("BE", 15 - k, 143 - k), S("G", 1024 * c + k, 1024 * c + 1024, 16), False, k == 15) for k in range(16)])
+        if c % 2:
+            act(S("FAR", 64 * c - 64, 64 * c + 64), S("p%d" % (c // 2), 0, 128), AF.Relu, bias=300.0, scale=-1.0 / 8192)
+    boost[0] = 0.0
+    peers = [T.cores[(rank + 1 + t) % N] for t in range(RO)]
+    backs = [T.cores[(rank - 1 - t) % N] for t in range(RO)]
+    sent = [0]
+
+    def send_lanes():
+        trs, at = [], 0
+        for t in range(RO):
+            en = topo.engines(core, peers[t])
+            k = len(en) // 2 if t == 0 else len(en) // 4
+            rid, pid, _s = topo.addr(peers[t])
+            trs.append(RemoteDMATransfer(dst_ids=[DstId(rid=rid, pnc=pid)], dma_engine_mask=sum(1 << e for e in en[at:at + k]),
+                                         remote_sem=T.sem["ln%d" % t], src=T.OWN[:, 288 * t:288 * t + 288], dst=T.LAND[:, 288 * t:288 * t + 288]))
+            at += k
+        sent[0] += at
+        return g.remote_dma_fused(trs, local_sem=T.sem.sent)
+    js = add("g", send_lanes, [], [S("OWN")], 3500, "rem", busy=1500)
+    readers["OWN"] = [x for x in readers["OWN"] if x[0] != js]
+    tail["g"] = js
+    chain[0] = True
+    iota(S("RST"), [[0, L], [-16384, 16]], 16384, 0)
+    dma("g", S("THI", part=slice(0, 1)), T.th[:], 2500, True)
+    dma("g", S("ENR", 16, 3088), T.y0[:], 9000)
+    iota(S("BBI"), [[0, 4], [1, 2], [2, 16]], 0, 0)
+    iota(S("LID"), [[12, 16], [192, 16]], -3071, 0)
+    for nm, c in (("IBG", 16777216.0), ("I16", 16.0)):
+        pick(S(nm), S("I1"), A.not_equal, c)
+    pick(S("AX", 0, 128), S("ONB"), A.is_gt, 0.0)
+    pick(S("TRI"), S("AX", 0, 128), A.not_equal, 1.0)
+    iota(S("C3"), [[0, 64]], 3071, 0)
+    iota(S("ENR", 0, 16), [[0, 16]], 0, 0)
+    iota(S("ENR", 3088, 3136), [[0, 48]], 0, 0)
+    iota(S("TT"), [[0, 48]], int(LIM), 0)
+    iota(S("NOUT", 512, 640), [[0, 128]], 0, 0)
+    chain[0] = False
+    act(S("BB"), S("BBI"), AF.Identity, scale=1.0 / 128)
+    for t in range(RO):
+        ne_t = len(topo.engines(backs[t], core))
+        j = add("x", None, [S("LAND", 288 * t, 288 * t + 288)], [], 0, "arr", "ln%d" % t, ne_t // 2 if t == 0 else ne_t // 4)
+        ops[j]["soft"].add(js)
+        ts(S("UVO", 64 * t, 64 * t + 32), S("LAND", 288 * t + 256, 288 * t + 288), 256.0, None, A.add)
+    act(S("WL"), IND(S("W"), S("LOFF")), AF.Identity)
+    for t in range(RO):
+        pb = "p%d" % (3 + t % 2)
+        mm([(S(pb, 256 * s, 256 * s + 256), S("SEL", 128 * s, 128 * s + 128), S("WL", 256 * t, 256 * t + 256), True, True) for s in range(2)])
+        act(S("UV", 512 * t, 512 * t + 512), S(pb), AF.Identity, scale=1.0 / 8192)
+    cp(S("THF", part=slice(0, 1)), S("THI", part=slice(0, 1)))
+    add("g", lambda: g.partition_broadcast(T.THB[:, :], T.THF[0:1, :], 128), [S("THB")], [S("THF")], 200)
+    ts(S("THM"), S("IOT", 0, 8), GF, None, A.is_equal)
+    tt(S("THF"), S("THM"), S("THB"), A.mult)
+    red(col("AC", 0), S("THF"), A.add)
+    ts(col("AC", 1), col("AC", 0), -256.0, CEN + 0.5, A.mult, A.add)
+    ms(col("AC", 2), 0.0)
+    cp(S("EBF"), S("EB"))
+    dma("s", S("ENR", 16, 3088, part=slice(0, 128, 16)), S("EBF"), 2500)
+    ring = {"d": 0, "z": 0, "r": 0}
+
+    for t in range(RO):
+        lastr = t == RO - 1
+        dbank, zbank = {}, {}
+
+        def pre(kind, lo, hi):
+            side, a, b = lo // 256, (lo % 256) // 16, (hi - 1) % 256 // 16 + 1
+            uo = S("UVO", 64 * t + 32 * side + a, 64 * t + 32 * side + b)
+            vo = S("UVO", 64 * t + 32 * side + 16 + a, 64 * t + 32 * side + 16 + b)
+            if kind == "P":
+                act(S("SS", lo, hi), IND(S("FAR"), uo), AF.Identity, bias=300.0, scale=-1.0)
+                act(S("X1", lo, hi), IND(S("FAR"), vo), AF.Identity, bias=300.0, scale=-1.0)
+            elif kind == "Q":
+                ts(S("X2", lo, hi), IND(S("NE"), vo), 1535.0, None, A.add)
+            else:
+                ts(S("AO", lo, hi), IND(S("NE"), uo), 3087.0, None, A.add)
+
+        def free_of_chain(fn, *args):
+            chain[0] = False
+            fn(*args)
+            chain[0] = True
+
+        def after_scan(lo, hi, mn):
+            ts(S("CO", lo, hi), mn, -1.0, 3087.0, A.mult, A.add)
+            if lo >= 256:
+                act(S("PEN", lo - 256, hi - 256), mn, AF.Relu, bias=67108864.0, scale=-16384.0)
+                tt(S("F2", lo - 256, hi - 256), S("SS", lo, hi), S("UV", 512 * t + lo, 512 * t + hi), A.is_equal)
+
+        def after_sum(j, lo, hi, kb):
+            if lo < 256:
+                ko = S("KOUT", 256 * t + lo, 256 * t + hi)
+                act(ko, kb, AF.Identity, bias=-CEN)
+                sem = "kin%d" % (4 * t + j)
+                rid, pid, _s = topo.addr(backs[t])
+                msk, cnt = topo.mask(core, backs[t]), len(topo.engines(core, backs[t]))
+                dst = T.KIN[:, 256 * t + lo:256 * t + hi]
+
+                def send():
+                    sent[0] += cnt
+                    return g.remote_dma(dst, ko["ap"], T.sem[sem], T.sem.sent, pid, rid, msk)
+                jj = add("g", send, [], [ko], 3000, "rem", busy=1200)
+                ja = add("x", None, [S("KIN", 256 * t + lo, 256 * t + hi)], [], 0, "arr", sem, len(topo.engines(peers[t], core)))
+                ops[ja]["soft"].add(jj)
+                return
+            a, b = lo - 256, hi - 256
+            tt(S("KEY", a, b), kb, S("KIN", 256 * t + a, 256 * t + b), A.add)
+            scan(S("SC", a, b), S("MMN", 0, b - a), S("KEY", a, b), col("SC", a - 1) if a % 128 else INI, A.add, A.min)
+            scan(S("SC", 256 + a, 256 + b), S("MMX", 0, b - a), S("KEY", a, b), col("SC", 255 + a) if a % 128 else INX, A.add, A.max)
+            if b % 128 == 0:
+                h = a // 128
+                ce, cd = col("SC", b - 1), col("SC", 255 + b)
+                ts(col("Q", h), col("C256", 0), ce, -0.25 - 0.5 * h, A.mult, A.add)
+                ts(S("Q", 4 + 4 * h, 8 + 4 * h), S("C256"), cd, -0.25 - 0.5 * h, A.mult, A.add)
+                ts(col("OFF", h), col("Q", h), -256.0, ce, A.mult, A.add)
+                ts(S("OFF", 2 + h, 10, 2), S("Q", 4 + 4 * h, 8 + 4 * h), -256.0, cd, A.mult, A.add)
+
+        def step(tok):
+            kind, j = tok[0], int(tok[1])
+            if kind in "PQO":
+                return pre(kind, *PRE[j])
+            lo, hi = CH[j]
+            w = hi - lo
+            nm, nb, ab = 512 // w, w // 32, 16 * L * (j % 2)
+            bk = int(tok[2]) if len(tok) > 2 else 0
+            if kind == "D":
+                pb = dbank[j, bk] = "p%d" % (ring["d"] % ND)
+                ring["d"] += 1
+                it = []
+                for x in range(nm):
+                    m, o = nm * bk + x, S(pb, x, 512, nm)
+                    it += [(o, S("IN8"), S("SS", lo, hi), True, False), (o, S("SEL", 128 * m, 128 * m + 128), S("X1", lo, hi), False, False),
+                           (o, S("SELH", 128 * m, 128 * m + 128), S("X2", lo, hi), False, True)]
+                mm(it)
+            elif kind == "A":
+                act(S("AB", ab + bk, ab + 16 * w, nb), S(dbank[j, bk]), AF.Abs, bias=-1535.0)
+            elif kind == "S":
+                scan(S("MN", ab, ab + 16 * w), S("RST", 0, 16 * w), S("AB", ab, ab + 16 * w), 0.0, A.max, A.min)
+                free_of_chain(after_scan, lo, hi, S("MN", ab + 15, ab + 16 * w, 16))
+            elif kind == "Y":
+                a = lo + 64 * bk
+                o, src = S("YA", 16 * a, 16 * a + 1024), IND(S("YW"), S("AO", a, a + 64))
+                if tok[3] == "v":
+                    cp(o, src)
+                else:
+                    act(o, src, AF.Identity)
+            elif kind == "X":
+                tt(S("MM", 16 * lo, 16 * hi), IND(S("YW"), S("CO", lo, hi)), S("YA", 16 * lo, 16 * hi), A.max)
+            elif kind == "Z":
+                pb = "p%d" % (ND + ring["z"] % NZ)
+                zbank[j, bk] = (pb, 512 * (ring["z"] % 4))
+                ring["z"] += 1
+                ye = S("LAND", 288 * t + lo, 288 * t + hi) if lo < 256 else S("OWN", 288 * t + lo - 256, 288 * t + hi - 256)
+                it = []
+                for x in range(nm):
+                    o = S(pb, w * x, w * x + w)
+                    it += [(o, S("I1"), ye, True, False), (o, S("IN1"), S("MM", 16 * lo + nm * bk + x, 16 * hi, 16), False, True)]
+                mm(it)
+            elif kind == "R":
+                pb, r0 = zbank[j, bk]
+                if tok[3] == "v":
+                    ts(S("RR", r0, r0 + 512), S(pb), 12.0, 0.0, A.add, A.max)
+                else:
+                    act(S("RR", r0, r0 + 512), S(pb), AF.Relu, bias=12.0)
+            elif kind == "U":
+                r0 = zbank[j, bk][1]
+                kb = S("p%d" % (5 + j % 2 if ND + NZ == 5 else 6), 0, w)
+                it = [(kb, S("O256"), S("RR", r0 + w * x, r0 + w * x + w), bk == 0 and x == 0, lo >= 256 and bk == nb - 1 and x == nm - 1) for x in range(nm)]
+                if lo < 256 and bk == nb - 1:
+                    it.append((kb, S("I1"), S("JJ", lo, hi), False, True))
+                mm(it)
+                if bk == nb - 1:
+                    free_of_chain(after_sum, j, lo, hi, kb)
+            elif kind == "T":
+                a, b = lo - 256, hi - 256
+                pb = S("p7", a, b)
+                mm([(pb, S("BE", 15 - k, 143 - k), S("YA", 16 * lo + k, 16 * hi, 16), k == 0, False) for k in range(16)]
+                   + [(pb, S("IBG"), S("F2", a, b), False, False), (pb, S("I1"), S("PEN", a, b), False, True)])
+                free_of_chain(act, S("K2", a, b), pb, AF.Identity, KB)
+
+        chain[0] = True
+        for tok in PLAN.split():
+            step(tok)
+        chain[0] = False
+        eo, do = S("OFF", 0, 2), S("OFF", 2, 4)
+        uw, vw = S("UV", 512 * t, 512 * t + 256), S("UV", 512 * t + 256, 512 * t + 512)
+        cp(S("KE"), IND(S("K2"), eo))
+        tr(S("TT", 8, 40), S("KE"))
+        red(col("MV", 0), S("TT", 7, 24), A.min)
+        red(col("MV", 1), S("TT", 24, 41), A.min)
+        for x in range(2):
+            ts(S("EQ", 16 * x, 16 * x + 16), S("TT", 8 + 16 * x, 24 + 16 * x), col("MV", x), None, A.is_equal)
+        tr(S("SL"), S("EQ"))
+        act(S("VP", 0, 32), IND(vw, eo), AF.Identity)
+        act(S("VP", 32, 64), IND(uw, do), AF.Identity)
+        act(S("VP", 64, 96), IND(vw, do), AF.Identity)
+        act(S("PS"), IND(S("JJ"), eo), AF.Identity)
+        act(S("YE"), IND(S("OWN", 288 * t, 288 * t + 256), eo), AF.Identity)
+        tt(S("SX"), IND(S("SS", 256, 512), eo), S("SL"), A.mult)
+        act(S("DD"), IND(S("LID"), S("OFF", 2, 10)), AF.Identity, bias=5.0 * t)
+        mm([(S("p7", 0, 128), S("I1"), S("BB"), True, False), (S("p7", 32, 128), S("I1"), S("VP"), False, False)])
+        mm([(S("p7", 32 * x, 32 * x + 32), S("ONB"), S("SL"), False, False) for x in range(4)]
+           + [(S("p7", 0, 32), S("O1"), S("SX"), False, True),
+              (S("p7", 128, 160), S("I16"), S("PS"), True, False), (S("p7", 128, 160), S("OKW"), S("SL"), False, True),
+              (S("p7", 160, 192), S("O1"), S("SL"), True, True)])
+        scan(S("WR"), S("MD"), S("p7", 0, 192), 0.0, A.add, A.max)
+        act(S("WB"), S("WR", 15, 128, 16), AF.Identity, bias=CBI, scale=-SC2)
+        ts(S("NO", 0, 8), S("WR", 15, 128, 16), COF, 511.0, A.add, A.min)
+        for h in range(2):
+            for x in range(4):
+                act(S("AX", 512 * h + 128 * x, 512 * h + 128 * x + 128), S("p7", 0, 128), AF.Abs, bias=col("WB", 2 * x + h), scale=SC2)
+            scan(S("CM", 256 * h, 256 * h + 256), S("AX", 512 * h, 512 * h + 256), S("AX", 512 * h + 256, 512 * h + 512), SC2, A.min, A.min)
+        mm([(S("p0", 0, 32), S("I1"), S("VP", 0, 32), True, True), (S("p0", 32, 64), S("O1"), S("SX"), True, True)])
+        cp(S("CN"), IND(S("NE"), S("NO", 0, 8)))
+        ts(S("EM"), S("CN", 0, 64), 0.0, None, A.is_equal)
+        mm([(S("p1", 0, 64), S("O1"), S("EM"), True, True), (S("p2", 0, 64), S("TRI"), S("EM"), True, True)])
+        scan(S("W2"), S("MD", 0, 64), S("p1", 0, 64), 0.0, A.add, A.max)
+        tt(S("OK", 0, 2), S("W2", 15, 32, 16), S("W2", 47, 64, 16), A.min)
+        tt(S("OK", 2, 4), S("OK", 0, 2), S("WR", 175, 192, 16), A.min)
+        ts(S("OK", 4, 6), S("OK", 2, 4), OFD, 4096.0, A.is_ge, A.mult)
+        ts(S("XF", 0, 8), S("NO", 0, 8), -1.0, 4096.0, A.mult, A.add)
+        ts(S("XF", 8, 10), do, -0.75, col("CF", 17 + t), A.mult, A.add)
+        for h in range(2):
+            ts(S("XP", h, 10, 2), S("XF", h, 10, 2), col("OK", 4 + h), CC2 - 4096.0, A.min, A.add)
+            ts(S("XM", h, 10, 2), S("XP", h, 10, 2), col("CM", 256 * h + 255), None, A.min)
+        tt(S("XN"), S("XM"), S("DUM"), A.max)
+        ts(S("SO"), S("XN"), -1.0, CC2, A.mult, A.add)
+        tt(S("KP"), S("CN"), S("DD"), A.not_equal)
+        act(S("FM"), S("p2", 0, 64), AF.Relu)
+        act(S("OT"), S("p0", 0, 64), AF.Identity, bias=300.0, scale=-1.0)
+        tt(S("M1"), S("FM"), S("DD", 0, 64), A.mult)
+        if not lastr:
+            cp(S("CR"), IND(S("FAR"), S("NO", 0, 8)))
+            tt(S("M2"), S("FM"), S("OT"), A.mult)
+            tt(S("N1", 0, 64), S("CN", 0, 64), S("M1"), A.add)
+            tt(S("N2", 0, 64), S("CR", 0, 64), S("M2"), A.add)
+            tt(IND(S("FAR"), S("SO", 4, 8)), S("CR", 64, 128), S("KP", 64, 128), A.mult)
+            tt(IND(S("NE"), S("SO", 4, 8)), S("CN", 64, 128), S("KP", 64, 128), A.mult)
+            tt(IND(S("FAR"), S("SO", 0, 4)), S("N2", 0, 64), S("KP", 0, 64), A.mult)
+            tt(IND(S("NE"), S("SO", 0, 4)), S("N1", 0, 64), S("KP", 0, 64), A.mult)
+        else:
+            act(S("NOUT", 0, 512), S("NE", 0, 512), AF.Identity, bias=3071.0)
+            tt(S("N1"), S("CN"), S("KP"), A.mult)
+            tt(S("N2", 0, 64), S("N1", 0, 64), S("M1"), A.add)
+            tt(IND(S("NOUT"), S("SO", 4, 8)), S("N1", 64, 128), S("C3"), A.add)
+            tt(IND(S("NOUT"), S("SO", 0, 4)), S("N2", 0, 64), S("C3"), A.add)
+        act(S("SG"), S("KEY"), AF.Sign, bias=col("AC", 1 if t == 0 else 3 + t))
+        tt(S("T2"), S("SG"), S("OWN", 288 * t, 288 * t + 256), A.add)
+        ts(S("YW", 16 + 5 * t, 3088, 12), IND(S("T2"), S("POFF")), 0.0, 63.0, A.max, A.min)
+        ts(S("NO", 8, 10), S("WR", 143, 160, 16), CKA, None, A.add)
+        tt(S("YS"), IND(S("YA", 4096, 8192), S("NO", 8, 10)), S("YE"), A.add)
+        ts(S("YI"), S("YS"), 0.5, -0.25, A.mult, A.add)
+        cp(IND(S("YW"), S("SO", 8, 10)), S("YI"))
+        tt(S("LH", 0, 32), S("OT", 0, 32), S("OT", 32, 64), A.min)
+        tt(S("LH", 32, 64), S("OT", 0, 32), S("OT", 32, 64), A.max)
+        ts(S("LH", 64, 96), S("LH", 32, 64), -1024.0, 556.0 * 1025, A.mult, A.add)
+        tt(IND(S("ENR"), S("SO", 8, 10)), S("LH", 64, 96), S("LH", 0, 32), A.subtract)
+        if not lastr:
+            ts(S("GO"), S("XN", 8, 10), CC2 - 3087.5, None, A.is_gt)
+            mm([(S("p1", 0, 1), S("O1"), col("GO", 0), True, False), (S("p1", 0, 1), S("O1"), col("GO", 1), False, True)])
+            ts(col("AI", 2 * t), S("p1", 0, 1), col("AC", 2 + t), None, A.add)
+            if t == 0:
+                cp(col("AC", 3), col("AI", 0))
+            ts(col("AI", 2 * t + 1), col("AI", 2 * t), 31, None, A.bitwise_and)
+            ts(col("AC", 4 + t), col("AI", 2 * t + 1), -2048.0, col("AC", 1), A.mult, A.add)
+    act(col("YW", 3087), col("SVC", 0), AF.Identity)
+    dma("s", T.y1[:, 0:1536], S("YW", 16, 1552), 3000)
+    dma("s", T.y1[:, 1536:3072], S("YW", 1552, 3088), 3000)
+    dma("a", T.ne1[:], S("NOUT", 0, 512), 2500)
+    dma("s", T.ends1[:], S("ENR", 16, 3088, part=slice(0, 128, 16)), 2500)
+
+    n = len(ops)
+    succ = [[] for _ in range(n)]
+    for i, o in enumerate(ops):
+        for j in o["hard"] | o["soft"]:
+            succ[j].append(i)
+    prio = [0.0] * n
+    for i in range(n - 1, -1, -1):
+        prio[i] = ops[i]["cost"] + max([prio[k] + (WAKE if i in ops[k]["hard"] else 0) for k in succ[i]], default=0.0)
+    prio = [p + o["boost"] for p, o in zip(prio, ops)]
+    left = [len(o["hard"] | o["soft"]) for o in ops]
+    ready_at, done_at = [0.0] * n, [0.0] * n
+    free = {e: 0.0 for e in "vapgsx"}
+    pool = {e: [] for e in "vapgsx"}
+    for i in range(n):
+        if left[i] == 0:
+            pool[ops[i]["eng"]].append(i)
+    order = []
+    while len(order) < n:
+        best = None
+        for e in pool:
+            if pool[e]:
+                t0 = max(free[e], min(ready_at[i] for i in pool[e]))
+                if best is None or t0 < best[0]:
+                    best = (t0, e)
+        t0, e = best
+        top = max(pool[e], key=lambda i: (prio[i] - max(0.0, ready_at[i] - t0) * 0, -i))
+        now = [i for i in pool[e] if ready_at[i] <= t0]
+        i = max(now, key=lambda i: (prio[i], -i))
+        if top not in now and t0 + ops[i]["busy"] - ready_at[top] > prio[i] + ops[i]["busy"] - prio[top] + 2 * (ready_at[top] - t0) and prio[top] > prio[i]:
+            fit = [k for k in now if t0 + ops[k]["busy"] <= ready_at[top] + 60]
+            i = max(fit, key=lambda k: (prio[k], -k)) if fit else top
+        t0 = max(t0, ready_at[i])
+        pool[e].remove(i)
+        order.append(i)
+        ops[i]["t0"] = t0
+        ops[i]["seq"] = len(order)
+        free[e] = t0 + ops[i]["busy"]
+        done_at[i] = t0 + ops[i]["cost"]
+        for k in succ[i]:
+            hard = i in ops[k]["hard"]
+            ready_at[k] = max(ready_at[k], done_at[i] + WAKE if hard else (done_at[i] if ops[k]["eng"] == "x" else t0))
+            left[k] -= 1
+            if left[k] == 0:
+                pool[ops[k]["eng"]].append(k)
+    queue = {"v": g.vector, "a": g.scalar, "p": g.tensor, "g": g, "s": g.sync}
+    needed = [False] * n
+    for o in ops:
+        for j in o["hard"]:
+            needed[j] = True
+    count = {"sv": 0, "sa": 0, "sp": 0, "sg": 0}
+    known = {e: {} for e in queue}
+    clock = [None] * n
+    for i in order:
+        o = ops[i]
+        e = o["eng"]
+        if e == "x":
+            clock[i] = {o["sem"]: o["val"]}
+            continue
+        kn = known[e]
+        want = {}
+        for j in o["hard"]:
+            p = ops[j]
+            if kn.get(p["sem"], 0) < p["val"] and want.get(p["sem"], (0, 0))[0] < p["val"]:
+                want[p["sem"]] = (p["val"], j)
+        for sem, (v, j) in sorted(want.items(), key=lambda x: -done_at[x[1][1]]):
+            if kn.get(sem, 0) < v:
+                queue[e].wait_ge(T.sem[sem], v)
+                for s2, v2 in clock[j].items():
+                    if kn.get(s2, 0) < v2:
+                        kn[s2] = v2
+        ins = o["fn"]()
+        clock[i] = dict(kn)
+        if o["kind"] == "dma":
+            ins.then_inc(T.sem[o["sem"]], 16)
+            clock[i][o["sem"]] = 16
+        elif o["kind"] == "c" and needed[i]:
+            o["sem"] = "s" + e
+            count[o["sem"]] += 1
+            o["val"] = count[o["sem"]]
+            ins.then_inc(T.sem[o["sem"]], 1)
+            clock[i][o["sem"]] = o["val"]
+    for sem, v in count.items():
+        if v:
+            g.wait_ge(T.sem[sem], v)
+    g.wait_ge(T.sem.sent, sent[0])
+    for o in ops:
+        if o["kind"] in ("dma", "arr"):
+            g.wait_ge(T.sem[o["sem"]], o["val"])
+    return ops

@@ -7,10 +7,10 @@ N, RO = 8, 3
 L = 128
 CH = [(0, 64), (64, 128), (128, 256), (256, 384), (384, 448), (448, 512)]
 PRE = [(0, 64), (64, 256), (256, 512)]
-PLAN = ("O0 P0 Q0 D01 P1 P2 Q1 D00 A01 O2 A00 O1 Y00v D10 D11 S0 Y21a A10 D20 Q2 X0 A11 D22 D23 A20 Z00 Y10a A23 D21 S1 A22 R00v Z01 D33 D30 "
-        "A21 D31 X1 Y20a U00 A33 A30 Z10 D32 S2 R01v Z11 A31 Y30a A32 R10a U01 D51 R11a D41 Y31a X2 Y50a Z20 Z22 R20a S3 D50 A51 A50 U10 U11 "
-        "T3 R22v Z21 R21a U20 D40 A41 Z23 A40 X3 U21 U22 R23a Z30 S5 Z31 R30a Y40a R31a S4 U23 Z32 U30 X5 R32a T5 T4 X4 Z33 U31 R33a U32 Z50 "
-        "Z40 R40v U33 R50a Z41 Z51 R51a U50 U40 R41v U41 U51")
+PLAN = ("Q0 P0 O0 D00 P1 Y00a D01 O2 A00 Q1 A01 O1 Y10v D11 D10 A11 A10 Q2 S0 S1 P2 C0 D23 D20 F4 D21 A23 A20 D22 C1 Y20a A21 A22 X0 D30 X1 "
+        "Z01 Z00 R01v R00a D33 A30 Y21a Z11 A33 Z10 U00 S2 R10a D32 D31 D40 A32 A31 U01 R11v D51 A40 Y31a Y30a D41 C2 F3 X2 Z21 K0 A41 U10 S3 "
+        "R21v U11 N3 K1 Z22 C3 R22v D50 A51 Z20 A50 Z23 X3 R20a R23a T3 U20 Y40a U21 Z31 S4 U22 E3 S5 U23 N4 R31a Z30 T4 C4 Z32 R30v K2 Z33 "
+        "U30 Y50a U31 C5 X4 R32a Z40 R33a Z41 X5 R40a U32 U33 F5 R41a E4 Z50 Z51 N5 R50a U40 U41 K3 R51v U50 U51 T5 E5 K4 K5")
 GPLAN = "vavavava"
 ND, NZ = 3, 2
 CEN = 256.0 * 18600
@@ -26,13 +26,13 @@ SB = {
     "YW": (3136, BF), "W": (3088, BF), "ENR": (3136, F32), "SVC": (8, BF),
     "EB": (192, I32), "EBF": (192, F32), "EI": (384, I32), "PC": (384, BF),
     "NEI": (512, I32), "NEO": (512, U16), "NE": (640, F32), "FAR": (640, F32), "NOUT": (640, F32),
-    "G": (8192, BF), "RM": (16, F32), "SEL": (2048, BF), "SELH": (2048, F16), "RST": (16 * L, BF),
+    "G": (8192, BF), "RM": (24, F32), "SEL": (2048, BF), "SELH": (2048, F16), "RST": (16 * L, BF),
     "OWN": (3 * 288, BF), "LAND": (3 * 288, BF), "UVO": (3 * 64, U16), "WL": (768, BF), "UV": (3 * 512, BF),
     "KOUT": (3 * 256, F32), "KIN": (3 * 256, F32),
     "AO": (512, U16), "CO": (512, U16), "SS": (512, BF), "X1": (512, BF), "X2": (512, F16),
     "AB": (2 * 16 * L, F32), "MN": (2 * 16 * L, F32), "YA": (8192, BF), "MM": (8192, BF), "RR": (4 * 512, BF),
     "PEN": (256, BF), "F2": (256, BF), "K2": (256, F32), "KEY": (256, F32), "SC": (512, F32),
-    "SG": (256, BF), "T2": (256, BF),
+    "SG": (256, BF), "T2": (512, BF),
     "IOT": (144, F32), "C3": (64, F32), "QG": (128, BF), "T16": (192, F32), "LI": (48, F32), "LID": (256, F32),
     "BBI": (128, BF), "BB": (128, BF), "CX": (512, BF), "JJ": (256, BF), "BE": (144, BF),
     "I1": (128, BF), "IN1": (128, BF), "IN8": (128, BF), "IBG": (128, BF), "I16": (128, BF),
@@ -54,7 +54,7 @@ for _i in range(8):
 SEMAPHORES = ["sv", "sa", "sp", "sg", "sent"] + ["d%d" % i for i in range(16)] + ["ln%d" % t for t in range(RO)] \
     + ["kin%d" % i for i in range(RO * 4)]
 
-CYC, PCYC, GATH, SCAT, WAKE = 1.0, 0.5, 1.6, 3.5, 120.0
+CYC, PCYC, GATH, SCAT, WAKE = 0.95, 0.475, 1.55, 3.5, 150.0
 
 
 def rank_program(g, core, T, topo):
@@ -215,7 +215,7 @@ def rank_program(g, core, T, topo):
     cp(S("CF", 0, 2), S("PI", 1, 3))
     ms(S("YW", 3088, 3136), 0.0)
     ts(S("O1"), S("QG"), GF, None, A.is_equal)
-    ts(S("RM"), S("T16", 0, 16), RF, 8192.0, A.is_equal, A.mult)
+    ts(S("RM", 0, 16), S("T16", 0, 16), RF, 8192.0, A.is_equal, A.mult)
     ts(col("CF", 20), RF, 15.0, 2304.0, A.is_equal, A.mult)
     ts(R192, RF, 192.0, None, A.mult)
     ms(S("W", 768, 3088), 0.0)
@@ -234,8 +234,11 @@ def rank_program(g, core, T, topo):
     chain[0] = False
     boost[0] = 1e6
     for m in range(16):
+        boost[0] = 1e6 if m < 12 else 0.4e6
         act(S("SEL", 128 * m, 128 * m + 128), S("O1"), AF.Identity, scale=col("RM", m))
+    boost[0] = 1e6
     ts(S("SELH", 0, 1024), S("SEL", 0, 1024), 1.0 / 8192, None, A.mult)
+    boost[0] = 0.4e6
     ts(S("SELH", 1024, 2048), S("SEL", 1024, 2048), 1.0 / 8192, None, A.mult)
     boost[0] = 0.0
     ts(R15, RF, 15.0, None, A.is_equal)
@@ -250,7 +253,7 @@ def rank_program(g, core, T, topo):
     ts(CKA, R15, BD, -BD, A.mult, A.add)
     for t in range(RO):
         ts(col("CF", 17 + t), RF, -191.25, 4080.0 - 5 * t, A.mult, A.add)
-    ts(OFD, R15, -BD, BD + 0.5, A.mult, A.add)
+    ts(OFD, R15, -BD, BD + 256.5, A.mult, A.add)
     ts(S("POFF"), S("IOT", 0, 16), R16, None, A.add)
     ts(S("XM", 0, 8), S("IOT", 0, 128, 16), RF, 512.0, A.add, A.add)
     ts(S("XM", 8, 10), S("IOT", 0, 32, 16), RF, 3088.0, A.add, A.add)
@@ -370,17 +373,6 @@ def rank_program(g, core, T, topo):
             else:
                 ts(S("AO", lo, hi), IND(S("NE"), uo), 3087.0, None, A.add)
 
-        def free_of_chain(fn, *args):
-            chain[0] = False
-            fn(*args)
-            chain[0] = True
-
-        def after_scan(lo, hi, mn):
-            ts(S("CO", lo, hi), mn, -1.0, 3087.0, A.mult, A.add)
-            if lo >= 256:
-                act(S("PEN", lo - 256, hi - 256), mn, AF.Relu, bias=67108864.0, scale=-16384.0)
-                tt(S("F2", lo - 256, hi - 256), S("SS", lo, hi), S("UV", 512 * t + lo, 512 * t + hi), A.is_equal)
-
         def after_sum(j, lo, hi, kb):
             if lo < 256:
                 ko = S("KOUT", 256 * t + lo, 256 * t + hi)
@@ -402,12 +394,14 @@ def rank_program(g, core, T, topo):
             scan(S("SC", a, b), S("MMN", 0, b - a), S("KEY", a, b), col("SC", a - 1) if a % 128 else INI, A.add, A.min)
             scan(S("SC", 256 + a, 256 + b), S("MMX", 0, b - a), S("KEY", a, b), col("SC", 255 + a) if a % 128 else INX, A.add, A.max)
             if b % 128 == 0:
+                chain[0] = False
                 h = a // 128
                 ce, cd = col("SC", b - 1), col("SC", 255 + b)
                 ts(col("Q", h), col("C256", 0), ce, -0.25 - 0.5 * h, A.mult, A.add)
                 ts(S("Q", 4 + 4 * h, 8 + 4 * h), S("C256"), cd, -0.25 - 0.5 * h, A.mult, A.add)
                 ts(col("OFF", h), col("Q", h), -256.0, ce, A.mult, A.add)
                 ts(S("OFF", 2 + h, 10, 2), S("Q", 4 + 4 * h, 8 + 4 * h), -256.0, cd, A.mult, A.add)
+                chain[0] = True
 
         def step(tok):
             kind, j = tok[0], int(tok[1])
@@ -430,7 +424,16 @@ def rank_program(g, core, T, topo):
                 act(S("AB", ab + bk, ab + 16 * w, nb), S(dbank[j, bk]), AF.Abs, bias=-1535.0)
             elif kind == "S":
                 scan(S("MN", ab, ab + 16 * w), S("RST", 0, 16 * w), S("AB", ab, ab + 16 * w), 0.0, A.max, A.min)
-                free_of_chain(after_scan, lo, hi, S("MN", ab + 15, ab + 16 * w, 16))
+            elif kind == "C":
+                ts(S("CO", lo, hi), S("MN", ab + 15, ab + 16 * w, 16), -1.0, 3087.0, A.mult, A.add)
+            elif kind == "N":
+                act(S("PEN", lo - 256, hi - 256), S("MN", ab + 15, ab + 16 * w, 16), AF.Relu, bias=67108864.0, scale=-16384.0)
+            elif kind == "F":
+                tt(S("F2", lo - 256, hi - 256), S("SS", lo, hi), S("UV", 512 * t + lo, 512 * t + hi), A.is_equal)
+            elif kind == "K":
+                after_sum(j, lo, hi, S("p%d" % (5 + j % 2), 0, w))
+            elif kind == "E":
+                act(S("K2", lo - 256, hi - 256), S("p7", lo - 256, hi - 256), AF.Identity, KB)
             elif kind == "Y":
                 a = lo + 64 * bk
                 o, src = S("YA", 16 * a, 16 * a + 1024), IND(S("YW"), S("AO", a, a + 64))
@@ -463,14 +466,11 @@ def rank_program(g, core, T, topo):
                 if lo < 256 and bk == nb - 1:
                     it.append((kb, S("I1"), S("JJ", lo, hi), False, True))
                 mm(it)
-                if bk == nb - 1:
-                    free_of_chain(after_sum, j, lo, hi, kb)
             elif kind == "T":
                 a, b = lo - 256, hi - 256
                 pb = S("p7", a, b)
                 mm([(pb, S("BE", 15 - k, 143 - k), S("YA", 16 * lo + k, 16 * hi, 16), k == 0, False) for k in range(16)]
                    + [(pb, S("IBG"), S("F2", a, b), False, False), (pb, S("I1"), S("PEN", a, b), False, True)])
-                free_of_chain(act, S("K2", a, b), pb, AF.Identity, KB)
 
         chain[0] = True
         for tok in PLAN.split():
@@ -494,10 +494,10 @@ def rank_program(g, core, T, topo):
         act(S("DD"), IND(S("LID"), S("OFF", 2, 10)), AF.Identity, bias=5.0 * t)
         mm([(S("p7", 0, 128), S("I1"), S("BB"), True, False), (S("p7", 32, 128), S("I1"), S("VP"), False, False)])
         mm([(S("p7", 32 * x, 32 * x + 32), S("ONB"), S("SL"), False, False) for x in range(4)]
-           + [(S("p7", 0, 32), S("O1"), S("SX"), False, True),
-              (S("p7", 128, 160), S("I16"), S("PS"), True, False), (S("p7", 128, 160), S("OKW"), S("SL"), False, True),
-              (S("p7", 160, 192), S("O1"), S("SL"), True, True)])
-        scan(S("WR"), S("MD"), S("p7", 0, 192), 0.0, A.add, A.max)
+           + [(S("p7", 0, 32), S("O1"), S("SX"), False, True)])
+        mm([(S("p3", 0, 32), S("I16"), S("PS"), True, False), (S("p3", 0, 32), S("OKW"), S("SL"), False, True)])
+        scan(S("WR", 0, 128), S("MD", 0, 128), S("p7", 0, 128), 0.0, A.add, A.max)
+        scan(S("WR", 128, 160), S("MD", 0, 32), S("p3", 0, 32), 0.0, A.add, A.max)
         act(S("WB"), S("WR", 15, 128, 16), AF.Identity, bias=CBI, scale=-SC2)
         ts(S("NO", 0, 8), S("WR", 15, 128, 16), COF, 511.0, A.add, A.min)
         for h in range(2):
@@ -507,24 +507,24 @@ def rank_program(g, core, T, topo):
         mm([(S("p0", 0, 32), S("I1"), S("VP", 0, 32), True, True), (S("p0", 32, 64), S("O1"), S("SX"), True, True)])
         cp(S("CN"), IND(S("NE"), S("NO", 0, 8)))
         ts(S("EM"), S("CN", 0, 64), 0.0, None, A.is_equal)
-        mm([(S("p1", 0, 64), S("O1"), S("EM"), True, True), (S("p2", 0, 64), S("TRI"), S("EM"), True, True)])
+        mm([(S("p1", 0, 64), S("O1"), S("EM"), True, False), (S("p1", 0, 32), S("O256"), S("SL"), False, False),
+            (S("p1", 32, 64), S("O256"), S("SL"), False, True)])
+        mm([(S("p2", 0, 64), S("TRI"), S("EM"), True, True)])
         scan(S("W2"), S("MD", 0, 64), S("p1", 0, 64), 0.0, A.add, A.max)
-        tt(S("OK", 0, 2), S("W2", 15, 32, 16), S("W2", 47, 64, 16), A.min)
-        tt(S("OK", 2, 4), S("OK", 0, 2), S("WR", 175, 192, 16), A.min)
-        ts(S("OK", 4, 6), S("OK", 2, 4), OFD, 4096.0, A.is_ge, A.mult)
+        ts(S("OK", 0, 4), S("W2", 15, 64, 16), OFD, 4096.0, A.is_ge, A.mult)
         ts(S("XF", 0, 8), S("NO", 0, 8), -1.0, 4096.0, A.mult, A.add)
         ts(S("XF", 8, 10), do, -0.75, col("CF", 17 + t), A.mult, A.add)
         for h in range(2):
-            ts(S("XP", h, 10, 2), S("XF", h, 10, 2), col("OK", 4 + h), CC2 - 4096.0, A.min, A.add)
-            ts(S("XM", h, 10, 2), S("XP", h, 10, 2), col("CM", 256 * h + 255), None, A.min)
+            ts(S("XP", h, 10, 2), S("XF", h, 10, 2), col("OK", h), col("OK", 2 + h), A.min, A.min)
+            ts(S("XM", h, 10, 2), S("XP", h, 10, 2), CC2 - 4096.0, col("CM", 256 * h + 255), A.add, A.min)
         tt(S("XN"), S("XM"), S("DUM"), A.max)
         ts(S("SO"), S("XN"), -1.0, CC2, A.mult, A.add)
         tt(S("KP"), S("CN"), S("DD"), A.not_equal)
-        act(S("FM"), S("p2", 0, 64), AF.Relu)
+        ts(S("FM"), S("p2", 0, 64), 0.0, None, A.max)
         act(S("OT"), S("p0", 0, 64), AF.Identity, bias=300.0, scale=-1.0)
         tt(S("M1"), S("FM"), S("DD", 0, 64), A.mult)
         if not lastr:
-            cp(S("CR"), IND(S("FAR"), S("NO", 0, 8)))
+            act(S("CR"), IND(S("FAR"), S("NO", 0, 8)), AF.Identity)
             tt(S("M2"), S("FM"), S("OT"), A.mult)
             tt(S("N1", 0, 64), S("CN", 0, 64), S("M1"), A.add)
             tt(S("N2", 0, 64), S("CR", 0, 64), S("M2"), A.add)
@@ -539,8 +539,10 @@ def rank_program(g, core, T, topo):
             tt(IND(S("NOUT"), S("SO", 4, 8)), S("N1", 64, 128), S("C3"), A.add)
             tt(IND(S("NOUT"), S("SO", 0, 4)), S("N2", 0, 64), S("C3"), A.add)
         act(S("SG"), S("KEY"), AF.Sign, bias=col("AC", 1 if t == 0 else 3 + t))
-        tt(S("T2"), S("SG"), S("OWN", 288 * t, 288 * t + 256), A.add)
-        ts(S("YW", 16 + 5 * t, 3088, 12), IND(S("T2"), S("POFF")), 0.0, 63.0, A.max, A.min)
+        mm([(S("p4", 0, 256), S("I1"), S("OWN", 288 * t, 288 * t + 256), True, False), (S("p4", 0, 256), S("I1"), S("SG"), False, True)])
+        act(S("T2", 0, 256), S("p4", 0, 256), AF.Relu)
+        act(S("T2", 256, 512), S("T2", 0, 256), AF.Relu, bias=63.0, scale=-1.0)
+        act(S("YW", 16 + 5 * t, 3088, 12), IND(S("T2", 256, 512), S("POFF")), AF.Identity, bias=63.0, scale=-1.0)
         ts(S("NO", 8, 10), S("WR", 143, 160, 16), CKA, None, A.add)
         tt(S("YS"), IND(S("YA", 4096, 8192), S("NO", 8, 10)), S("YE"), A.add)
         ts(S("YI"), S("YS"), 0.5, -0.25, A.mult, A.add)

@@ -1,3 +1,4 @@
+import numpy as np
 from concourse.bass import DstId, RemoteDMATransfer
 from concourse.mybir import AluOpType, AxisListType, ActivationFunctionType
 
@@ -7,45 +8,75 @@ N, RO = 8, 3
 L = 128
 CH = [(0, 64), (64, 128), (128, 256), (256, 384), (384, 448), (448, 512)]
 PRE = [(0, 64), (64, 256), (256, 512)]
-PLAN = ("Q0 P0 O0 D00 P1 Y00a D01 O2 A00 Q1 A01 O1 Y10v D11 D10 A11 A10 Q2 S0 S1 P2 C0 D23 D20 F4 D21 A23 A20 D22 C1 Y20a A21 A22 X0 D30 X1 "
-        "Z01 Z00 R01v R00a D33 A30 Y21a Z11 A33 Z10 U00 S2 R10a D32 D31 D40 A32 A31 U01 R11v D51 A40 Y31a Y30a D41 C2 F3 X2 Z21 K0 A41 U10 S3 "
-        "R21v U11 N3 K1 Z22 C3 R22v D50 A51 Z20 A50 Z23 X3 R20a R23a T3 U20 Y40a U21 Z31 S4 U22 E3 S5 U23 N4 R31a Z30 T4 C4 Z32 R30v K2 Z33 "
-        "U30 Y50a U31 C5 X4 R32a Z40 R33a Z41 X5 R40a U32 U33 F5 R41a E4 Z50 Z51 N5 R50a U40 U41 K3 R51v U50 U51 T5 E5 K4 K5")
+YENG = "vvaavvaaaaaaaaaa"
+PENG = ("aaa", "aaa", "aaa")
+CHAINED = False
+CNE = "v"
+CLIP = ((3, 4), (3, 4), (3, 4))
+STAGES = (("P", 3), ("D", 1), ("Y", 1), ("X", 0), ("SCN", 1), ("MFTE", 0), ("RUK", -1))
+
+
+def round_plan():
+    out = []
+    for s in range(-3, len(CH) + 1):
+        for kinds, j in STAGES:
+            j += s
+            if not 0 <= j < len(CH):
+                continue
+            lo, hi = CH[j]
+            for k in kinds:
+                if k == "P":
+                    out += ["%s%d" % (x, PRE.index(p)) for p in PRE if p[0] == lo for x in "POQ"]
+                elif k == "D":
+                    out += ["%s%d%d" % (x, j, b) for b in range((hi - lo) // 32) for x in "DA"]
+                elif k == "Y":
+                    on, b = YENG[lo // 32:hi // 32], 0
+                    while b < len(on):
+                        more = 2 if on[b:b + 2] in ("aa", "vv") else 1
+                        out.append("Y%d%d%s%d" % (j, b, on[b], more))
+                        b += more
+                elif k not in "NFTE" or lo >= 256:
+                    out.append("%s%d" % (k, j))
+    return " ".join(out)
+
+
+PLAN = round_plan()
 GPLAN = "vavavava"
-ND, NZ = 3, 2
+ND = 5
 CEN = 256.0 * 18600
 BIGK = 10485760.0
 KEYMAX = 4800000.0
 BD = 8192.0
 LIM = 12000000.0
 SC2 = 1048576.0
-CC2 = 126976.0
+CC2 = 131072.0
+CUT, LOW, HIGH, NONE = 1024, 16, 1040, 4111
 
 F32, BF, I32, U16, F16 = "float32", "bfloat16", "int32", "uint16", "float16"
 SB = {
-    "YW": (3136, BF), "W": (3088, BF), "ENR": (3136, F32), "SVC": (8, BF),
+    "YW": (4160, BF), "YL": (1024, BF), "W": (3088, BF), "ENR": (3136, F32), "SVC": (8, BF),
     "EB": (192, I32), "EBF": (192, F32), "EI": (384, I32), "PC": (384, BF),
     "NEI": (512, I32), "NEO": (512, U16), "NE": (640, F32), "FAR": (640, F32), "NOUT": (640, F32),
-    "G": (8192, BF), "RM": (24, F32), "SEL": (2048, BF), "SELH": (2048, F16), "RST": (16 * L, BF),
-    "OWN": (3 * 288, BF), "LAND": (3 * 288, BF), "UVO": (3 * 64, U16), "WL": (768, BF), "UV": (3 * 512, BF),
+    "RM": (24, F32), "SEL": (2048, BF), "RST": (16 * L, BF), "TR": (2 * 16 * 544, BF), "O4K": (128, BF), "ON256": (128, BF),
+    "LN": (3 * 576, BF), "IN64": (128, BF), "UVO": (3 * 64, U16), "UV": (3 * 512, BF),
     "KOUT": (3 * 256, F32), "KIN": (3 * 256, F32),
     "AO": (512, U16), "CO": (512, U16), "SS": (512, BF), "X1": (512, BF), "X2": (512, F16),
-    "AB": (2 * 16 * L, F32), "MN": (2 * 16 * L, F32), "YA": (8192, BF), "MM": (8192, BF), "RR": (4 * 512, BF),
+    "AB": (8192, F16), "MN": (8192, F16), "YA": (8192, BF), "MM": (8192, BF), "RR": (4096, BF),
     "PEN": (256, BF), "F2": (256, BF), "K2": (256, F32), "KEY": (256, F32), "SC": (512, F32),
     "SG": (256, BF), "T2": (512, BF),
-    "IOT": (144, F32), "C3": (64, F32), "QG": (128, BF), "T16": (192, F32), "LI": (48, F32), "LID": (256, F32),
+    "IOT": (144, F32), "C3": (64, F32), "QG": (128, BF), "T16": (128, BF), "LI": (144, F32), "LID": (768, F32),
     "BBI": (128, BF), "BB": (128, BF), "CX": (512, BF), "JJ": (256, BF), "BE": (144, BF),
     "I1": (128, BF), "IN1": (128, BF), "IN8": (128, BF), "IBG": (128, BF), "I16": (128, BF),
     "O1": (128, BF), "O256": (128, BF), "ONB": (128, BF), "OKW": (128, BF), "TRI": (128, BF),
-    "MMN": (128, BF), "MMX": (128, BF), "E1": (192, BF), "E2": (192, BF), "MD": (192, BF),
-    "PI": (8, I32), "CF": (32, F32), "LOFF": (48, U16), "POFF": (16, U16), "DUM": (10, F32), "C256": (4, F32),
+    "MMN": (128, BF), "MMX": (128, BF), "E1": (128, BF), "E2": (128, BF), "MD": (128, BF),
+    "PI": (8, I32), "CF": (32, F32), "LOFF": (96, U16), "POFF": (16, U16), "DUM": (12, F32), "C256": (4, F32),
     "THI": (8, I32), "THF": (8, F32), "THB": (8, F32), "THM": (8, F32), "AC": (16, F32), "AI": (8, I32),
     "Q": (16, I32), "OFF": (10, U16), "KE": (32, F32), "TT": (48, F32), "MV": (2, F32), "EQ": (32, BF), "SL": (32, BF),
-    "SE": (32, BF), "SX": (32, BF), "VP": (96, BF), "PS": (32, BF), "YE": (32, BF), "DD": (128, F32),
+    "SX": (32, BF), "VP": (96, BF), "PS": (32, BF), "YE": (32, BF), "DD": (128, F32),
     "WR": (192, F32), "WB": (8, F32), "NO": (10, U16), "AX": (1024, BF), "CM": (1024, BF),
-    "CN": (128, F32), "CR": (128, F32), "EM": (64, BF), "KP": (128, F32), "FM": (64, F32), "OT": (64, F32),
-    "M1": (64, F32), "M2": (64, F32), "N1": (128, F32), "N2": (128, F32),
-    "W2": (64, F32), "OK": (8, F32), "XF": (10, F32), "XP": (10, F32), "XM": (10, F32), "XN": (10, F32), "SO": (10, U16),
+    "CN": (128, F32), "CR": (128, F32), "EM": (64, BF), "KP": (128, F32), "IF": (128, F32), "CB": (128, BF),
+    "TRN": (128, BF), "ON1": (128, BF), "N1": (128, F32), "N2": (128, F32),
+    "W2": (64, F32), "OK": (8, F32), "XF": (16, F32), "XP": (12, F32), "XM": (12, F32), "XN": (12, F32), "SO": (12, U16),
     "YS": (32, F32), "YI": (32, I32), "LH": (96, F32), "GO": (2, BF),
 }
 SCRATCH = {k: ("sbuf", [128, w], d) for k, (w, d) in SB.items()}
@@ -55,6 +86,64 @@ SEMAPHORES = ["sv", "sa", "sp", "sg", "sent"] + ["d%d" % i for i in range(16)] +
     + ["kin%d" % i for i in range(RO * 4)]
 
 CYC, PCYC, GATH, SCAT, WAKE = 0.95, 0.475, 1.55, 3.5, 150.0
+PASSES = 600
+JOG = 1500.0
+REACH = 6000.0
+SEED = 0
+ORDER = {}
+
+
+def arrange(ops):
+    n = len(ops)
+    busy = [o["busy"] for o in ops]
+    pred, succ = [[] for _ in ops], [[] for _ in ops]
+    for k, o in enumerate(ops):
+        for i in o["hard"] | o["soft"]:
+            lag = ops[i]["cost"] + WAKE if i in o["hard"] else ops[i]["cost"] if o["eng"] == "x" else busy[i]
+            pred[k].append((i, lag))
+            succ[i].append((k, lag + busy[k] - busy[i]))
+
+    def place(key, before, after, first):
+        at, left = list(first), [len(x) for x in before]
+        pool = [(key[i], i) for i in range(n) if not left[i]]
+        taken = {e: [] for e in "vapgsx"}
+        while pool:
+            i = min(pool)
+            pool.remove(i)
+            i = i[1]
+            t0 = at[i]
+            row = taken[ops[i]["eng"]]
+            x = len(row)
+            while x and row[x - 1][1] > t0:
+                x -= 1
+            while x < len(row) and row[x][0] < t0 + busy[i]:
+                t0 = max(t0, row[x][1])
+                x += 1
+            row.insert(x, (t0, t0 + busy[i]))
+            at[i] = t0
+            for k, lag in after[i]:
+                if at[k] < t0 + lag:
+                    at[k] = t0 + lag
+                left[k] -= 1
+                if not left[k]:
+                    pool.append((key[k], k))
+        return at
+
+    fore = [[(k, lag + busy[i] - busy[k]) for k, lag in succ[i]] for i in range(n)]
+    back = [[(i, lag + busy[k] - busy[i]) for i, lag in pred[k]] for k in range(n)]
+    rest, span, cost = [ops[i]["cost"] - busy[i] for i in range(n)], np.array(busy), np.array([o["cost"] for o in ops])
+    key, best = -np.arange(n), None
+    rng = np.random.RandomState(SEED)
+    for p in range(PASSES):
+        path = np.array(place(key.tolist(), succ, back, rest))
+        fw = np.array(place((-path - span).tolist(), pred, fore, [0.0] * n))
+        end = float((fw + cost).max())
+        if best is None or end <= best[0]:
+            best = (end, fw)
+        near = np.abs(best[1] - best[0] * rng.rand()) < REACH
+        key = -best[1] - span - JOG * rng.rand() * rng.rand(n) * near * (rng.rand(n) < 0.3)
+    ORDER["end"] = best[0]
+    return best[1].tolist()
 
 
 def rank_program(g, core, T, topo):
@@ -157,6 +246,9 @@ def rank_program(g, core, T, topo):
         return add("a", lambda: g.scalar.activation(out["ap"], in0["ap"], f, bias=val(bias), scale=val(scale)), [out], [in0, bias, scale],
                    65 + max(64, in0["n"] * (GATH if in0["ind"] else 1)) * CYC)
 
+    def lin(eng, out, in0, scale, bias):
+        return ts(out, in0, scale, bias, A.mult, A.add) if eng == "v" else act(out, in0, AF.Identity, bias=bias, scale=scale)
+
     def mm(items):
         def fn():
             r = None
@@ -164,7 +256,7 @@ def rank_program(g, core, T, topo):
                 r = g.tensor.matmul(o["ap"], l["ap"], x["ap"], st, sp)
             return r
         return add("p", fn, [it[0] for it in items], [it[1] for it in items] + [it[2] for it in items],
-                   40 + sum(max(64, it[2]["n"]) for it in items) * PCYC)
+                   40 + sum(max(64, it[2]["n"]) * (4 if it[2]["dt"] == F32 else 1) for it in items) * PCYC)
 
     def iota(out, pat, base, cm):
         def fn():
@@ -175,6 +267,9 @@ def rank_program(g, core, T, topo):
 
     def pick(out, in0, op, fill):
         return add("g", lambda: g.affine_select(out["ap"], in0["ap"], [[1, 128]], op, fill, 0, -1), [out], [in0], 170 + 256 * CYC)
+
+    def spread(out, in0):
+        return add("g", lambda: g.affine_select(out["ap"], in0["ap"], [[0, in0["n"]]], A.is_equal, 0.0, 0, 0), [out], [in0], 170 + 2 * in0["n"] * CYC)
 
     ndma = [0]
 
@@ -194,16 +289,18 @@ def rank_program(g, core, T, topo):
 
     dma("s", S("EB"), T.ends0[:], 2200)
     dma("a", S("NEI"), T.ne0[:], 2500)
-    dma("s", S("YW", 16, 3088), T.y0[:], 4500)
+    dma("s", S("YL"), T.y0[:, 0:CUT], 3200)
+    dma("s", S("YW", CUT + HIGH, NONE + 1), T.y0[:, CUT:], 4500)
     chain[0] = True
     iota(col("PI", 0), [[0, 1]], 0, 1)
     iota(S("QG"), [[1, 8], [0, 16]], 0, 0)
-    iota(S("T16"), [[0, 12], [1, 16]], 0, 0)
-    iota(S("LI"), [[5, 3], [12, 16]], 16, 0)
+    iota(S("T16"), [[0, 8], [1, 16]], 0, 0)
+    iota(S("LI", 0, 48), [[5, 3], [12, 16]], 16, 0)
     iota(S("IOT"), [[1, 144]], 0, 0)
     iota(S("CX"), [[1, 512]], -256, 0)
-    iota(S("JJ"), [[1, 256]], 0, 0)
     chain[0] = False
+    iota(S("JJ"), [[1, 256]], 0, 0)
+    iota(dict(S("YW", LOW + 1, CUT + HIGH, 2), acc=S("YW", LOW, CUT + HIGH)["acc"]), [[0, CUT]], 0, 0)
     RF, GF = col("CF", 0), col("CF", 1)
     R15, R192, R16, G16, R1, R1W, INI, INX, NBC, KB, COF, CBI, CKA, CYO, OFD = [col("CF", c) for c in range(2, 17)]
     boost[0] = 2e6
@@ -213,9 +310,9 @@ def rank_program(g, core, T, topo):
     ts(col("PI", 2), col("PI", 0), 4, None, A.logical_shift_right)
     ms(S("YW", 0, 16), 255.0)
     cp(S("CF", 0, 2), S("PI", 1, 3))
-    ms(S("YW", 3088, 3136), 0.0)
+    ms(S("YW", NONE + 1, 4160), 0.0)
     ts(S("O1"), S("QG"), GF, None, A.is_equal)
-    ts(S("RM", 0, 16), S("T16", 0, 16), RF, 8192.0, A.is_equal, A.mult)
+    ts(S("RM", 0, 16), S("T16", 0, 16), RF, None, A.is_equal)
     ts(col("CF", 20), RF, 15.0, 2304.0, A.is_equal, A.mult)
     ts(R192, RF, 192.0, None, A.mult)
     ms(S("W", 768, 3088), 0.0)
@@ -224,11 +321,19 @@ def rank_program(g, core, T, topo):
     ts(S("PC", 0, 191), S("EI", 0, 191), -256.0, None, A.add)
     ts(col("PC", 191), col("EI", 191), -256.0, col("CF", 20), A.add, A.add)
     ts(S("PC", 192, 384), S("EI", 192, 384), -256.0, None, A.add)
-    ts(S("LOFF"), S("LI"), R192, None, A.add)
+    ts(S("LOFF", 0, 48), S("LI", 0, 48), R192, None, A.add)
+    ts(S("LI", 48, 96), S("LOFF", 0, 48), 2.0, -16.0, A.mult, A.add)
+    ts(S("LI", 96, 144), S("LOFF", 0, 48), 1024.0, None, A.add)
+    tt(S("LI", 0, 48), S("LI", 48, 96), S("LI", 96, 144), A.min)
+    cp(S("LOFF", 48, 96), S("LI", 0, 48))
+    cp(S("YW", LOW, CUT + HIGH, 2), S("YL"))
     ts(S("NEO"), S("NEI"), 16.0, None, A.add)
     ts(G16, GF, 16.0, 15.0, A.mult, A.add)
     ts(S("BE"), S("IOT", 0, 144), G16, 8192.0, A.is_equal, A.mult)
     ts(S("NE", 0, 512), S("NEI"), -3071.0, None, A.add)
+    chain[0] = False
+    act(S("p7"), S("NE", 0, 512), AF.Relu, bias=-2047.0, scale=-1.0)
+    tt(S("NE", 0, 512), S("NE", 0, 512), S("p7"), A.subtract)
     ms(S("NE", 512, 640), 0.0)
     ms(S("FAR", 512, 640), 0.0)
     chain[0] = False
@@ -236,10 +341,6 @@ def rank_program(g, core, T, topo):
     for m in range(16):
         boost[0] = 1e6 if m < 12 else 0.4e6
         act(S("SEL", 128 * m, 128 * m + 128), S("O1"), AF.Identity, scale=col("RM", m))
-    boost[0] = 1e6
-    ts(S("SELH", 0, 1024), S("SEL", 0, 1024), 1.0 / 8192, None, A.mult)
-    boost[0] = 0.4e6
-    ts(S("SELH", 1024, 2048), S("SEL", 1024, 2048), 1.0 / 8192, None, A.mult)
     boost[0] = 0.0
     ts(R15, RF, 15.0, None, A.is_equal)
     ts(R16, RF, 16.0, None, A.mult)
@@ -252,18 +353,20 @@ def rank_program(g, core, T, topo):
     ts(CBI, R15, -BD * SC2, (BD + 0.125) * SC2, A.mult, A.add)
     ts(CKA, R15, BD, -BD, A.mult, A.add)
     for t in range(RO):
-        ts(col("CF", 17 + t), RF, -191.25, 4080.0 - 5 * t, A.mult, A.add)
+        ts(col("CF", 17 + t), RF, -191.25, 8176.0 - 5 * t, A.mult, A.add)
     ts(OFD, R15, -BD, BD + 256.5, A.mult, A.add)
     ts(S("POFF"), S("IOT", 0, 16), R16, None, A.add)
     ts(S("XM", 0, 8), S("IOT", 0, 128, 16), RF, 512.0, A.add, A.add)
     ts(S("XM", 8, 10), S("IOT", 0, 32, 16), RF, 3088.0, A.add, A.add)
+    ts(S("XM", 10, 12), S("IOT", 0, 32, 16), RF, NONE + 1.0, A.add, A.add)
     ts(S("DUM"), S("XM"), -1.0, CC2, A.mult, A.add)
     ms(S("C256"), 1.0 / 256)
-    for nm, c in (("O256", 256.0), ("ONB", -1024.0), ("OKW", RF)):
+    ms(dict(S("TR", 0, 2 * 16 * 544, 16), acc=S("TR")["acc"]), 255.0)
+    for nm, c in (("O256", 256.0), ("ONB", -1024.0), ("OKW", RF), ("O4K", 4096.0), ("ON256", -256.0), ("ON1", -1.0)):
         ts(S(nm), S("QG"), GF, c, A.is_equal, A.mult)
     chain[0] = True
     pick(S("I1"), S("O1"), A.is_equal, 0.0)
-    for nm, c in (("IN8", -8192.0), ("IN1", -1.0)):
+    for nm, c in (("IN8", -8192.0), ("IN64", -64.0), ("IN1", -1.0)):
         pick(S(nm), S("I1"), A.not_equal, c)
     chain[0] = False
     ts(S("E1", 0, 128), S("T16", 0, 128), RF, BIGK, A.is_equal, A.mult)
@@ -272,6 +375,7 @@ def rank_program(g, core, T, topo):
     tt(S("MMX"), S("E2", 0, 128), S("E1", 0, 128), A.subtract)
     ts(S("E1"), S("T16"), RF, -3 * BD, A.is_equal, A.mult)
     ts(S("E2"), S("T16"), R1, BD, A.is_equal, A.mult)
+
     tt(S("MD"), S("E1"), S("E2"), A.add)
     boost[0] = 2e6
     dma("s", S("W", 16, 3088, part=slice(0, 128, 16)), S("PC", 0, 192), 2200)
@@ -280,24 +384,24 @@ def rank_program(g, core, T, topo):
     ops[j]["hard"].update(ops[j - 1]["hard"])
     last_w["W"].append((j - 1, last_w["W"][-1][1]))
     for t in range(RO):
-        act(S("OWN", 288 * t, 288 * t + 256), IND(S("YW"), S("LOFF", 16 * t, 16 * t + 16)), AF.Identity)
+        act(S("LN", 576 * t + 288, 576 * t + 544), IND(S("YW"), S("LOFF", 48 + 16 * t, 64 + 16 * t)), AF.Identity, bias=12.0)
         for s in range(2):
-            act(S("OWN", 288 * t + 256 + 16 * s, 288 * t + 272 + 16 * s), S("PC", 192 * s + 5 * t, 192 * s + 192, 12), AF.Identity)
+            act(S("LN", 576 * t + 544 + 16 * s, 576 * t + 560 + 16 * s), S("PC", 192 * s + 5 * t, 192 * s + 192, 12), AF.Identity)
     boost[0] = 0.0
     for t in range(RO):
-        ts(S("UVO", 64 * t + 32, 64 * t + 64), S("OWN", 288 * t + 256, 288 * t + 288), 256.0, None, A.add)
-    cp(col("SVC", 0), col("YW", 3087))
-    ms(col("YW", 3087), 255.0)
+        ts(S("UVO", 64 * t + 32, 64 * t + 64), S("LN", 576 * t + 544, 576 * t + 576), 256.0, None, A.add)
+    cp(col("SVC", 0), col("YW", NONE))
+    ms(col("YW", NONE), 255.0)
     boost[0] = 0.5e6
     for c in range(8):
-        o, src = S("G", 1024 * c, 1024 * c + 1024), IND(S("W"), S("NEO", 64 * c, 64 * c + 64))
+        o, src = S("MM", 1024 * c, 1024 * c + 1024), IND(S("W"), S("NEO", 64 * c, 64 * c + 64))
         if GPLAN[c] == "v":
             cp(o, src)
         else:
             act(o, src, AF.Identity)
         pb = S("p%d" % (c // 2), 64 * (c % 2), 64 * (c % 2) + 64)
         mm([(pb, S("IN8"), S("CX", 64 * c, 64 * c + 64), True, False)]
-           + [(pb, S("BE", 15 - k, 143 - k), S("G", 1024 * c + k, 1024 * c + 1024, 16), False, k == 15) for k in range(16)])
+           + [(pb, S("BE", 15 - k, 143 - k), S("MM", 1024 * c + k, 1024 * c + 1024, 16), False, k == 15) for k in range(16)])
         if c % 2:
             act(S("FAR", 64 * c - 64, 64 * c + 64), S("p%d" % (c // 2), 0, 128), AF.Relu, bias=300.0, scale=-1.0 / 8192)
     boost[0] = 0.0
@@ -312,23 +416,30 @@ def rank_program(g, core, T, topo):
             k = len(en) // 2 if t == 0 else len(en) // 4
             rid, pid, _s = topo.addr(peers[t])
             trs.append(RemoteDMATransfer(dst_ids=[DstId(rid=rid, pnc=pid)], dma_engine_mask=sum(1 << e for e in en[at:at + k]),
-                                         remote_sem=T.sem["ln%d" % t], src=T.OWN[:, 288 * t:288 * t + 288], dst=T.LAND[:, 288 * t:288 * t + 288]))
+                                         remote_sem=T.sem["ln%d" % t], src=T.LN[:, 576 * t + 288:576 * t + 576], dst=T.LN[:, 576 * t:576 * t + 288]))
             at += k
         sent[0] += at
         return g.remote_dma_fused(trs, local_sem=T.sem.sent)
-    js = add("g", send_lanes, [], [S("OWN")], 3500, "rem", busy=1500)
-    readers["OWN"] = [x for x in readers["OWN"] if x[0] != js]
-    tail["g"] = js
-    chain[0] = True
+    js = add("g", send_lanes, [], [S("LN", 576 * t + 288, 576 * t + 576) for t in range(RO)], 3500, "rem", busy=1500)
     iota(S("RST"), [[0, L], [-16384, 16]], 16384, 0)
     dma("g", S("THI", part=slice(0, 1)), T.th[:], 2500, True)
     dma("g", S("ENR", 16, 3088), T.y0[:], 9000)
     iota(S("BBI"), [[0, 4], [1, 2], [2, 16]], 0, 0)
-    iota(S("LID"), [[12, 16], [192, 16]], -3071, 0)
+    for t in range(RO):
+        iota(S("LID", 256 * t, 256 * t + 256), [[12, 16], [192, 16]], 5 * t - 3071, 0)
+        for r in range(16 if t < RO - 1 else 0):
+            c = min(16, max(0, -((192 * r + 5 * t - CUT) // 12)))
+            if c:
+                iota(S("LID", 256 * t + r, 256 * t + 16 * c, 16), [[24, c]], 2 * (192 * r + 5 * t) + LOW - NONE, 0)
     for nm, c in (("IBG", 16777216.0), ("I16", 16.0)):
         pick(S(nm), S("I1"), A.not_equal, c)
-    pick(S("AX", 0, 128), S("ONB"), A.is_gt, 0.0)
-    pick(S("TRI"), S("AX", 0, 128), A.not_equal, 1.0)
+    for nm, c in (("TRI", 16384.0), ("TRN", -16384.0)):
+        ts(S("AX", 0, 128), S("QG"), GF, -2 * c, A.is_equal, A.mult)
+        pick(S("AX", 128, 256), S("AX", 0, 128), A.is_gt, 0.0)
+        pick(S(nm), S("AX", 128, 256), A.not_equal, c)
+    iota(S("IF"), [[0, 128]], 0, 0)
+    pick(S("IF"), S("IF"), A.not_equal, 1.0)
+    iota(S("CB"), [[-16084, 2], [0, 64]], 16384, 0)
     iota(S("C3"), [[0, 64]], 3071, 0)
     iota(S("ENR", 0, 16), [[0, 16]], 0, 0)
     iota(S("ENR", 3088, 3136), [[0, 48]], 0, 0)
@@ -338,14 +449,14 @@ def rank_program(g, core, T, topo):
     act(S("BB"), S("BBI"), AF.Identity, scale=1.0 / 128)
     for t in range(RO):
         ne_t = len(topo.engines(backs[t], core))
-        j = add("x", None, [S("LAND", 288 * t, 288 * t + 288)], [], 0, "arr", "ln%d" % t, ne_t // 2 if t == 0 else ne_t // 4)
+        j = add("x", None, [S("LN", 576 * t, 576 * t + 288)], [], 0, "arr", "ln%d" % t, ne_t // 2 if t == 0 else ne_t // 4)
         ops[j]["soft"].add(js)
-        ts(S("UVO", 64 * t, 64 * t + 32), S("LAND", 288 * t + 256, 288 * t + 288), 256.0, None, A.add)
-    act(S("WL"), IND(S("W"), S("LOFF")), AF.Identity)
-    for t in range(RO):
-        pb = "p%d" % (3 + t % 2)
-        mm([(S(pb, 256 * s, 256 * s + 256), S("SEL", 128 * s, 128 * s + 128), S("WL", 256 * t, 256 * t + 256), True, True) for s in range(2)])
-        act(S("UV", 512 * t, 512 * t + 512), S(pb), AF.Identity, scale=1.0 / 8192)
+        ts(S("UVO", 64 * t, 64 * t + 32), S("LN", 576 * t + 256, 576 * t + 288), 256.0, None, A.add)
+    def own_ends(t, pb):
+        mm([(S(pb, 256 * s + r, 256 * s + 256, 16), S("SEL", 128 * s, 128 * s + 128), S("W", 16 + 192 * r + 5 * t, 208 + 192 * r, 12), True, True)
+            for s in range(2) for r in range(16)])
+        act(S("UV", 512 * t, 512 * t + 512), S(pb), AF.Identity)
+    own_ends(0, "p6")
     cp(S("THF", part=slice(0, 1)), S("THI", part=slice(0, 1)))
     add("g", lambda: g.partition_broadcast(T.THB[:, :], T.THF[0:1, :], 128), [S("THB")], [S("THF")], 200)
     ts(S("THM"), S("IOT", 0, 8), GF, None, A.is_equal)
@@ -359,19 +470,32 @@ def rank_program(g, core, T, topo):
 
     for t in range(RO):
         lastr = t == RO - 1
-        dbank, zbank = {}, {}
+        dbank = {}
+        trb = 16 * 544 * (t % 2)
+        runs = []
+        for j, (lo, hi) in enumerate(CH):
+            if j not in CLIP[t]:
+                gap = 32 * (lo >= 256)
+                if runs and (runs[-1][1] == lo + gap or (t and runs[-1][1] == lo)):
+                    runs[-1][1] = hi + gap
+                else:
+                    runs.append([lo + gap, hi + gap])
+        for a, b in runs:
+            for k in range(1, 16):
+                spread(S("TR", trb + 16 * a + k, trb + 16 * b, 16), S("LN", 576 * t + a, 576 * t + b))
 
         def pre(kind, lo, hi):
             side, a, b = lo // 256, (lo % 256) // 16, (hi - 1) % 256 // 16 + 1
             uo = S("UVO", 64 * t + 32 * side + a, 64 * t + 32 * side + b)
             vo = S("UVO", 64 * t + 32 * side + 16 + a, 64 * t + 32 * side + 16 + b)
+            on = PENG[PRE.index((lo, hi))]
             if kind == "P":
-                act(S("SS", lo, hi), IND(S("FAR"), uo), AF.Identity, bias=300.0, scale=-1.0)
-                act(S("X1", lo, hi), IND(S("FAR"), vo), AF.Identity, bias=300.0, scale=-1.0)
+                lin(on[0], S("SS", lo, hi), IND(S("FAR"), uo), -1.0, 300.0)
+                lin(on[1], S("X1", lo, hi), IND(S("FAR"), vo), -64.0, 300.0 * 64)
             elif kind == "Q":
-                ts(S("X2", lo, hi), IND(S("NE"), vo), 1535.0, None, A.add)
+                lin(on[2], S("X2", lo, hi), IND(S("NE"), vo), -1.0 / 256, 1.0 / 256)
             else:
-                ts(S("AO", lo, hi), IND(S("NE"), uo), 3087.0, None, A.add)
+                ts(S("AO", lo, hi), IND(S("NE"), uo), float(NONE), None, A.add)
 
         def after_sum(j, lo, hi, kb):
             if lo < 256:
@@ -401,7 +525,7 @@ def rank_program(g, core, T, topo):
                 ts(S("Q", 4 + 4 * h, 8 + 4 * h), S("C256"), cd, -0.25 - 0.5 * h, A.mult, A.add)
                 ts(col("OFF", h), col("Q", h), -256.0, ce, A.mult, A.add)
                 ts(S("OFF", 2 + h, 10, 2), S("Q", 4 + 4 * h, 8 + 4 * h), -256.0, cd, A.mult, A.add)
-                chain[0] = True
+                chain[0] = CHAINED
 
         def step(tok):
             kind, j = tok[0], int(tok[1])
@@ -409,73 +533,81 @@ def rank_program(g, core, T, topo):
                 return pre(kind, *PRE[j])
             lo, hi = CH[j]
             w = hi - lo
-            nm, nb, ab = 512 // w, w // 32, 16 * L * (j % 2)
+            nm, nb, ab = 512 // w, w // 32, 16 * (lo % 256)
             bk = int(tok[2]) if len(tok) > 2 else 0
+            at = lo if lo < 256 else lo + 32
+            top = S("LN", 576 * t + at, 576 * t + at + w)
+            kb = S("p%d" % (5 + j % 2), 0, w)
             if kind == "D":
                 pb = dbank[j, bk] = "p%d" % (ring["d"] % ND)
                 ring["d"] += 1
                 it = []
                 for x in range(nm):
                     m, o = nm * bk + x, S(pb, x, 512, nm)
-                    it += [(o, S("IN8"), S("SS", lo, hi), True, False), (o, S("SEL", 128 * m, 128 * m + 128), S("X1", lo, hi), False, False),
-                           (o, S("SELH", 128 * m, 128 * m + 128), S("X2", lo, hi), False, True)]
+                    it += [(o, S("IN64"), S("SS", lo, hi), True, False), (o, S("SEL", 128 * m, 128 * m + 128), S("X1", lo, hi), False, False),
+                           (o, S("SEL", 128 * m, 128 * m + 128), S("X2", lo, hi), False, True)]
                 mm(it)
             elif kind == "A":
-                act(S("AB", ab + bk, ab + 16 * w, nb), S(dbank[j, bk]), AF.Abs, bias=-1535.0)
+                act(S("AB", 16 * lo + bk, 16 * hi, nb), S(dbank[j, bk]), AF.Abs)
             elif kind == "S":
-                scan(S("MN", ab, ab + 16 * w), S("RST", 0, 16 * w), S("AB", ab, ab + 16 * w), 0.0, A.max, A.min)
+                for a in range(lo, hi, L):
+                    b = min(hi, a + L)
+                    scan(S("MN", 16 * a, 16 * b), S("RST", 0, 16 * (b - a)), S("AB", 16 * a, 16 * b), 0.0, A.max, A.min)
             elif kind == "C":
-                ts(S("CO", lo, hi), S("MN", ab + 15, ab + 16 * w, 16), -1.0, 3087.0, A.mult, A.add)
+                ts(S("CO", lo, hi), S("MN", 16 * lo + 15, 16 * hi, 16), -256.0, NONE + 1.0, A.mult, A.add)
             elif kind == "N":
-                act(S("PEN", lo - 256, hi - 256), S("MN", ab + 15, ab + 16 * w, 16), AF.Relu, bias=67108864.0, scale=-16384.0)
+                act(S("PEN", lo - 256, hi - 256), S("MN", 16 * lo + 15, 16 * hi, 16), AF.Relu, bias=33554432.0, scale=-1048576.0)
             elif kind == "F":
                 tt(S("F2", lo - 256, hi - 256), S("SS", lo, hi), S("UV", 512 * t + lo, 512 * t + hi), A.is_equal)
             elif kind == "K":
-                after_sum(j, lo, hi, S("p%d" % (5 + j % 2), 0, w))
+                after_sum(j, lo, hi, kb)
             elif kind == "E":
                 act(S("K2", lo - 256, hi - 256), S("p7", lo - 256, hi - 256), AF.Identity, KB)
             elif kind == "Y":
-                a = lo + 64 * bk
-                o, src = S("YA", 16 * a, 16 * a + 1024), IND(S("YW"), S("AO", a, a + 64))
+                a = lo + 32 * bk
+                b = a + 32 * int(tok[4])
+                o, src = S("YA", 16 * a, 16 * b), IND(S("YW"), S("AO", a, b))
                 if tok[3] == "v":
                     cp(o, src)
                 else:
                     act(o, src, AF.Identity)
             elif kind == "X":
                 tt(S("MM", 16 * lo, 16 * hi), IND(S("YW"), S("CO", lo, hi)), S("YA", 16 * lo, 16 * hi), A.max)
-            elif kind == "Z":
-                pb = "p%d" % (ND + ring["z"] % NZ)
-                zbank[j, bk] = (pb, 512 * (ring["z"] % 4))
-                ring["z"] += 1
-                ye = S("LAND", 288 * t + lo, 288 * t + hi) if lo < 256 else S("OWN", 288 * t + lo - 256, 288 * t + hi - 256)
-                it = []
-                for x in range(nm):
-                    o = S(pb, w * x, w * x + w)
-                    it += [(o, S("I1"), ye, True, False), (o, S("IN1"), S("MM", 16 * lo + nm * bk + x, 16 * hi, 16), False, True)]
-                mm(it)
+            elif kind in "MRU" and j in CLIP[t]:
+                for b in range(nb if kind != "M" else 0):
+                    r0 = ab + 512 * b
+                    if kind == "R":
+                        pb = "p%d" % (ring["d"] % ND)
+                        ring["d"] += 1
+                        mm([it for x in range(nm) for it in ((S(pb, w * x, w * x + w), S("I1"), top, True, False),
+                                                            (S(pb, w * x, w * x + w), S("IN1"), S("MM", 16 * lo + nm * b + x, 16 * hi, 16), False, True))])
+                        act(S("RR", r0, r0 + 512), S(pb), AF.Relu)
+                    else:
+                        mm([(kb, S("O256"), S("RR", r0 + w * x, r0 + w * x + w), b == 0 and x == 0, lo >= 256 and b == nb - 1 and x == nm - 1) for x in range(nm)]
+                           + ([(kb, S("I1"), S("JJ", lo, hi), False, True)] if lo < 256 and b == nb - 1 else []))
+            elif kind == "M":
+                tt(S("MM", 16 * lo, 16 * hi, 16), S("MM", 16 * lo, 16 * hi, 16), top, A.min)
             elif kind == "R":
-                pb, r0 = zbank[j, bk]
-                if tok[3] == "v":
-                    ts(S("RR", r0, r0 + 512), S(pb), 12.0, 0.0, A.add, A.max)
-                else:
-                    act(S("RR", r0, r0 + 512), S(pb), AF.Relu, bias=12.0)
+                scan(S("RR", ab, ab + 16 * w), S("TR", trb + 16 * at, trb + 16 * (at + w)), S("MM", 16 * lo, 16 * hi), 0.0, A.max, A.min)
             elif kind == "U":
-                r0 = zbank[j, bk][1]
-                kb = S("p%d" % (5 + j % 2 if ND + NZ == 5 else 6), 0, w)
-                it = [(kb, S("O256"), S("RR", r0 + w * x, r0 + w * x + w), bk == 0 and x == 0, lo >= 256 and bk == nb - 1 and x == nm - 1) for x in range(nm)]
-                if lo < 256 and bk == nb - 1:
-                    it.append((kb, S("I1"), S("JJ", lo, hi), False, True))
-                mm(it)
+                mm([(kb, S("O4K"), top, True, False)] + ([(kb, S("I1"), S("JJ", lo, hi), False, False)] if lo < 256 else [])
+                   + [(kb, S("ON256"), S("RR", ab + k, ab + 16 * w, 16), False, k == 15) for k in range(16)])
             elif kind == "T":
                 a, b = lo - 256, hi - 256
                 pb = S("p7", a, b)
                 mm([(pb, S("BE", 15 - k, 143 - k), S("YA", 16 * lo + k, 16 * hi, 16), k == 0, False) for k in range(16)]
                    + [(pb, S("IBG"), S("F2", a, b), False, False), (pb, S("I1"), S("PEN", a, b), False, True)])
 
-        chain[0] = True
+        if lastr:
+            act(S("p7"), S("NE", 0, 512), AF.Identity, bias=2047.5, scale=0.5)
+            act(S("NOUT", 0, 512), S("NE", 0, 512), AF.Identity, bias=3071.0)
+            tt(S("NOUT", 0, 512), S("NOUT", 0, 512), S("p7"), A.max)
+        chain[0] = CHAINED
         for tok in PLAN.split():
             step(tok)
         chain[0] = False
+        if not lastr:
+            own_ends(t + 1, "p0")
         eo, do = S("OFF", 0, 2), S("OFF", 2, 4)
         uw, vw = S("UV", 512 * t, 512 * t + 256), S("UV", 512 * t + 256, 512 * t + 512)
         cp(S("KE"), IND(S("K2"), eo))
@@ -489,9 +621,9 @@ def rank_program(g, core, T, topo):
         act(S("VP", 32, 64), IND(uw, do), AF.Identity)
         act(S("VP", 64, 96), IND(vw, do), AF.Identity)
         act(S("PS"), IND(S("JJ"), eo), AF.Identity)
-        act(S("YE"), IND(S("OWN", 288 * t, 288 * t + 256), eo), AF.Identity)
+        act(S("YE"), IND(S("LN", 576 * t + 288, 576 * t + 544), eo), AF.Identity, bias=-12.0)
         tt(S("SX"), IND(S("SS", 256, 512), eo), S("SL"), A.mult)
-        act(S("DD"), IND(S("LID"), S("OFF", 2, 10)), AF.Identity, bias=5.0 * t)
+        act(S("DD"), IND(S("LID", 256 * t, 256 * t + 256), S("OFF", 2, 10)), AF.Identity)
         mm([(S("p7", 0, 128), S("I1"), S("BB"), True, False), (S("p7", 32, 128), S("I1"), S("VP"), False, False)])
         mm([(S("p7", 32 * x, 32 * x + 32), S("ONB"), S("SL"), False, False) for x in range(4)]
            + [(S("p7", 0, 32), S("O1"), S("SX"), False, True)])
@@ -504,53 +636,58 @@ def rank_program(g, core, T, topo):
             for x in range(4):
                 act(S("AX", 512 * h + 128 * x, 512 * h + 128 * x + 128), S("p7", 0, 128), AF.Abs, bias=col("WB", 2 * x + h), scale=SC2)
             scan(S("CM", 256 * h, 256 * h + 256), S("AX", 512 * h, 512 * h + 256), S("AX", 512 * h + 256, 512 * h + 512), SC2, A.min, A.min)
-        mm([(S("p0", 0, 32), S("I1"), S("VP", 0, 32), True, True), (S("p0", 32, 64), S("O1"), S("SX"), True, True)])
-        cp(S("CN"), IND(S("NE"), S("NO", 0, 8)))
-        ts(S("EM"), S("CN", 0, 64), 0.0, None, A.is_equal)
+        mm([(S("p0", 0, 32), S("I1"), S("VP", 0, 32), True, False), (S("p0", 0, 32), S("O1"), S("SX"), False, True),
+            (S("p0", 32, 64), S("IN1"), S("VP", 0, 32), True, False), (S("p0", 32, 64), S("O1"), S("SX"), False, True)])
+        ts(S("EM"), IND(S("NE"), S("NO", 0, 4)), 0.0, None, A.is_equal)
+        lin(CNE, S("CN"), IND(S("NOUT" if lastr else "NE"), S("NO", 0, 8)), 1.0, -3071.0 if lastr else 0.0)
         mm([(S("p1", 0, 64), S("O1"), S("EM"), True, False), (S("p1", 0, 32), S("O256"), S("SL"), False, False),
             (S("p1", 32, 64), S("O256"), S("SL"), False, True)])
-        mm([(S("p2", 0, 64), S("TRI"), S("EM"), True, True)])
+        mm([(S("p2", 0, 64), S("I1"), S("CB", 0, 64), True, False), (S("p2", 0, 64), S("IF"), S("DD", 0, 64), False, False),
+            (S("p2", 0, 64), S("TRN"), S("EM"), False, True)])
+        if not lastr:
+            mm([(S("p5", 0, 64), S("IN1"), S("CB", 0, 64), True, False), (S("p5", 0, 64), S("I1"), S("CB", 64, 128), False, False),
+                (S("p5", 0, 32), S("IN1"), S("VP", 0, 32), False, False), (S("p5", 32, 64), S("ON1"), S("SX"), False, False),
+                (S("p5", 0, 64), S("TRI"), S("EM"), False, True)])
         scan(S("W2"), S("MD", 0, 64), S("p1", 0, 64), 0.0, A.add, A.max)
-        ts(S("OK", 0, 4), S("W2", 15, 64, 16), OFD, 4096.0, A.is_ge, A.mult)
-        ts(S("XF", 0, 8), S("NO", 0, 8), -1.0, 4096.0, A.mult, A.add)
+        ts(S("OK", 0, 4), S("W2", 15, 64, 16), OFD, 8192.0, A.is_ge, A.mult)
+        ts(S("XF", 0, 8), S("NO", 0, 8), -1.0, 8192.0, A.mult, A.add)
         ts(S("XF", 8, 10), do, -0.75, col("CF", 17 + t), A.mult, A.add)
+        act(S("XF", 12, 14), S("XF", 8, 10), AF.Identity, bias=-8176.0, scale=2.0)
+        act(S("XF", 14, 16), S("XF", 8, 10), AF.Identity, bias=-1024.0)
+        tt(S("XF", 10, 12), S("XF", 12, 14), S("XF", 14, 16), A.max)
         for h in range(2):
-            ts(S("XP", h, 10, 2), S("XF", h, 10, 2), col("OK", h), col("OK", 2 + h), A.min, A.min)
-            ts(S("XM", h, 10, 2), S("XP", h, 10, 2), CC2 - 4096.0, col("CM", 256 * h + 255), A.add, A.min)
+            ts(S("XP", h, 12, 2), S("XF", h, 12, 2), col("OK", h), col("OK", 2 + h), A.min, A.min)
+            ts(S("XM", h, 12, 2), S("XP", h, 12, 2), CC2 - 8192.0, col("CM", 256 * h + 255), A.add, A.min)
         tt(S("XN"), S("XM"), S("DUM"), A.max)
         ts(S("SO"), S("XN"), -1.0, CC2, A.mult, A.add)
         tt(S("KP"), S("CN"), S("DD"), A.not_equal)
-        ts(S("FM"), S("p2", 0, 64), 0.0, None, A.max)
-        act(S("OT"), S("p0", 0, 64), AF.Identity, bias=300.0, scale=-1.0)
-        tt(S("M1"), S("FM"), S("DD", 0, 64), A.mult)
+        act(S("LH", 0, 32), S("p0", 0, 32), AF.Identity, bias=512.5 * 512, scale=512.5)
+        act(S("LH", 32, 64), S("p0", 32, 64), AF.Abs, scale=511.5)
         if not lastr:
             act(S("CR"), IND(S("FAR"), S("NO", 0, 8)), AF.Identity)
-            tt(S("M2"), S("FM"), S("OT"), A.mult)
-            tt(S("N1", 0, 64), S("CN", 0, 64), S("M1"), A.add)
-            tt(S("N2", 0, 64), S("CR", 0, 64), S("M2"), A.add)
+            tt(S("N1", 0, 64), S("CN", 0, 64), S("p2", 0, 64), A.min)
+            tt(S("N2", 0, 64), S("CR", 0, 64), S("p5", 0, 64), A.max)
             tt(IND(S("FAR"), S("SO", 4, 8)), S("CR", 64, 128), S("KP", 64, 128), A.mult)
             tt(IND(S("NE"), S("SO", 4, 8)), S("CN", 64, 128), S("KP", 64, 128), A.mult)
             tt(IND(S("FAR"), S("SO", 0, 4)), S("N2", 0, 64), S("KP", 0, 64), A.mult)
             tt(IND(S("NE"), S("SO", 0, 4)), S("N1", 0, 64), S("KP", 0, 64), A.mult)
         else:
-            act(S("NOUT", 0, 512), S("NE", 0, 512), AF.Identity, bias=3071.0)
             tt(S("N1"), S("CN"), S("KP"), A.mult)
-            tt(S("N2", 0, 64), S("N1", 0, 64), S("M1"), A.add)
+            tt(S("N2", 0, 64), S("N1", 0, 64), S("p2", 0, 64), A.min)
             tt(IND(S("NOUT"), S("SO", 4, 8)), S("N1", 64, 128), S("C3"), A.add)
             tt(IND(S("NOUT"), S("SO", 0, 4)), S("N2", 0, 64), S("C3"), A.add)
         act(S("SG"), S("KEY"), AF.Sign, bias=col("AC", 1 if t == 0 else 3 + t))
-        mm([(S("p4", 0, 256), S("I1"), S("OWN", 288 * t, 288 * t + 256), True, False), (S("p4", 0, 256), S("I1"), S("SG"), False, True)])
-        act(S("T2", 0, 256), S("p4", 0, 256), AF.Relu)
-        act(S("T2", 256, 512), S("T2", 0, 256), AF.Relu, bias=63.0, scale=-1.0)
-        act(S("YW", 16 + 5 * t, 3088, 12), IND(S("T2", 256, 512), S("POFF")), AF.Identity, bias=63.0, scale=-1.0)
+        mm([(S("p4", 0, 256), S("I1"), S("LN", 576 * t + 288, 576 * t + 544), True, False), (S("p4", 0, 256), S("I1"), S("SG"), False, True)])
+        act(S("T2", 0, 256), S("p4", 0, 256), AF.Relu, bias=-12.0)
+        act(S("T2", 256, 512), IND(S("T2", 0, 256), S("POFF")), AF.Relu, bias=63.0, scale=-1.0)
+        low = -((5 * t - CUT) // 12)
+        act(S("YW", LOW + 10 * t, CUT + HIGH, 24), S("T2", 256, 256 + low), AF.Identity, bias=63.0, scale=-1.0)
+        act(S("YW", HIGH + 5 * t + 12 * low, NONE + 1, 12), S("T2", 256 + low, 512), AF.Identity, bias=63.0, scale=-1.0)
         ts(S("NO", 8, 10), S("WR", 143, 160, 16), CKA, None, A.add)
         tt(S("YS"), IND(S("YA", 4096, 8192), S("NO", 8, 10)), S("YE"), A.add)
         ts(S("YI"), S("YS"), 0.5, -0.25, A.mult, A.add)
-        cp(IND(S("YW"), S("SO", 8, 10)), S("YI"))
-        tt(S("LH", 0, 32), S("OT", 0, 32), S("OT", 32, 64), A.min)
-        tt(S("LH", 32, 64), S("OT", 0, 32), S("OT", 32, 64), A.max)
-        ts(S("LH", 64, 96), S("LH", 32, 64), -1024.0, 556.0 * 1025, A.mult, A.add)
-        tt(IND(S("ENR"), S("SO", 8, 10)), S("LH", 64, 96), S("LH", 0, 32), A.subtract)
+        cp(IND(S("YW"), S("SO", 10, 12)), S("YI"))
+        tt(IND(S("ENR"), S("SO", 8, 10)), S("LH", 0, 32), S("LH", 32, 64), A.subtract)
         if not lastr:
             ts(S("GO"), S("XN", 8, 10), CC2 - 3087.5, None, A.is_gt)
             mm([(S("p1", 0, 1), S("O1"), col("GO", 0), True, False), (S("p1", 0, 1), S("O1"), col("GO", 1), False, True)])
@@ -559,56 +696,19 @@ def rank_program(g, core, T, topo):
                 cp(col("AC", 3), col("AI", 0))
             ts(col("AI", 2 * t + 1), col("AI", 2 * t), 31, None, A.bitwise_and)
             ts(col("AC", 4 + t), col("AI", 2 * t + 1), -2048.0, col("AC", 1), A.mult, A.add)
-    act(col("YW", 3087), col("SVC", 0), AF.Identity)
-    dma("s", T.y1[:, 0:1536], S("YW", 16, 1552), 3000)
-    dma("s", T.y1[:, 1536:3072], S("YW", 1552, 3088), 3000)
+    act(col("YW", NONE), col("SVC", 0), AF.Identity)
+    cp(S("YL"), S("YW", LOW, CUT + HIGH, 2))
+    dma("s", T.y1[:, CUT:], S("YW", CUT + HIGH, NONE + 1), 4500)
+    dma("s", T.y1[:, 0:CUT], S("YL"), 3200)
     dma("a", T.ne1[:], S("NOUT", 0, 512), 2500)
     dma("s", T.ends1[:], S("ENR", 16, 3088, part=slice(0, 128, 16)), 2500)
 
     n = len(ops)
-    succ = [[] for _ in range(n)]
-    for i, o in enumerate(ops):
-        for j in o["hard"] | o["soft"]:
-            succ[j].append(i)
-    prio = [0.0] * n
-    for i in range(n - 1, -1, -1):
-        prio[i] = ops[i]["cost"] + max([prio[k] + (WAKE if i in ops[k]["hard"] else 0) for k in succ[i]], default=0.0)
-    prio = [p + o["boost"] for p, o in zip(prio, ops)]
-    left = [len(o["hard"] | o["soft"]) for o in ops]
-    ready_at, done_at = [0.0] * n, [0.0] * n
-    free = {e: 0.0 for e in "vapgsx"}
-    pool = {e: [] for e in "vapgsx"}
-    for i in range(n):
-        if left[i] == 0:
-            pool[ops[i]["eng"]].append(i)
-    order = []
-    while len(order) < n:
-        best = None
-        for e in pool:
-            if pool[e]:
-                t0 = max(free[e], min(ready_at[i] for i in pool[e]))
-                if best is None or t0 < best[0]:
-                    best = (t0, e)
-        t0, e = best
-        top = max(pool[e], key=lambda i: (prio[i] - max(0.0, ready_at[i] - t0) * 0, -i))
-        now = [i for i in pool[e] if ready_at[i] <= t0]
-        i = max(now, key=lambda i: (prio[i], -i))
-        if top not in now and t0 + ops[i]["busy"] - ready_at[top] > prio[i] + ops[i]["busy"] - prio[top] + 2 * (ready_at[top] - t0) and prio[top] > prio[i]:
-            fit = [k for k in now if t0 + ops[k]["busy"] <= ready_at[top] + 60]
-            i = max(fit, key=lambda k: (prio[k], -k)) if fit else top
-        t0 = max(t0, ready_at[i])
-        pool[e].remove(i)
-        order.append(i)
-        ops[i]["t0"] = t0
-        ops[i]["seq"] = len(order)
-        free[e] = t0 + ops[i]["busy"]
-        done_at[i] = t0 + ops[i]["cost"]
-        for k in succ[i]:
-            hard = i in ops[k]["hard"]
-            ready_at[k] = max(ready_at[k], done_at[i] + WAKE if hard else (done_at[i] if ops[k]["eng"] == "x" else t0))
-            left[k] -= 1
-            if left[k] == 0:
-                pool[ops[k]["eng"]].append(k)
+    if "start" not in ORDER:
+        ORDER["start"] = arrange(ops)
+    start = ORDER["start"]
+    order = sorted(range(n), key=lambda i: (start[i], i))
+    done_at = [start[i] + ops[i]["cost"] for i in range(n)]
     queue = {"v": g.vector, "a": g.scalar, "p": g.tensor, "g": g, "s": g.sync}
     needed = [False] * n
     for o in ops:

@@ -6,14 +6,21 @@ A = AluOpType
 AF = ActivationFunctionType
 N, RO = 8, 3
 L = 128
-CH = [(0, 64), (64, 128), (128, 256), (256, 384), (384, 448), (448, 512)]
-PRE = [(0, 64), (64, 256), (256, 512)]
-YENG = "vvaavvaaaaaaaaaa"
-PENG = ("aaa", "aaa", "aaa")
+CH = [(0, 64), (64, 128), (128, 192), (192, 256), (256, 384), (384, 448), (448, 512)]
+PRE = [(0, 64), (64, 128), (128, 256), (256, 512)]
+YENG = "vvvvvaaaaaaaaaaa"
+PENG = ("aaa", "aaa", "aaa", "aaa")
+PENG0 = ("aaa", "aaa", "aaa", "aaa")
 CHAINED = False
+SPE = "gggggggggggggggg"
+FIRST = ((0, 128), (128, 256))
+MIX = 64
 CNE = "v"
-CLIP = ((3, 4), (3, 4), (3, 4))
-STAGES = (("P", 3), ("D", 1), ("Y", 1), ("X", 0), ("SCN", 1), ("MFTE", 0), ("RUK", -1))
+SELA = 16
+CLIP = ((4, 5), (4,), (4,))
+STAGES = (("D", 1), ("Y", 1), ("X", 0), ("SCN", 1), ("MFTE", 0), ("RUK", -1))
+JOIN = ("aa", "vv")
+RLAT = 3000.0
 
 
 def round_plan():
@@ -25,27 +32,27 @@ def round_plan():
                 continue
             lo, hi = CH[j]
             for k in kinds:
-                if k == "P":
-                    out += ["%s%d" % (x, PRE.index(p)) for p in PRE if p[0] == lo for x in "POQ"]
-                elif k == "D":
+                if k == "D":
                     out += ["%s%d%d" % (x, j, b) for b in range((hi - lo) // 32) for x in "DA"]
                 elif k == "Y":
                     on, b = YENG[lo // 32:hi // 32], 0
                     while b < len(on):
-                        more = 2 if on[b:b + 2] in ("aa", "vv") else 1
+                        more = 2 if on[b:b + 2] in JOIN else 1
                         out.append("Y%d%d%s%d" % (j, b, on[b], more))
                         b += more
-                elif k not in "NFTE" or lo >= 256:
+                elif k not in "NFTEMRU" or lo >= 256:
                     out.append("%s%d" % (k, j))
     return " ".join(out)
 
 
 PLAN = round_plan()
-GPLAN = "vavavava"
+GPLAN = "vvaavvaavvaavvaa"
+FARE = "vvvv"
 ND = 5
-CEN = 256.0 * 18600
+CEN = 256.0 * 18432
+FOLD = 40.0
 BIGK = 10485760.0
-KEYMAX = 4800000.0
+KEYMAX = 4850000.0
 BD = 8192.0
 LIM = 12000000.0
 SC2 = 1048576.0
@@ -54,42 +61,47 @@ CUT, LOW, HIGH, NONE = 1024, 16, 1040, 4111
 
 F32, BF, I32, U16, F16 = "float32", "bfloat16", "int32", "uint16", "float16"
 SB = {
-    "YW": (4160, BF), "YL": (1024, BF), "W": (3088, BF), "ENR": (3136, F32), "SVC": (8, BF),
+    "YW": (4160, BF), "YL": (1024, BF), "W": (3136, BF), "ENR": (3136, F32), "SVC": (8, BF),
     "EB": (192, I32), "EBF": (192, F32), "EI": (384, I32), "PC": (384, BF),
     "NEI": (512, I32), "NEO": (512, U16), "NE": (640, F32), "FAR": (640, F32), "NOUT": (640, F32),
     "RM": (24, F32), "SEL": (2048, BF), "RST": (16 * L, BF), "TR": (2 * 16 * 544, BF), "O4K": (128, BF), "ON256": (128, BF),
     "LN": (3 * 576, BF), "IN64": (128, BF), "UVO": (3 * 64, U16), "UV": (3 * 512, BF),
-    "KOUT": (3 * 256, F32), "KIN": (3 * 256, F32),
-    "AO": (512, U16), "CO": (512, U16), "SS": (512, BF), "X1": (512, BF), "X2": (512, F16),
+    "RI": (3 * 4096, BF),
+    "AO": (512, U16), "CO": (512, U16), "SS": (512, BF), "X1": (512, F16), "X2": (512, F16), "XA": (1024, F16), "SEP": (1024, BF),
     "AB": (8192, F16), "MN": (8192, F16), "YA": (8192, BF), "MM": (8192, BF), "RR": (4096, BF),
-    "PEN": (256, BF), "F2": (256, BF), "K2": (256, F32), "KEY": (256, F32), "SC": (512, F32),
+    "PEN": (256, BF), "F2": (256, BF), "K2": (256, F32), "SC": (512, F32),
     "SG": (256, BF), "T2": (512, BF),
     "IOT": (144, F32), "C3": (64, F32), "QG": (128, BF), "T16": (128, BF), "LI": (144, F32), "LID": (768, F32),
-    "BBI": (128, BF), "BB": (128, BF), "CX": (512, BF), "JJ": (256, BF), "BE": (144, BF),
-    "I1": (128, BF), "IN1": (128, BF), "IN8": (128, BF), "IBG": (128, BF), "I16": (128, BF),
+    "BBI": (128, BF), "BB": (384, BF), "CX": (512, BF), "JJ": (256, BF), "BE": (144, BF),
+    "I1": (128, BF), "IN1": (128, BF), "IN8": (128, BF), "IBG": (128, BF),
     "O1": (128, BF), "O256": (128, BF), "ONB": (128, BF), "OKW": (128, BF), "TRI": (128, BF),
     "MMN": (128, BF), "MMX": (128, BF), "E1": (128, BF), "E2": (128, BF), "MD": (128, BF),
-    "PI": (8, I32), "CF": (32, F32), "LOFF": (96, U16), "POFF": (16, U16), "DUM": (12, F32), "C256": (4, F32),
-    "THI": (8, I32), "THF": (8, F32), "THB": (8, F32), "THM": (8, F32), "AC": (16, F32), "AI": (8, I32),
-    "Q": (16, I32), "OFF": (10, U16), "KE": (32, F32), "TT": (48, F32), "MV": (2, F32), "EQ": (32, BF), "SL": (32, BF),
+    "PI": (8, I32), "CF": (32, F32), "LOFF": (96, U16), "POFF": (16, U16), "DUM": (12, F32),
+    "THI": (8, I32), "THF": (8, F32), "THB": (8, F32), "AC": (16, F32), "AI": (8, I32),
+    "Q": (16, I32), "OFF": (10, U16), "KE": (32, F32), "TT": (32, F32), "MV": (32, F32), "EQ": (32, BF), "SL": (32, BF),
     "SX": (32, BF), "VP": (96, BF), "PS": (32, BF), "YE": (32, BF), "DD": (128, F32),
-    "WR": (192, F32), "WB": (8, F32), "NO": (10, U16), "AX": (1024, BF), "CM": (1024, BF),
-    "CN": (128, F32), "CR": (128, F32), "EM": (64, BF), "KP": (128, F32), "IF": (128, F32), "CB": (128, BF),
+    "WR": (192, F32), "NO": (10, U16), "AX": (1024, BF), "CM": (1024, BF),
+    "CN": (128, F32), "CR": (128, F32), "EM": (64, BF), "KP": (128, F32), "IF": (128, F32), "CB": (192, BF),
     "TRN": (128, BF), "ON1": (128, BF), "N1": (128, F32), "N2": (128, F32),
     "W2": (64, F32), "OK": (8, F32), "XF": (16, F32), "XP": (12, F32), "XM": (12, F32), "XN": (12, F32), "SO": (12, U16),
-    "YS": (32, F32), "YI": (32, I32), "LH": (96, F32), "GO": (2, BF),
+    "YS": (32, F32), "YI": (32, I32), "LH": (96, F32), "GO": (4, BF),
 }
 SCRATCH = {k: ("sbuf", [128, w], d) for k, (w, d) in SB.items()}
 for _i in range(8):
     SCRATCH["p%d" % _i] = ("psum", [128, 512], F32)
-SEMAPHORES = ["sv", "sa", "sp", "sg", "sent"] + ["d%d" % i for i in range(16)] + ["ln%d" % t for t in range(RO)] \
-    + ["kin%d" % i for i in range(RO * 4)]
+SEMAPHORES = ["sv", "sa", "sp", "sg", "sent"] + ["d%d" % i for i in range(70)] + ["ln%d" % t for t in range(RO)] \
+    + ["in%d" % i for i in range(30)] + ["out%d" % i for i in range(30)]
 
-CYC, PCYC, GATH, SCAT, WAKE = 0.95, 0.475, 1.55, 3.5, 150.0
-PASSES = 600
+CYC, GATH, SCAT = 0.95, 1.55, 3.5
+PCYC = 0.5
+WAKE = 150.0
+PASSES = 150
 JOG = 1500.0
-REACH = 6000.0
-SEED = 0
+REACH = 10000.0
+SEED = 2
+SWAPS = 17000
+FLIP = 0.3
+EASE = 250.0
 ORDER = {}
 
 
@@ -106,7 +118,7 @@ def arrange(ops):
     def place(key, before, after, first):
         at, left = list(first), [len(x) for x in before]
         pool = [(key[i], i) for i in range(n) if not left[i]]
-        taken = {e: [] for e in "vapgsx"}
+        taken = {e: [] for e in "vapgsxd"}
         while pool:
             i = min(pool)
             pool.remove(i)
@@ -140,10 +152,68 @@ def arrange(ops):
         end = float((fw + cost).max())
         if best is None or end <= best[0]:
             best = (end, fw)
-        near = np.abs(best[1] - best[0] * rng.rand()) < REACH
-        key = -best[1] - span - JOG * rng.rand() * rng.rand(n) * near * (rng.rand(n) < 0.3)
+        if p == 0 or end <= now[0] + EASE * (1 - p / PASSES) * rng.rand():
+            now = (end, fw)
+        near = np.abs(now[1] - now[0] * rng.rand()) < REACH * rng.rand()
+        key = -now[1] - span - JOG * rng.rand() * rng.rand(n) * near * (rng.rand(n) < 0.3)
+    eng, cost = [o["eng"] for o in ops], cost.tolist()
+
+    def run(seq):
+        at, by, free, last = [0.0] * n, [None] * n, {}, {}
+        for k in seq:
+            t0, why = free.get(eng[k], 0.0), (last.get(eng[k]), True)
+            for i, lag in pred[k]:
+                if at[i] + lag > t0:
+                    t0, why = at[i] + lag, (i, False)
+            at[k], by[k], free[eng[k]], last[eng[k]] = t0, why, t0 + busy[k], k
+        k = max(seq, key=lambda i: at[i] + cost[i])
+        end, held = at[k] + cost[k], []
+        while k is not None:
+            if by[k][1] and by[k][0] is not None:
+                held.append((by[k][0], k))
+            k = by[k][0]
+        return end, at, held, seq
+
+    def other(i):
+        eng[i], cost[i] = ops[i]["alt"][0::2] if eng[i] == ops[i]["eng"] else (ops[i]["eng"], ops[i]["cost"])
+        busy[i] = cost[i]
+        for k, _lag in succ[i]:
+            pred[k] = [(x, cost[i] + WAKE if x == i else lag) for x, lag in pred[k]]
+
+    now = best = run(sorted(range(n), key=lambda i: (best[1][i], i)))
+    where = list(eng)
+    for p in range(SWAPS):
+        j, k = now[2][rng.randint(len(now[2]))]
+        seq, moved = now[3], None
+        if ops[j]["alt"] and rng.rand() < FLIP:
+            moved = j
+            other(j)
+        else:
+            a, b = seq.index(j), seq.index(k)
+            part = seq[a:b + 1]
+            if rng.rand() < 0.5:
+                lead = {k}
+                for i in part[-2::-1]:
+                    if any(x in lead for x, _lag in succ[i]):
+                        lead.add(i)
+            else:
+                lead = {j}
+                for i in part[1:]:
+                    if any(x in lead for x, _lag in pred[i]):
+                        lead.add(i)
+                lead = set(part) - lead
+            if j in lead or k not in lead:
+                continue
+            seq = seq[:a] + [i for i in part if i in lead] + [i for i in part if i not in lead] + seq[b + 1:]
+        new = run(seq)
+        if new[0] <= now[0] + EASE * (1 - p / SWAPS) * rng.rand():
+            now = new
+            if now[0] < best[0]:
+                best, where = now, list(eng)
+        elif moved is not None:
+            other(moved)
     ORDER["end"] = best[0]
-    return best[1].tolist()
+    return best[1], where
 
 
 def rank_program(g, core, T, topo):
@@ -195,7 +265,7 @@ def rank_program(g, core, T, topo):
             last_w[name] = [(j, mm & ~m) for j, mm in last_w.get(name, []) if mm & ~m] + [(i, m)]
             readers[name] = [(j, mm & ~m) for j, mm in readers.get(name, []) if mm & ~m or j == i]
         ops.append({"eng": eng, "fn": fn, "hard": hard, "soft": soft - hard, "cost": cost, "kind": kind, "tag": wr[0][0] if wr else "", "sem": sem, "val": val,
-                    "busy": cost if busy is None else busy, "boost": boost[0]})
+                    "busy": cost if busy is None else busy, "alt": None})
         if chain[0]:
             if eng in tail and tail[eng] not in hard:
                 ops[i]["soft"].add(tail[eng])
@@ -218,6 +288,9 @@ def rank_program(g, core, T, topo):
         return 30 + max(64, n * f) * CYC
 
     def ts(out, in0, s1, s2, op0, op1=None):
+        if (op0, op1) in ((A.mult, A.add), (A.mult, None)) and not chain[0] and all(v["dt"] in (F32, BF) and not v["ps"] for v in (out, in0)):
+            return lin("v", out, in0, s1, s2 or 0.0)
+
         def fn():
             if op1 is None:
                 return g.vector.tensor_scalar(out["ap"], in0["ap"], val(s1), None, op0)
@@ -242,12 +315,20 @@ def rank_program(g, core, T, topo):
     def tr(out, in0):
         return add("v", lambda: g.vector.transpose(out["ap"], in0["ap"]), [out], [in0], vcost(out, [in0]))
 
+    def acost(in0):
+        return 65 + max(64, in0["n"] * (GATH if in0["ind"] else 1)) * CYC
+
     def act(out, in0, f, bias=0.0, scale=1.0):
-        return add("a", lambda: g.scalar.activation(out["ap"], in0["ap"], f, bias=val(bias), scale=val(scale)), [out], [in0, bias, scale],
-                   65 + max(64, in0["n"] * (GATH if in0["ind"] else 1)) * CYC)
+        if f == AF.Identity and not out["ps"] and not in0["ps"]:
+            return lin("a", out, in0, scale, bias)
+        return add("a", lambda: g.scalar.activation(out["ap"], in0["ap"], f, bias=val(bias), scale=val(scale)), [out], [in0, bias, scale], acost(in0))
 
     def lin(eng, out, in0, scale, bias):
-        return ts(out, in0, scale, bias, A.mult, A.add) if eng == "v" else act(out, in0, AF.Identity, bias=bias, scale=scale)
+        on = {"v": (lambda: g.vector.tensor_scalar(out["ap"], in0["ap"], val(scale), val(bias), A.mult, A.add), vcost(out, [in0])),
+              "a": (lambda: g.scalar.activation(out["ap"], in0["ap"], AF.Identity, bias=val(bias), scale=val(scale)), acost(in0))}
+        i = add(eng, on[eng][0], [out], [in0, scale, bias], on[eng][1])
+        ops[i]["alt"] = ("a",) + on["a"] if eng == "v" else ("v",) + on["v"]
+        return i
 
     def mm(items):
         def fn():
@@ -284,6 +365,12 @@ def rank_program(g, core, T, topo):
             return q.dma_start(val(out), val(in0))
         return add(eng, fn, [out] if isinstance(out, dict) else [], [in0], cost, "dma", sem, 16, 1000 if eng == "g" else 100)
 
+    def both(pairs, on, cost):
+        i, j = [dma(e, out, in0, cost) for e, (out, in0) in zip(on, pairs)]
+        ops[j]["hard"].discard(i)
+        ops[j]["hard"].update(ops[i]["hard"])
+        last_w[ops[j]["tag"]].append((i, last_w[ops[j]["tag"]][-1][1]))
+
     def col(name, c):
         return S(name, c, c + 1)
 
@@ -300,6 +387,7 @@ def rank_program(g, core, T, topo):
     iota(S("CX"), [[1, 512]], -256, 0)
     chain[0] = False
     iota(S("JJ"), [[1, 256]], 0, 0)
+    iota(S("CB", 128, 192), [[0, 64]], 300, 0)
     iota(dict(S("YW", LOW + 1, CUT + HIGH, 2), acc=S("YW", LOW, CUT + HIGH)["acc"]), [[0, CUT]], 0, 0)
     RF, GF = col("CF", 0), col("CF", 1)
     R15, R192, R16, G16, R1, R1W, INI, INX, NBC, KB, COF, CBI, CKA, CYO, OFD = [col("CF", c) for c in range(2, 17)]
@@ -315,12 +403,13 @@ def rank_program(g, core, T, topo):
     ts(S("RM", 0, 16), S("T16", 0, 16), RF, None, A.is_equal)
     ts(col("CF", 20), RF, 15.0, 2304.0, A.is_equal, A.mult)
     ts(R192, RF, 192.0, None, A.mult)
-    ms(S("W", 768, 3088), 0.0)
+    ms(S("W", 768, 3136), 0.0)
     ts(S("EI", 0, 192), S("EB"), 10, None, A.logical_shift_right)
     ts(S("EI", 192, 384), S("EB"), 1023, None, A.bitwise_and)
     ts(S("PC", 0, 191), S("EI", 0, 191), -256.0, None, A.add)
     ts(col("PC", 191), col("EI", 191), -256.0, col("CF", 20), A.add, A.add)
     ts(S("PC", 192, 384), S("EI", 192, 384), -256.0, None, A.add)
+    chain[0] = False
     ts(S("LOFF", 0, 48), S("LI", 0, 48), R192, None, A.add)
     ts(S("LI", 48, 96), S("LOFF", 0, 48), 2.0, -16.0, A.mult, A.add)
     ts(S("LI", 96, 144), S("LOFF", 0, 48), 1024.0, None, A.add)
@@ -338,30 +427,31 @@ def rank_program(g, core, T, topo):
     ms(S("FAR", 512, 640), 0.0)
     chain[0] = False
     boost[0] = 1e6
-    for m in range(16):
-        boost[0] = 1e6 if m < 12 else 0.4e6
-        act(S("SEL", 128 * m, 128 * m + 128), S("O1"), AF.Identity, scale=col("RM", m))
+    for m in range(16 if MIX else 2):
+        lin("a" if m < SELA else "v", S("SEL", 128 * m, 128 * m + 128), S("O1"), col("RM", m), 0.0)
     boost[0] = 0.0
+    tt(S("RM", 16, 24), S("RM", 0, 16, 2), S("RM", 1, 16, 2), A.add)
+    for m in range(8):
+        lin("v" if MIX else "a", S("SEP", 128 * m, 128 * m + 128), S("O1"), col("RM", 16 + m), 0.0)
     ts(R15, RF, 15.0, None, A.is_equal)
     ts(R16, RF, 16.0, None, A.mult)
     ts(R1, RF, 1.0, None, A.add)
     ts(R1W, R15, -16.0, R1, A.mult, A.add)
     ts(INI, R15, BIGK, KEYMAX - BIGK, A.mult, A.add)
     ts(INX, R15, -BIGK, BIGK - KEYMAX, A.mult, A.add)
-    ts(KB, RF, 512.0, None, A.mult)
+    ts(KB, RF, 0.5, 0.25, A.mult, A.add)
     ts(COF, R15, BD, 1280.0 - BD, A.mult, A.add)
-    ts(CBI, R15, -BD * SC2, (BD + 0.125) * SC2, A.mult, A.add)
     ts(CKA, R15, BD, -BD, A.mult, A.add)
+    ts(S("BB", 256, 384), S("T16"), 0.0, CKA, A.mult, A.subtract)
     for t in range(RO):
-        ts(col("CF", 17 + t), RF, -191.25, 8176.0 - 5 * t, A.mult, A.add)
+        ts(col("CF", 17 + t), RF, -191.25 / SC2, (8176.0 - 5 * t) / SC2, A.mult, A.add)
     ts(OFD, R15, -BD, BD + 256.5, A.mult, A.add)
     ts(S("POFF"), S("IOT", 0, 16), R16, None, A.add)
     ts(S("XM", 0, 8), S("IOT", 0, 128, 16), RF, 512.0, A.add, A.add)
     ts(S("XM", 8, 10), S("IOT", 0, 32, 16), RF, 3088.0, A.add, A.add)
     ts(S("XM", 10, 12), S("IOT", 0, 32, 16), RF, NONE + 1.0, A.add, A.add)
-    ts(S("DUM"), S("XM"), -1.0, CC2, A.mult, A.add)
-    ms(S("C256"), 1.0 / 256)
-    ms(dict(S("TR", 0, 2 * 16 * 544, 16), acc=S("TR")["acc"]), 255.0)
+    ts(S("DUM"), S("XM"), -1.0 / SC2, CC2 / SC2, A.mult, A.add)
+    ms(S("CF", 24, 28), 1.0 / 256)
     for nm, c in (("O256", 256.0), ("ONB", -1024.0), ("OKW", RF), ("O4K", 4096.0), ("ON256", -256.0), ("ON1", -1.0)):
         ts(S(nm), S("QG"), GF, c, A.is_equal, A.mult)
     chain[0] = True
@@ -378,32 +468,25 @@ def rank_program(g, core, T, topo):
 
     tt(S("MD"), S("E1"), S("E2"), A.add)
     boost[0] = 2e6
-    dma("s", S("W", 16, 3088, part=slice(0, 128, 16)), S("PC", 0, 192), 2200)
-    j = dma("a", S("W", 16, 3088, part=slice(1, 128, 16)), S("PC", 192, 384), 2200)
-    ops[j]["hard"].discard(j - 1)
-    ops[j]["hard"].update(ops[j - 1]["hard"])
-    last_w["W"].append((j - 1, last_w["W"][-1][1]))
+    both([(S("W", 16, 3088, part=slice(s, 128, 16)), S("PC", 192 * s, 192 * s + 192)) for s in range(2)], "sa", 2200)
     for t in range(RO):
         act(S("LN", 576 * t + 288, 576 * t + 544), IND(S("YW"), S("LOFF", 48 + 16 * t, 64 + 16 * t)), AF.Identity, bias=12.0)
-        for s in range(2):
-            act(S("LN", 576 * t + 544 + 16 * s, 576 * t + 560 + 16 * s), S("PC", 192 * s + 5 * t, 192 * s + 192, 12), AF.Identity)
-    boost[0] = 0.0
-    for t in range(RO):
+        act(S("LN", 576 * t + 544, 576 * t + 576), S("PC", 5 * t, 384, 12), AF.Identity)
         ts(S("UVO", 64 * t + 32, 64 * t + 64), S("LN", 576 * t + 544, 576 * t + 576), 256.0, None, A.add)
     cp(col("SVC", 0), col("YW", NONE))
     ms(col("YW", NONE), 255.0)
     boost[0] = 0.5e6
     for c in range(8):
-        o, src = S("MM", 1024 * c, 1024 * c + 1024), IND(S("W"), S("NEO", 64 * c, 64 * c + 64))
-        if GPLAN[c] == "v":
-            cp(o, src)
-        else:
-            act(o, src, AF.Identity)
+        on = GPLAN[2 * c:2 * c + 2]
+        for e, a, b in [(on[0], 64 * c, 64 * c + 64)] if on[0] == on[1] else [(on[0], 64 * c, 64 * c + 32), (on[1], 64 * c + 32, 64 * c + 64)]:
+            lin(e, S("MM", 16 * a, 16 * b), IND(S("W"), S("NEO", a, b)), 1.0, 0.0)
         pb = S("p%d" % (c // 2), 64 * (c % 2), 64 * (c % 2) + 64)
-        mm([(pb, S("IN8"), S("CX", 64 * c, 64 * c + 64), True, False)]
+        mm([(pb, S("IN8"), S("CX", 64 * c, 64 * c + 64), True, False), (pb, S("IN8"), S("CB", 128, 192), False, False)]
            + [(pb, S("BE", 15 - k, 143 - k), S("MM", 1024 * c + k, 1024 * c + 1024, 16), False, k == 15) for k in range(16)])
-        if c % 2:
-            act(S("FAR", 64 * c - 64, 64 * c + 64), S("p%d" % (c // 2), 0, 128), AF.Relu, bias=300.0, scale=-1.0 / 8192)
+        if c % 2 and FARE[c // 2] == "a":
+            act(S("FAR", 64 * c - 64, 64 * c + 64), S("p%d" % (c // 2), 0, 128), AF.Relu, scale=-1.0 / 8192)
+        elif c % 2:
+            ts(S("FAR", 64 * c - 64, 64 * c + 64), S("p%d" % (c // 2), 0, 128), -1.0 / 8192, 0.0, A.mult, A.max)
     boost[0] = 0.0
     peers = [T.cores[(rank + 1 + t) % N] for t in range(RO)]
     backs = [T.cores[(rank - 1 - t) % N] for t in range(RO)]
@@ -420,8 +503,10 @@ def rank_program(g, core, T, topo):
             at += k
         sent[0] += at
         return g.remote_dma_fused(trs, local_sem=T.sem.sent)
-    js = add("g", send_lanes, [], [S("LN", 576 * t + 288, 576 * t + 576) for t in range(RO)], 3500, "rem", busy=1500)
-    iota(S("RST"), [[0, L], [-16384, 16]], 16384, 0)
+    js = add("g", send_lanes, [], [S("LN", 576 * t + 288, 576 * t + 576) for t in range(RO)], 5500, "rem", busy=3200)
+    iota(S("RST", 0, 4 * L), [[0, L // 4], [-16384, 16]], 16384, 0)
+    for x in range(1, 4):
+        dma("s", S("RST", 4 * L * x, 4 * L * x + 4 * L), S("RST", 0, 4 * L), 2500)
     dma("g", S("THI", part=slice(0, 1)), T.th[:], 2500, True)
     dma("g", S("ENR", 16, 3088), T.y0[:], 9000)
     iota(S("BBI"), [[0, 4], [1, 2], [2, 16]], 0, 0)
@@ -431,22 +516,20 @@ def rank_program(g, core, T, topo):
             c = min(16, max(0, -((192 * r + 5 * t - CUT) // 12)))
             if c:
                 iota(S("LID", 256 * t + r, 256 * t + 16 * c, 16), [[24, c]], 2 * (192 * r + 5 * t) + LOW - NONE, 0)
-    for nm, c in (("IBG", 16777216.0), ("I16", 16.0)):
-        pick(S(nm), S("I1"), A.not_equal, c)
-    for nm, c in (("TRI", 16384.0), ("TRN", -16384.0)):
-        ts(S("AX", 0, 128), S("QG"), GF, -2 * c, A.is_equal, A.mult)
-        pick(S("AX", 128, 256), S("AX", 0, 128), A.is_gt, 0.0)
-        pick(S(nm), S("AX", 128, 256), A.not_equal, c)
-    iota(S("IF"), [[0, 128]], 0, 0)
-    pick(S("IF"), S("IF"), A.not_equal, 1.0)
-    iota(S("CB"), [[-16084, 2], [0, 64]], 16384, 0)
+    pick(S("IBG"), S("I1"), A.not_equal, 16777216.0)
+    ts(S("AX", 0, 128), S("QG"), GF, -CEN / 32, A.is_equal, A.mult)
+    pick(S("AX", 128, 256), S("AX", 0, 128), A.is_gt, 0.0)
+    pick(S("TRI"), S("AX", 128, 256), A.not_equal, CEN / 64)
+    ts(S("TRN"), S("TRI"), -1.0, None, A.mult)
+    spread(S("IF"), S("I1"))
+    iota(S("CB", 0, 128), [[0, 128]], int(CEN) // 64, 0)
     iota(S("C3"), [[0, 64]], 3071, 0)
     iota(S("ENR", 0, 16), [[0, 16]], 0, 0)
     iota(S("ENR", 3088, 3136), [[0, 48]], 0, 0)
-    iota(S("TT"), [[0, 48]], int(LIM), 0)
     iota(S("NOUT", 512, 640), [[0, 128]], 0, 0)
     chain[0] = False
-    act(S("BB"), S("BBI"), AF.Identity, scale=1.0 / 128)
+    ts(S("BB", 0, 128), S("BBI"), 1.0 / 128, None, A.mult)
+    ts(S("BB", 128, 256), S("BBI"), 1.0 / 128, 0.125, A.mult, A.add)
     for t in range(RO):
         ne_t = len(topo.engines(backs[t], core))
         j = add("x", None, [S("LN", 576 * t, 576 * t + 288)], [], 0, "arr", "ln%d" % t, ne_t // 2 if t == 0 else ne_t // 4)
@@ -459,36 +542,56 @@ def rank_program(g, core, T, topo):
     own_ends(0, "p6")
     cp(S("THF", part=slice(0, 1)), S("THI", part=slice(0, 1)))
     add("g", lambda: g.partition_broadcast(T.THB[:, :], T.THF[0:1, :], 128), [S("THB")], [S("THF")], 200)
-    ts(S("THM"), S("IOT", 0, 8), GF, None, A.is_equal)
-    tt(S("THF"), S("THM"), S("THB"), A.mult)
+    ts(S("AC", 8, 16), S("IOT", 0, 8), GF, None, A.is_equal)
+    tt(S("THF"), S("AC", 8, 16), S("THB"), A.mult)
     red(col("AC", 0), S("THF"), A.add)
     ts(col("AC", 1), col("AC", 0), -256.0, CEN + 0.5, A.mult, A.add)
-    ms(col("AC", 2), 0.0)
     cp(S("EBF"), S("EB"))
     dma("s", S("ENR", 16, 3088, part=slice(0, 128, 16)), S("EBF"), 2500)
-    ring = {"d": 0, "z": 0, "r": 0}
+    ring = {"d": 0, "w": 0}
+
+    def write(to, frm, pairs, cost):
+        k = ring["w"]
+        ring["w"] += 1
+        rid, pid, _s = topo.addr(to)
+        en = topo.engines(core, to)
+        cuts = [0, len(en)] if len(pairs) == 1 else [0, len(en) // 2, 3 * len(en) // 4, len(en)]
+
+        def send():
+            return g.remote_dma_fused([RemoteDMATransfer(dst_ids=[DstId(rid=rid, pnc=pid)], dma_engine_mask=sum(1 << e for e in en[a:b]), remote_sem=T.sem["in%d" % k],
+                                                         srcs=[x["ap"] for x in srcs], dsts=[land["ap"]], alu_op=3 if len(srcs) > 1 else 0)
+                                       for (land, srcs), a, b in zip(pairs, cuts, cuts[1:])], local_sem=T.sem["out%d" % k])
+        jj = add("g", send, [], [x for _l, srcs in pairs for x in srcs], RLAT + cost, "rem", "out%d" % k, len(en), busy=1200)
+        jd = add("d", None, [], [], RLAT - 1200 + cost, "way", busy=cost)
+        ja = add("x", None, [land for land, _x in pairs], [], 0, "arr", "in%d" % k, len(topo.engines(frm, core)))
+        ops[jd]["soft"].add(jj)
+        ops[ja]["soft"].add(jd)
 
     for t in range(RO):
         lastr = t == RO - 1
         dbank = {}
         trb = 16 * 544 * (t % 2)
-        runs = []
+        runs = [[0, 256]] if t else [list(x) for x in FIRST]
         for j, (lo, hi) in enumerate(CH):
-            if j not in CLIP[t]:
-                gap = 32 * (lo >= 256)
-                if runs and (runs[-1][1] == lo + gap or (t and runs[-1][1] == lo)):
-                    runs[-1][1] = hi + gap
+            if j not in CLIP[t] and lo >= 256:
+                if runs[-1][1] == lo + 32:
+                    runs[-1][1] = hi + 32
                 else:
-                    runs.append([lo + gap, hi + gap])
+                    runs.append([lo + 32, hi + 32])
         for a, b in runs:
-            for k in range(1, 16):
-                spread(S("TR", trb + 16 * a + k, trb + 16 * b, 16), S("LN", 576 * t + a, 576 * t + b))
+            for k in range(16):
+                o, src = S("TR", trb + 16 * a + k, trb + 16 * b, 16), S("LN", 576 * t + a, 576 * t + b)
+                on = SPE[k] if a > 256 and t else "g"
+                if on == "g":
+                    spread(o, src)
+                else:
+                    lin(on, o, src, 1.0, 0.0)
 
         def pre(kind, lo, hi):
             side, a, b = lo // 256, (lo % 256) // 16, (hi - 1) % 256 // 16 + 1
             uo = S("UVO", 64 * t + 32 * side + a, 64 * t + 32 * side + b)
             vo = S("UVO", 64 * t + 32 * side + 16 + a, 64 * t + 32 * side + 16 + b)
-            on = PENG[PRE.index((lo, hi))]
+            on = (PENG if t else PENG0)[PRE.index((lo, hi))]
             if kind == "P":
                 lin(on[0], S("SS", lo, hi), IND(S("FAR"), uo), -1.0, 300.0)
                 lin(on[1], S("X1", lo, hi), IND(S("FAR"), vo), -64.0, 300.0 * 64)
@@ -499,38 +602,24 @@ def rank_program(g, core, T, topo):
 
         def after_sum(j, lo, hi, kb):
             if lo < 256:
-                ko = S("KOUT", 256 * t + lo, 256 * t + hi)
-                act(ko, kb, AF.Identity, bias=-CEN)
-                sem = "kin%d" % (4 * t + j)
-                rid, pid, _s = topo.addr(backs[t])
-                msk, cnt = topo.mask(core, backs[t]), len(topo.engines(core, backs[t]))
-                dst = T.KIN[:, 256 * t + lo:256 * t + hi]
-
-                def send():
-                    sent[0] += cnt
-                    return g.remote_dma(dst, ko["ap"], T.sem[sem], T.sem.sent, pid, rid, msk)
-                jj = add("g", send, [], [ko], 3000, "rem", busy=1200)
-                ja = add("x", None, [S("KIN", 256 * t + lo, 256 * t + hi)], [], 0, "arr", sem, len(topo.engines(peers[t], core)))
-                ops[ja]["soft"].add(jj)
-                return
+                a, b = 4096 * t + 16 * lo, 4096 * t + 16 * hi
+                return write(backs[t], peers[t], [(S("RI", a, b), [S("TR", trb + 16 * lo, trb + 16 * hi), S("MM", 16 * lo, 16 * hi)])], FOLD * (hi - lo))
             a, b = lo - 256, hi - 256
-            tt(S("KEY", a, b), kb, S("KIN", 256 * t + a, 256 * t + b), A.add)
-            scan(S("SC", a, b), S("MMN", 0, b - a), S("KEY", a, b), col("SC", a - 1) if a % 128 else INI, A.add, A.min)
-            scan(S("SC", 256 + a, 256 + b), S("MMX", 0, b - a), S("KEY", a, b), col("SC", 255 + a) if a % 128 else INX, A.add, A.max)
+            scan(S("SC", a, b), S("MMN", 0, b - a), kb, col("SC", a - 1) if a % 128 else INI, A.add, A.min)
+            scan(S("SC", 256 + a, 256 + b), S("MMX", 0, b - a), kb, col("SC", 255 + a) if a % 128 else INX, A.add, A.max)
+            act(S("SG", a, b), kb, AF.Sign, bias=col("AC", 1 if t == 0 else 3 + t))
             if b % 128 == 0:
                 chain[0] = False
                 h = a // 128
                 ce, cd = col("SC", b - 1), col("SC", 255 + b)
-                ts(col("Q", h), col("C256", 0), ce, -0.25 - 0.5 * h, A.mult, A.add)
-                ts(S("Q", 4 + 4 * h, 8 + 4 * h), S("C256"), cd, -0.25 - 0.5 * h, A.mult, A.add)
+                ts(col("Q", h), col("CF", 24), ce, -0.25 - 0.5 * h, A.mult, A.add)
+                ts(S("Q", 4 + 4 * h, 8 + 4 * h), S("CF", 24, 28), cd, -0.25 - 0.5 * h, A.mult, A.add)
                 ts(col("OFF", h), col("Q", h), -256.0, ce, A.mult, A.add)
                 ts(S("OFF", 2 + h, 10, 2), S("Q", 4 + 4 * h, 8 + 4 * h), -256.0, cd, A.mult, A.add)
                 chain[0] = CHAINED
 
         def step(tok):
             kind, j = tok[0], int(tok[1])
-            if kind in "PQO":
-                return pre(kind, *PRE[j])
             lo, hi = CH[j]
             w = hi - lo
             nm, nb, ab = 512 // w, w // 32, 16 * (lo % 256)
@@ -538,39 +627,42 @@ def rank_program(g, core, T, topo):
             at = lo if lo < 256 else lo + 32
             top = S("LN", 576 * t + at, 576 * t + at + w)
             kb = S("p%d" % (5 + j % 2), 0, w)
+            if kind == "U":
+                ri = 4096 * t + 16 * (lo - 256)
+                mm([(kb, S("I1"), S("JJ", lo - 256, hi - 256), True, False)] + [(kb, S("O4K"), top, False, False)] * (1 if j in CLIP[t] else 2) + [
+                    (kb, S("IN64"), S("CB", 0, w), False, False)] + [(kb, S("ON256"), S("RI", ri + k, ri + 16 * w, 16), False, False) for k in range(16)])
+            least = S("MN", 16 * lo + 15, 16 * hi, 16)
             if kind == "D":
                 pb = dbank[j, bk] = "p%d" % (ring["d"] % ND)
                 ring["d"] += 1
                 it = []
                 for x in range(nm):
                     m, o = nm * bk + x, S(pb, x, 512, nm)
-                    it += [(o, S("IN64"), S("SS", lo, hi), True, False), (o, S("SEL", 128 * m, 128 * m + 128), S("X1", lo, hi), False, False),
-                           (o, S("SEL", 128 * m, 128 * m + 128), S("X2", lo, hi), False, True)]
+                    it.append((o, S("IN64"), S("SS", lo, hi), True, False))
+                    if lo < MIX:
+                        it += [(o, S("SEL", 128 * m, 128 * m + 128), S(nm_, lo, hi), False, nm_ == "X2") for nm_ in ("X1", "X2")]
+                    else:
+                        it.append((o, S("SEP", 128 * (m // 2), 128 * (m // 2) + 128), S("XA", 512 * (m % 2) + lo, 512 * (m % 2) + hi), False, True))
                 mm(it)
             elif kind == "A":
                 act(S("AB", 16 * lo + bk, 16 * hi, nb), S(dbank[j, bk]), AF.Abs)
             elif kind == "S":
-                for a in range(lo, hi, L):
-                    b = min(hi, a + L)
-                    scan(S("MN", 16 * a, 16 * b), S("RST", 0, 16 * (b - a)), S("AB", 16 * a, 16 * b), 0.0, A.max, A.min)
+                scan(S("MN", 16 * lo, 16 * hi), S("RST", 0, 16 * w), S("AB", 16 * lo, 16 * hi), 0.0, A.max, A.min)
             elif kind == "C":
-                ts(S("CO", lo, hi), S("MN", 16 * lo + 15, 16 * hi, 16), -256.0, NONE + 1.0, A.mult, A.add)
+                ts(S("CO", lo, hi), least, -256.0, NONE + 1.0, A.mult, A.add)
             elif kind == "N":
-                act(S("PEN", lo - 256, hi - 256), S("MN", 16 * lo + 15, 16 * hi, 16), AF.Relu, bias=33554432.0, scale=-1048576.0)
+                act(S("PEN", lo - 256, hi - 256), least, AF.Relu, bias=33554432.0, scale=-1048576.0)
             elif kind == "F":
                 tt(S("F2", lo - 256, hi - 256), S("SS", lo, hi), S("UV", 512 * t + lo, 512 * t + hi), A.is_equal)
             elif kind == "K":
                 after_sum(j, lo, hi, kb)
             elif kind == "E":
-                act(S("K2", lo - 256, hi - 256), S("p7", lo - 256, hi - 256), AF.Identity, KB)
+                act(S("K2", lo - 256, hi - 256), S("p7", lo - 256, hi - 256), AF.Identity, KB, 1.0 / 1024)
             elif kind == "Y":
                 a = lo + 32 * bk
                 b = a + 32 * int(tok[4])
                 o, src = S("YA", 16 * a, 16 * b), IND(S("YW"), S("AO", a, b))
-                if tok[3] == "v":
-                    cp(o, src)
-                else:
-                    act(o, src, AF.Identity)
+                lin(tok[3], o, src, 1.0, 0.0)
             elif kind == "X":
                 tt(S("MM", 16 * lo, 16 * hi), IND(S("YW"), S("CO", lo, hi)), S("YA", 16 * lo, 16 * hi), A.max)
             elif kind in "MRU" and j in CLIP[t]:
@@ -583,84 +675,90 @@ def rank_program(g, core, T, topo):
                                                             (S(pb, w * x, w * x + w), S("IN1"), S("MM", 16 * lo + nm * b + x, 16 * hi, 16), False, True))])
                         act(S("RR", r0, r0 + 512), S(pb), AF.Relu)
                     else:
-                        mm([(kb, S("O256"), S("RR", r0 + w * x, r0 + w * x + w), b == 0 and x == 0, lo >= 256 and b == nb - 1 and x == nm - 1) for x in range(nm)]
-                           + ([(kb, S("I1"), S("JJ", lo, hi), False, True)] if lo < 256 and b == nb - 1 else []))
+                        mm([(kb, S("O256"), S("RR", r0 + w * x, r0 + w * x + w), False, b == nb - 1 and x == nm - 1) for x in range(nm)])
             elif kind == "M":
                 tt(S("MM", 16 * lo, 16 * hi, 16), S("MM", 16 * lo, 16 * hi, 16), top, A.min)
             elif kind == "R":
                 scan(S("RR", ab, ab + 16 * w), S("TR", trb + 16 * at, trb + 16 * (at + w)), S("MM", 16 * lo, 16 * hi), 0.0, A.max, A.min)
             elif kind == "U":
-                mm([(kb, S("O4K"), top, True, False)] + ([(kb, S("I1"), S("JJ", lo, hi), False, False)] if lo < 256 else [])
-                   + [(kb, S("ON256"), S("RR", ab + k, ab + 16 * w, 16), False, k == 15) for k in range(16)])
+                mm([(kb, S("ON256"), S("RR", ab + k, ab + 16 * w, 16), False, k == 15) for k in range(16)])
             elif kind == "T":
                 a, b = lo - 256, hi - 256
                 pb = S("p7", a, b)
                 mm([(pb, S("BE", 15 - k, 143 - k), S("YA", 16 * lo + k, 16 * hi, 16), k == 0, False) for k in range(16)]
                    + [(pb, S("IBG"), S("F2", a, b), False, False), (pb, S("I1"), S("PEN", a, b), False, True)])
 
-        if lastr:
-            act(S("p7"), S("NE", 0, 512), AF.Identity, bias=2047.5, scale=0.5)
-            act(S("NOUT", 0, 512), S("NE", 0, 512), AF.Identity, bias=3071.0)
-            tt(S("NOUT", 0, 512), S("NOUT", 0, 512), S("p7"), A.max)
-        chain[0] = CHAINED
+        for lo, hi in PRE:
+            for kind in "PQO":
+                pre(kind, lo, hi)
+            for odd in range(2 if lo >= MIX else 0):
+                both([(S("XA", 512 * odd + lo, 512 * odd + hi, part=slice(x, 128, 2)), S(nm_, lo, hi, part=slice(odd, 128, 2)))
+                      for x, nm_ in enumerate(("X1", "X2"))], "ss", 2600)
         for tok in PLAN.split():
             step(tok)
-        chain[0] = False
+        if lastr:
+            act(S("p0"), S("NE", 0, 512), AF.Identity, bias=2047.5, scale=0.5)
+            act(S("NOUT", 0, 512), S("NE", 0, 512), AF.Identity, bias=3071.0)
+            tt(S("NOUT", 0, 512), S("NOUT", 0, 512), S("p0"), A.max)
+            dma("s", S("W", 16 + CUT, 3088), S("YW", CUT + HIGH, NONE + 1), 4000)
+            cp(S("W", 16, 16 + CUT), S("YW", LOW, CUT + HIGH, 2))
+            act(col("W", 3087), col("SVC", 0), AF.Identity)
         if not lastr:
             own_ends(t + 1, "p0")
         eo, do = S("OFF", 0, 2), S("OFF", 2, 4)
         uw, vw = S("UV", 512 * t, 512 * t + 256), S("UV", 512 * t + 256, 512 * t + 512)
-        cp(S("KE"), IND(S("K2"), eo))
-        tr(S("TT", 8, 40), S("KE"))
-        red(col("MV", 0), S("TT", 7, 24), A.min)
-        red(col("MV", 1), S("TT", 24, 41), A.min)
+        lin("v", S("KE"), IND(S("K2"), eo), 1.0, 0.0)
+        tr(S("TT"), S("KE"))
+        scan(S("MV"), S("RST", 0, 32), S("TT"), 0.0, A.max, A.min)
         for x in range(2):
-            ts(S("EQ", 16 * x, 16 * x + 16), S("TT", 8 + 16 * x, 24 + 16 * x), col("MV", x), None, A.is_equal)
+            ts(S("EQ", 16 * x, 16 * x + 16), S("TT", 16 * x, 16 * x + 16), col("MV", 16 * x + 15), None, A.is_equal)
         tr(S("SL"), S("EQ"))
         act(S("VP", 0, 32), IND(vw, eo), AF.Identity)
         act(S("VP", 32, 64), IND(uw, do), AF.Identity)
         act(S("VP", 64, 96), IND(vw, do), AF.Identity)
-        act(S("PS"), IND(S("JJ"), eo), AF.Identity)
+        act(S("PS"), IND(S("JJ"), eo), AF.Identity, scale=16.0)
         act(S("YE"), IND(S("LN", 576 * t + 288, 576 * t + 544), eo), AF.Identity, bias=-12.0)
         tt(S("SX"), IND(S("SS", 256, 512), eo), S("SL"), A.mult)
         act(S("DD"), IND(S("LID", 256 * t, 256 * t + 256), S("OFF", 2, 10)), AF.Identity)
-        mm([(S("p7", 0, 128), S("I1"), S("BB"), True, False), (S("p7", 32, 128), S("I1"), S("VP"), False, False)])
-        mm([(S("p7", 32 * x, 32 * x + 32), S("ONB"), S("SL"), False, False) for x in range(4)]
-           + [(S("p7", 0, 32), S("O1"), S("SX"), False, True)])
-        mm([(S("p3", 0, 32), S("I16"), S("PS"), True, False), (S("p3", 0, 32), S("OKW"), S("SL"), False, True)])
+        mm([(S("p7", 0, 128), S("I1"), S("BB", 0, 128), True, False), (S("p7", 32, 128), S("I1"), S("VP"), False, False)])
+        mm([(S("p1", 0, 128), S("I1"), S("BB", 128, 256), True, False), (S("p1", 0, 128), S("I1"), S("BB", 256, 384), False, False),
+            (S("p1", 32, 128), S("I1"), S("VP"), False, False)])
+        for pb in ("p7", "p1"):
+            mm([(S(pb, 32 * x, 32 * x + 32), S("ONB"), S("SL"), False, False) for x in range(4)] + [(S(pb, 0, 32), S("O1"), S("SX"), False, True)])
+        mm([(S("p3", 0, 32), S("I1"), S("PS"), True, False), (S("p3", 0, 32), S("OKW"), S("SL"), False, True)])
         scan(S("WR", 0, 128), S("MD", 0, 128), S("p7", 0, 128), 0.0, A.add, A.max)
         scan(S("WR", 128, 160), S("MD", 0, 32), S("p3", 0, 32), 0.0, A.add, A.max)
-        act(S("WB"), S("WR", 15, 128, 16), AF.Identity, bias=CBI, scale=-SC2)
         ts(S("NO", 0, 8), S("WR", 15, 128, 16), COF, 511.0, A.add, A.min)
         for h in range(2):
             for x in range(4):
-                act(S("AX", 512 * h + 128 * x, 512 * h + 128 * x + 128), S("p7", 0, 128), AF.Abs, bias=col("WB", 2 * x + h), scale=SC2)
-            scan(S("CM", 256 * h, 256 * h + 256), S("AX", 512 * h, 512 * h + 256), S("AX", 512 * h + 256, 512 * h + 512), SC2, A.min, A.min)
+                act(S("AX", 512 * h + 128 * x, 512 * h + 128 * x + 128), S("p1", 0, 128), AF.Abs, bias=col("WR", 32 * x + 16 * h + 15), scale=-1.0)
+            scan(S("CM", 256 * h, 256 * h + 256), S("AX", 512 * h, 512 * h + 256), S("AX", 512 * h + 256, 512 * h + 512), 1.0, A.min, A.min)
         mm([(S("p0", 0, 32), S("I1"), S("VP", 0, 32), True, False), (S("p0", 0, 32), S("O1"), S("SX"), False, True),
             (S("p0", 32, 64), S("IN1"), S("VP", 0, 32), True, False), (S("p0", 32, 64), S("O1"), S("SX"), False, True)])
         ts(S("EM"), IND(S("NE"), S("NO", 0, 4)), 0.0, None, A.is_equal)
         lin(CNE, S("CN"), IND(S("NOUT" if lastr else "NE"), S("NO", 0, 8)), 1.0, -3071.0 if lastr else 0.0)
-        mm([(S("p1", 0, 64), S("O1"), S("EM"), True, False), (S("p1", 0, 32), S("O256"), S("SL"), False, False),
-            (S("p1", 32, 64), S("O256"), S("SL"), False, True)])
+        mm([(S("p7", 0, 64), S("O1"), S("EM"), True, False), (S("p7", 0, 32), S("O256"), S("SL"), False, False),
+            (S("p7", 32, 64), S("O256"), S("SL"), False, True)])
         mm([(S("p2", 0, 64), S("I1"), S("CB", 0, 64), True, False), (S("p2", 0, 64), S("IF"), S("DD", 0, 64), False, False),
             (S("p2", 0, 64), S("TRN"), S("EM"), False, True)])
         if not lastr:
-            mm([(S("p5", 0, 64), S("IN1"), S("CB", 0, 64), True, False), (S("p5", 0, 64), S("I1"), S("CB", 64, 128), False, False),
+            mm([(S("p5", 0, 64), S("IN1"), S("CB", 0, 64), True, False), (S("p5", 0, 64), S("I1"), S("CB", 128, 192), False, False),
                 (S("p5", 0, 32), S("IN1"), S("VP", 0, 32), False, False), (S("p5", 32, 64), S("ON1"), S("SX"), False, False),
                 (S("p5", 0, 64), S("TRI"), S("EM"), False, True)])
-        scan(S("W2"), S("MD", 0, 64), S("p1", 0, 64), 0.0, A.add, A.max)
-        ts(S("OK", 0, 4), S("W2", 15, 64, 16), OFD, 8192.0, A.is_ge, A.mult)
-        ts(S("XF", 0, 8), S("NO", 0, 8), -1.0, 8192.0, A.mult, A.add)
-        ts(S("XF", 8, 10), do, -0.75, col("CF", 17 + t), A.mult, A.add)
-        act(S("XF", 12, 14), S("XF", 8, 10), AF.Identity, bias=-8176.0, scale=2.0)
-        act(S("XF", 14, 16), S("XF", 8, 10), AF.Identity, bias=-1024.0)
-        tt(S("XF", 10, 12), S("XF", 12, 14), S("XF", 14, 16), A.max)
+        scan(S("W2"), S("MD", 0, 64), S("p7", 0, 64), 0.0, A.add, A.max)
+        ts(S("OK", 0, 4), S("W2", 15, 64, 16), OFD, 8192.0 / SC2, A.is_ge, A.mult)
+        ts(S("XF", 0, 8), S("NO", 0, 8), -1.0 / SC2, 8192.0 / SC2, A.mult, A.add)
+        ts(S("XF", 8, 10), do, -0.75 / SC2, col("CF", 17 + t), A.mult, A.add)
+        if not lastr:
+            act(S("XF", 12, 14), S("XF", 8, 10), AF.Identity, bias=-8176.0 / SC2, scale=2.0)
+            act(S("XF", 14, 16), S("XF", 8, 10), AF.Identity, bias=-1024.0 / SC2)
+            tt(S("XF", 10, 12), S("XF", 12, 14), S("XF", 14, 16), A.max)
         for h in range(2):
             ts(S("XP", h, 12, 2), S("XF", h, 12, 2), col("OK", h), col("OK", 2 + h), A.min, A.min)
-            ts(S("XM", h, 12, 2), S("XP", h, 12, 2), CC2 - 8192.0, col("CM", 256 * h + 255), A.add, A.min)
+            ts(S("XM", h, 12, 2), S("XP", h, 12, 2), (CC2 - 8192.0) / SC2, col("CM", 256 * h + 255), A.add, A.min)
         tt(S("XN"), S("XM"), S("DUM"), A.max)
-        ts(S("SO"), S("XN"), -1.0, CC2, A.mult, A.add)
-        tt(S("KP"), S("CN"), S("DD"), A.not_equal)
+        ts(S("SO"), S("XN"), -SC2, CC2, A.mult, A.add)
+        tt(S("KP"), S("CN") if lastr else IND(S("NE"), S("NO", 0, 8)), S("DD"), A.not_equal)
         act(S("LH", 0, 32), S("p0", 0, 32), AF.Identity, bias=512.5 * 512, scale=512.5)
         act(S("LH", 32, 64), S("p0", 32, 64), AF.Abs, scale=511.5)
         if not lastr:
@@ -676,37 +774,38 @@ def rank_program(g, core, T, topo):
             tt(S("N2", 0, 64), S("N1", 0, 64), S("p2", 0, 64), A.min)
             tt(IND(S("NOUT"), S("SO", 4, 8)), S("N1", 64, 128), S("C3"), A.add)
             tt(IND(S("NOUT"), S("SO", 0, 4)), S("N2", 0, 64), S("C3"), A.add)
-        act(S("SG"), S("KEY"), AF.Sign, bias=col("AC", 1 if t == 0 else 3 + t))
         mm([(S("p4", 0, 256), S("I1"), S("LN", 576 * t + 288, 576 * t + 544), True, False), (S("p4", 0, 256), S("I1"), S("SG"), False, True)])
         act(S("T2", 0, 256), S("p4", 0, 256), AF.Relu, bias=-12.0)
         act(S("T2", 256, 512), IND(S("T2", 0, 256), S("POFF")), AF.Relu, bias=63.0, scale=-1.0)
         low = -((5 * t - CUT) // 12)
-        act(S("YW", LOW + 10 * t, CUT + HIGH, 24), S("T2", 256, 256 + low), AF.Identity, bias=63.0, scale=-1.0)
-        act(S("YW", HIGH + 5 * t + 12 * low, NONE + 1, 12), S("T2", 256 + low, 512), AF.Identity, bias=63.0, scale=-1.0)
+        if lastr:
+            act(S("W", 16 + 5 * t, 3088, 12), S("T2", 256, 512), AF.Identity, bias=63.0, scale=-1.0)
+        else:
+            act(S("YW", LOW + 10 * t, CUT + HIGH, 24), S("T2", 256, 256 + low), AF.Identity, bias=63.0, scale=-1.0)
+            act(S("YW", HIGH + 5 * t + 12 * low, NONE + 1, 12), S("T2", 256 + low, 512), AF.Identity, bias=63.0, scale=-1.0)
         ts(S("NO", 8, 10), S("WR", 143, 160, 16), CKA, None, A.add)
         tt(S("YS"), IND(S("YA", 4096, 8192), S("NO", 8, 10)), S("YE"), A.add)
         ts(S("YI"), S("YS"), 0.5, -0.25, A.mult, A.add)
-        cp(IND(S("YW"), S("SO", 10, 12)), S("YI"))
+        cp(IND(S("W"), S("SO", 8, 10)) if lastr else IND(S("YW"), S("SO", 10, 12)), S("YI"))
         tt(IND(S("ENR"), S("SO", 8, 10)), S("LH", 0, 32), S("LH", 32, 64), A.subtract)
         if not lastr:
-            ts(S("GO"), S("XN", 8, 10), CC2 - 3087.5, None, A.is_gt)
-            mm([(S("p1", 0, 1), S("O1"), col("GO", 0), True, False), (S("p1", 0, 1), S("O1"), col("GO", 1), False, True)])
-            ts(col("AI", 2 * t), S("p1", 0, 1), col("AC", 2 + t), None, A.add)
-            if t == 0:
-                cp(col("AC", 3), col("AI", 0))
+            ts(S("GO", 2 * t, 2 * t + 2), S("XN", 8, 10), (CC2 - 3087.5) / SC2, None, A.is_gt)
+            mm([(S("p6", 0, 1), S("O1"), col("GO", x), x == 0, x == 2 * t + 1) for x in range(2 * t + 2)])
+            cp(col("AI", 2 * t), S("p6", 0, 1))
             ts(col("AI", 2 * t + 1), col("AI", 2 * t), 31, None, A.bitwise_and)
             ts(col("AC", 4 + t), col("AI", 2 * t + 1), -2048.0, col("AC", 1), A.mult, A.add)
-    act(col("YW", NONE), col("SVC", 0), AF.Identity)
-    cp(S("YL"), S("YW", LOW, CUT + HIGH, 2))
-    dma("s", T.y1[:, CUT:], S("YW", CUT + HIGH, NONE + 1), 4500)
-    dma("s", T.y1[:, 0:CUT], S("YL"), 3200)
+    dma("s", T.y1[:, 0:1536], S("W", 16, 1552), 4500)
+    dma("a", T.y1[:, 1536:3072], S("W", 1552, 3088), 4500)
     dma("a", T.ne1[:], S("NOUT", 0, 512), 2500)
     dma("s", T.ends1[:], S("ENR", 16, 3088, part=slice(0, 128, 16)), 2500)
 
     n = len(ops)
     if "start" not in ORDER:
         ORDER["start"] = arrange(ops)
-    start = ORDER["start"]
+    start, where = ORDER["start"]
+    for o, e in zip(ops, where):
+        if e != o["eng"]:
+            o["eng"], o["fn"], o["cost"] = o["alt"]
     order = sorted(range(n), key=lambda i: (start[i], i))
     done_at = [start[i] + ops[i]["cost"] for i in range(n)]
     queue = {"v": g.vector, "a": g.scalar, "p": g.tensor, "g": g, "s": g.sync}
@@ -720,7 +819,7 @@ def rank_program(g, core, T, topo):
     for i in order:
         o = ops[i]
         e = o["eng"]
-        if e == "x":
+        if e in "xd":
             clock[i] = {o["sem"]: o["val"]}
             continue
         kn = known[e]
@@ -740,6 +839,8 @@ def rank_program(g, core, T, topo):
         if o["kind"] == "dma":
             ins.then_inc(T.sem[o["sem"]], 16)
             clock[i][o["sem"]] = 16
+        elif o["kind"] == "rem" and o["sem"]:
+            clock[i][o["sem"]] = o["val"]
         elif o["kind"] == "c" and needed[i]:
             o["sem"] = "s" + e
             count[o["sem"]] += 1
@@ -751,6 +852,6 @@ def rank_program(g, core, T, topo):
             g.wait_ge(T.sem[sem], v)
     g.wait_ge(T.sem.sent, sent[0])
     for o in ops:
-        if o["kind"] in ("dma", "arr"):
+        if o["kind"] in ("dma", "arr", "rem") and o["sem"]:
             g.wait_ge(T.sem[o["sem"]], o["val"])
     return ops

import numpy as np
from concourse.bass import DstId, RemoteDMATransfer
from concourse.mybir import AluOpType, AxisListType, ActivationFunctionType

A = AluOpType
AF = ActivationFunctionType
N, RO = 8, 3
L = 128
CH = [(0, 64), (64, 128), (128, 192), (192, 256), (256, 384), (384, 448), (448, 512)]
PRE = [(0, 64), (64, 128), (128, 256), (256, 512)]
YENG = "vvvvvaaaaaaaaaaa"
PENG = ("aaa", "aaa", "aaa", "aaa")
PENG0 = ("aaa", "aaa", "aaa", "aaa")
CHAINED = False
SPE = "gggggggggggggggg"
FIRST = ((0, 128), (128, 256))
MIX = 64
CNE = "v"
SELA = 16
CLIP = ((4, 5), (4,), (4,))
STAGES = (("D", 1), ("Y", 1), ("X", 0), ("SCN", 1), ("MFTE", 0), ("RUK", -1))
JOIN = ("aa", "vv")
RLAT = 3000.0


def round_plan():
    out = []
    for s in range(-3, len(CH) + 1):
        for kinds, j in STAGES:
            j += s
            if not 0 <= j < len(CH):
                continue
            lo, hi = CH[j]
            for k in kinds:
                if k == "D":
                    out += ["%s%d%d" % (x, j, b) for b in range((hi - lo) // 32) for x in "DA"]
                elif k == "Y":
                    on, b = YENG[lo // 32:hi // 32], 0
                    while b < len(on):
                        more = 2 if on[b:b + 2] in JOIN else 1
                        out.append("Y%d%d%s%d" % (j, b, on[b], more))
                        b += more
                elif k not in "NFTEMRU" or lo >= 256:
                    out.append("%s%d" % (k, j))
    return " ".join(out)


PLAN = round_plan()
GPLAN = "vvaavvaavvaavvaa"
FARE = "vvvv"
ND = 5
CEN = 256.0 * 18432
FOLD = 40.0
BIGK = 10485760.0
KEYMAX = 4850000.0
BD = 8192.0
LIM = 12000000.0
SC2 = 1048576.0
CC2 = 131072.0
CUT, LOW, HIGH, NONE = 1024, 16, 1040, 4111

F32, BF, I32, U16, F16 = "float32", "bfloat16", "int32", "uint16", "float16"
SB = {
    "YW": (4160, BF), "YL": (1024, BF), "W": (3136, BF), "ENR": (3136, F32), "SVC": (8, BF),
    "EB": (192, I32), "EBF": (192, F32), "EI": (384, I32), "PC": (384, BF),
    "NEI": (512, I32), "NEO": (512, U16), "NE": (640, F32), "FAR": (640, F32), "NOUT": (640, F32),
    "RM": (24, F32), "SEL": (2048, BF), "RST": (16 * L, BF), "TR": (2 * 16 * 544, BF), "O4K": (128, BF), "ON256": (128, BF),
    "LN": (3 * 576, BF), "IN64": (128, BF), "UVO": (3 * 64, U16), "UV": (3 * 512, BF),
    "RI": (3 * 4096, BF),
    "AO": (512, U16), "CO": (512, U16), "SS": (512, BF), "X1": (512, F16), "X2": (512, F16), "XA": (1024, F16), "SEP": (1024, BF),
    "AB": (8192, F16), "MN": (8192, F16), "YA": (8192, BF), "MM": (8192, BF), "RR": (4096, BF),
    "PEN": (256, BF), "F2": (256, BF), "K2": (256, F32), "SC": (512, F32),
    "SG": (256, BF), "T2": (512, BF),
    "IOT": (144, F32), "C3": (64, F32), "QG": (128, BF), "T16": (128, BF), "LI": (144, F32), "LID": (768, F32),
    "BBI": (128, BF), "BB": (384, BF), "CX": (512, BF), "JJ": (256, BF), "BE": (144, BF),
    "I1": (128, BF), "IN1": (128, BF), "IN8": (128, BF), "IBG": (128, BF),
    "O1": (128, BF), "O256": (128, BF), "ONB": (128, BF), "OKW": (128, BF), "TRI": (128, BF),
    "MMN": (128, BF), "MMX": (128, BF), "E1": (128, BF), "E2": (128, BF), "MD": (128, BF),
    "PI": (8, I32), "CF": (32, F32), "LOFF": (96, U16), "POFF": (16, U16), "DUM": (12, F32),
    "THI": (8, I32), "THF": (8, F32), "THB": (8, F32), "AC": (16, F32), "AI": (8, I32),
    "Q": (16, I32), "OFF": (10, U16), "KE": (32, F32), "TT": (32, F32), "MV": (32, F32), "EQ": (32, BF), "SL": (32, BF),
    "SX": (32, BF), "VP": (96, BF), "PS": (32, BF), "YE": (32, BF), "DD": (128, F32),
    "WR": (192, F32), "NO": (10, U16), "AX": (1024, BF), "CM": (1024, BF),
    "CN": (128, F32), "CR": (128, F32), "EM": (64, BF), "KP": (128, F32), "IF": (128, F32), "CB": (192, BF),
    "TRN": (128, BF), "ON1": (128, BF), "N1": (128, F32), "N2": (128, F32),
    "W2": (64, F32), "OK": (8, F32), "XF": (16, F32), "XP": (12, F32), "XM": (12, F32), "XN": (12, F32), "SO": (12, U16),
    "YS": (32, F32), "YI": (32, I32), "LH": (96, F32), "GO": (4, BF),
}
SCRATCH = {k: ("sbuf", [128, w], d) for k, (w, d) in SB.items()}
for _i in range(8):
    SCRATCH["p%d" % _i] = ("psum", [128, 512], F32)
SEMAPHORES = ["sv", "sa", "sp", "sg", "sent"] + ["d%d" % i for i in range(70)] + ["ln%d" % t for t in range(RO)] \
    + ["in%d" % i for i in range(30)] + ["out%d" % i for i in range(30)]

CYC, GATH, SCAT = 0.95, 1.55, 3.5
PCYC = 0.5
WAKE = 150.0
PASSES = 150
JOG = 1500.0
REACH = 10000.0
SEED = 2
SWAPS = 17000
FLIP = 0.3
EASE = 250.0
ORDER = {}


def arrange(ops):
    n = len(ops)
    busy = [o["busy"] for o in ops]
    pred, succ = [[] for _ in ops], [[] for _ in ops]
    for k, o in enumerate(ops):
        for i in o["hard"] | o["soft"]:
            lag = ops[i]["cost"] + WAKE if i in o["hard"] else ops[i]["cost"] if o["eng"] == "x" else busy[i]
            pred[k].append((i, lag))
            succ[i].append((k, lag + busy[k] - busy[i]))

    def place(key, before, after, first):
        at, left = list(first), [len(x) for x in before]
        pool = [(key[i], i) for i in range(n) if not left[i]]
        taken = {e: [] for e in "vapgsxd"}
        while pool:
            i = min(pool)
            pool.remove(i)
            i = i[1]
            t0 = at[i]
            row = taken[ops[i]["eng"]]
            x = len(row)
            while x and row[x - 1][1] > t0:
                x -= 1
            while x < len(row) and row[x][0] < t0 + busy[i]:
                t0 = max(t0, row[x][1])
                x += 1
            row.insert(x, (t0, t0 + busy[i]))
            at[i] = t0
            for k, lag in after[i]:
                if at[k] < t0 + lag:
                    at[k] = t0 + lag
                left[k] -= 1
                if not left[k]:
                    pool.append((key[k], k))
        return at

    fore = [[(k, lag + busy[i] - busy[k]) for k, lag in succ[i]] for i in range(n)]
    back = [[(i, lag + busy[k] - busy[i]) for i, lag in pred[k]] for k in range(n)]
    rest, span, cost = [ops[i]["cost"] - busy[i] for i in range(n)], np.array(busy), np.array([o["cost"] for o in ops])
    key, best = -np.arange(n), None
    rng = np.random.RandomState(SEED)
    for p in range(PASSES):
        path = np.array(place(key.tolist(), succ, back, rest))
        fw = np.array(place((-path - span).tolist(), pred, fore, [0.0] * n))
        end = float((fw + cost).max())
        if best is None or end <= best[0]:
            best = (end, fw)
        if p == 0 or end <= now[0] + EASE * (1 - p / PASSES) * rng.rand():
            now = (end, fw)
        near = np.abs(now[1] - now[0] * rng.rand()) < REACH * rng.rand()
        key = -now[1] - span - JOG * rng.rand() * rng.rand(n) * near * (rng.rand(n) < 0.3)
    eng, cost = [o["eng"] for o in ops], cost.tolist()

    def run(seq):
        at, by, free, last = [0.0] * n, [None] * n, {}, {}
        for k in seq:
            t0, why = free.get(eng[k], 0.0), (last.get(eng[k]), True)
            for i, lag in pred[k]:
                if at[i] + lag > t0:
                    t0, why = at[i] + lag, (i, False)
            at[k], by[k], free[eng[k]], last[eng[k]] = t0, why, t0 + busy[k], k
        k = max(seq, key=lambda i: at[i] + cost[i])
        end, held = at[k] + cost[k], []
        while k is not None:
            if by[k][1] and by[k][0] is not None:
                held.append((by[k][0], k))
            k = by[k][0]
        return end, at, held, seq

    def other(i):
        eng[i], cost[i] = ops[i]["alt"][0::2] if eng[i] == ops[i]["eng"] else (ops[i]["eng"], ops[i]["cost"])
        busy[i] = cost[i]
        for k, _lag in succ[i]:
            pred[k] = [(x, cost[i] + WAKE if x == i else lag) for x, lag in pred[k]]

    now = best = run(sorted(range(n), key=lambda i: (best[1][i], i)))
    where = list(eng)
    for p in range(SWAPS):
        j, k = now[2][rng.randint(len(now[2]))]
        seq, moved = now[3], None
        if ops[j]["alt"] and rng.rand() < FLIP:
            moved = j
            other(j)
        else:
            a, b = seq.index(j), seq.index(k)
            part = seq[a:b + 1]
            if rng.rand() < 0.5:
                lead = {k}
                for i in part[-2::-1]:
                    if any(x in lead for x, _lag in succ[i]):
                        lead.add(i)
            else:
                lead = {j}
                for i in part[1:]:
                    if any(x in lead for x, _lag in pred[i]):
                        lead.add(i)
                lead = set(part) - lead
            if j in lead or k not in lead:
                continue
            seq = seq[:a] + [i for i in part if i in lead] + [i for i in part if i not in lead] + seq[b + 1:]
        new = run(seq)
        if new[0] <= now[0] + EASE * (1 - p / SWAPS) * rng.rand():
            now = new
            if now[0] < best[0]:
                best, where = now, list(eng)
        elif moved is not None:
            other(moved)
    ORDER["end"] = best[0]
    return best[1], where


def rank_program(g, core, T, topo):
    rank = T.rank_of(core)
    if rank is None:
        return
    ops = []
    last_w, readers, bank_last = {}, {}, {}
    masks = {}
    boost, chain, tail = [0.0], [False], {}

    def S(name, a=None, b=None, s=None, part=None):
        w = 512 if name not in SB else SB[name][0]
        a = 0 if a is None else a
        b = w if b is None else b
        key = (a, b, s)
        if key not in masks:
            masks[key] = ((1 << (b - a)) - 1) << a if s is None else sum(1 << c for c in range(a, b, s))
        cols = slice(a, b) if s is None else slice(a, b, s)
        t = T[name]
        return {"ap": t[:, cols] if part is None else t[part, cols], "acc": [(name, masks[key])],
                "n": len(range(a, b, s or 1)), "dt": F32 if name not in SB else SB[name][1], "ps": name not in SB, "ind": False}

    def IND(win, off):
        return {"ap": win["ap"].indirect(off["ap"]), "acc": win["acc"], "off": off["acc"], "n": 16 * off["n"],
                "dt": win["dt"], "ps": False, "ind": True}

    def add(eng, fn, outs, ins, cost, kind="c", sem=None, val=0, busy=None):
        i = len(ops)
        hard, soft = set(), set()
        rd = [x for v in ins if isinstance(v, dict) for x in v["acc"] + v.get("off", [])]
        rd += [x for v in outs for x in v.get("off", [])]
        wr = [x for v in outs for x in v["acc"]]
        for name, m in rd + wr:
            if name not in SB:
                j = bank_last.get(name)
                if j is not None and j != i:
                    (soft if ops[j]["eng"] == eng else hard).add(j)
                bank_last[name] = i
        for name, m in rd:
            hard.update(j for j, mm in last_w.get(name, []) if mm & m)
        for name, m in wr:
            for j, mm in last_w.get(name, []) + readers.get(name, []):
                if mm & m and j != i:
                    (soft if eng == "p" and ops[j]["eng"] == "p" else hard).add(j)
        for name, m in rd:
            readers.setdefault(name, []).append((i, m))
        for name, m in wr:
            last_w[name] = [(j, mm & ~m) for j, mm in last_w.get(name, []) if mm & ~m] + [(i, m)]
            readers[name] = [(j, mm & ~m) for j, mm in readers.get(name, []) if mm & ~m or j == i]
        ops.append({"eng": eng, "fn": fn, "hard": hard, "soft": soft - hard, "cost": cost, "kind": kind, "tag": wr[0][0] if wr else "", "sem": sem, "val": val,
                    "busy": cost if busy is None else busy, "alt": None})
        if chain[0]:
            if eng in tail and tail[eng] not in hard:
                ops[i]["soft"].add(tail[eng])
            tail[eng] = i
        return i

    def val(x):
        return x["ap"] if isinstance(x, dict) else x

    def vcost(out, ins, two=False, fast=True):
        n = max(v["n"] for v in ins + [out])
        if out["ind"]:
            return 50 + out["n"] * SCAT * CYC
        if any(v["ind"] for v in ins):
            return 50 + out["n"] * GATH * CYC
        n = out["n"] if len(ins) == 0 else ins[0]["n"]
        f = 0.5 if fast and all(v["dt"] in (BF, F16, U16) for v in ins + [out]) else 1.0
        if two and not any(v["ps"] for v in ins):
            f *= 2
        return 30 + max(64, n * f) * CYC

    def ts(out, in0, s1, s2, op0, op1=None):
        if (op0, op1) in ((A.mult, A.add), (A.mult, None)) and not chain[0] and all(v["dt"] in (F32, BF) and not v["ps"] for v in (out, in0)):
            return lin("v", out, in0, s1, s2 or 0.0)

        def fn():
            if op1 is None:
                return g.vector.tensor_scalar(out["ap"], in0["ap"], val(s1), None, op0)
            return g.vector.tensor_scalar(out["ap"], in0["ap"], val(s1), val(s2), op0, op1)
        return add("v", fn, [out], [in0, s1, s2], vcost(out, [in0]))

    def tt(out, in0, in1, op):
        return add("v", lambda: g.vector.tensor_tensor(out["ap"], in0["ap"], in1["ap"], op), [out], [in0, in1], vcost(out, [in0, in1], True))

    def cp(out, in0):
        return add("v", lambda: g.vector.tensor_copy(out["ap"], in0["ap"]), [out], [in0], vcost(out, [in0]))

    def ms(out, c):
        return add("v", lambda: g.vector.memset(out["ap"], c), [out], [], vcost(out, []))

    def scan(out, d0, d1, init, op0, op1):
        return add("v", lambda: g.vector.tensor_tensor_scan(out["ap"], d0["ap"], d1["ap"], val(init), op0, op1), [out], [d0, d1, init], vcost(out, [d0, d1]))

    def red(out, in0, op):
        return add("v", lambda: g.vector.tensor_reduce(out["ap"], in0["ap"], AxisListType.X, op), [out], [in0], vcost(out, [in0], False, False))

    def tr(out, in0):
        return add("v", lambda: g.vector.transpose(out["ap"], in0["ap"]), [out], [in0], vcost(out, [in0]))

    def acost(in0):
        return 65 + max(64, in0["n"] * (GATH if in0["ind"] else 1)) * CYC

    def act(out, in0, f, bias=0.0, scale=1.0):
        if f == AF.Identity and not out["ps"] and not in0["ps"]:
            return lin("a", out, in0, scale, bias)
        return add("a", lambda: g.scalar.activation(out["ap"], in0["ap"], f, bias=val(bias), scale=val(scale)), [out], [in0, bias, scale], acost(in0))

    def lin(eng, out, in0, scale, bias):
        on = {"v": (lambda: g.vector.tensor_scalar(out["ap"], in0["ap"], val(scale), val(bias), A.mult, A.add), vcost(out, [in0])),
              "a": (lambda: g.scalar.activation(out["ap"], in0["ap"], AF.Identity, bias=val(bias), scale=val(scale)), acost(in0))}
        i = add(eng, on[eng][0], [out], [in0, scale, bias], on[eng][1])
        ops[i]["alt"] = ("a",) + on["a"] if eng == "v" else ("v",) + on["v"]
        return i

    def mm(items):
        def fn():
            r = None
            for o, l, x, st, sp in items:
                r = g.tensor.matmul(o["ap"], l["ap"], x["ap"], st, sp)
            return r
        return add("p", fn, [it[0] for it in items], [it[1] for it in items] + [it[2] for it in items],
                   40 + sum(max(64, it[2]["n"]) * (4 if it[2]["dt"] == F32 else 1) for it in items) * PCYC)

    def iota(out, pat, base, cm):
        def fn():
            if out["dt"] == I32:
                return g.iota(out["ap"], pat, base, cm)
            return g.iota(out["ap"], pat, base, cm, allow_small_or_imprecise_dtypes=True)
        return add("g", fn, [out], [], 130 + 2 * out["n"] * CYC)

    def pick(out, in0, op, fill):
        return add("g", lambda: g.affine_select(out["ap"], in0["ap"], [[1, 128]], op, fill, 0, -1), [out], [in0], 170 + 256 * CYC)

    def spread(out, in0):
        return add("g", lambda: g.affine_select(out["ap"], in0["ap"], [[0, in0["n"]]], A.is_equal, 0.0, 0, 0), [out], [in0], 170 + 2 * in0["n"] * CYC)

    ndma = [0]

    def dma(eng, out, in0, cost, slow=False):
        sem = "d%d" % ndma[0]
        ndma[0] += 1
        q = {"s": g.sync, "a": g.scalar, "g": g}[eng]

        def fn():
            if slow:
                return q.dma_start(val(out), val(in0), allow_slow_non_contiguous=True)
            return q.dma_start(val(out), val(in0))
        return add(eng, fn, [out] if isinstance(out, dict) else [], [in0], cost, "dma", sem, 16, 1000 if eng == "g" else 100)

    def both(pairs, on, cost):
        i, j = [dma(e, out, in0, cost) for e, (out, in0) in zip(on, pairs)]
        ops[j]["hard"].discard(i)
        ops[j]["hard"].update(ops[i]["hard"])
        last_w[ops[j]["tag"]].append((i, last_w[ops[j]["tag"]][-1][1]))

    def col(name, c):
        return S(name, c, c + 1)

    dma("s", S("EB"), T.ends0[:], 2200)
    dma("a", S("NEI"), T.ne0[:], 2500)
    dma("s", S("YL"), T.y0[:, 0:CUT], 3200)
    dma("s", S("YW", CUT + HIGH, NONE + 1), T.y0[:, CUT:], 4500)
    chain[0] = True
    iota(col("PI", 0), [[0, 1]], 0, 1)
    iota(S("QG"), [[1, 8], [0, 16]], 0, 0)
    iota(S("T16"), [[0, 8], [1, 16]], 0, 0)
    iota(S("LI", 0, 48), [[5, 3], [12, 16]], 16, 0)
    iota(S("IOT"), [[1, 144]], 0, 0)
    iota(S("CX"), [[1, 512]], -256, 0)
    chain[0] = False
    iota(S("JJ"), [[1, 256]], 0, 0)
    iota(S("CB", 128, 192), [[0, 64]], 300, 0)
    iota(dict(S("YW", LOW + 1, CUT + HIGH, 2), acc=S("YW", LOW, CUT + HIGH)["acc"]), [[0, CUT]], 0, 0)
    RF, GF = col("CF", 0), col("CF", 1)
    R15, R192, R16, G16, R1, R1W, INI, INX, NBC, KB, COF, CBI, CKA, CYO, OFD = [col("CF", c) for c in range(2, 17)]
    boost[0] = 2e6
    chain[0] = True
    ms(S("W", 0, 768), 0.0)
    ts(col("PI", 1), col("PI", 0), 15, None, A.bitwise_and)
    ts(col("PI", 2), col("PI", 0), 4, None, A.logical_shift_right)
    ms(S("YW", 0, 16), 255.0)
    cp(S("CF", 0, 2), S("PI", 1, 3))
    ms(S("YW", NONE + 1, 4160), 0.0)
    ts(S("O1"), S("QG"), GF, None, A.is_equal)
    ts(S("RM", 0, 16), S("T16", 0, 16), RF, None, A.is_equal)
    ts(col("CF", 20), RF, 15.0, 2304.0, A.is_equal, A.mult)
    ts(R192, RF, 192.0, None, A.mult)
    ms(S("W", 768, 3136), 0.0)
    ts(S("EI", 0, 192), S("EB"), 10, None, A.logical_shift_right)
    ts(S("EI", 192, 384), S("EB"), 1023, None, A.bitwise_and)
    ts(S("PC", 0, 191), S("EI", 0, 191), -256.0, None, A.add)
    ts(col("PC", 191), col("EI", 191), -256.0, col("CF", 20), A.add, A.add)
    ts(S("PC", 192, 384), S("EI", 192, 384), -256.0, None, A.add)
    chain[0] = False
    ts(S("LOFF", 0, 48), S("LI", 0, 48), R192, None, A.add)
    ts(S("LI", 48, 96), S("LOFF", 0, 48), 2.0, -16.0, A.mult, A.add)
    ts(S("LI", 96, 144), S("LOFF", 0, 48), 1024.0, None, A.add)
    tt(S("LI", 0, 48), S("LI", 48, 96), S("LI", 96, 144), A.min)
    cp(S("LOFF", 48, 96), S("LI", 0, 48))
    cp(S("YW", LOW, CUT + HIGH, 2), S("YL"))
    ts(S("NEO"), S("NEI"), 16.0, None, A.add)
    ts(G16, GF, 16.0, 15.0, A.mult, A.add)
    ts(S("BE"), S("IOT", 0, 144), G16, 8192.0, A.is_equal, A.mult)
    ts(S("NE", 0, 512), S("NEI"), -3071.0, None, A.add)
    chain[0] = False
    act(S("p7"), S("NE", 0, 512), AF.Relu, bias=-2047.0, scale=-1.0)
    tt(S("NE", 0, 512), S("NE", 0, 512), S("p7"), A.subtract)
    ms(S("NE", 512, 640), 0.0)
    ms(S("FAR", 512, 640), 0.0)
    chain[0] = False
    boost[0] = 1e6
    for m in range(16 if MIX else 2):
        lin("a" if m < SELA else "v", S("SEL", 128 * m, 128 * m + 128), S("O1"), col("RM", m), 0.0)
    boost[0] = 0.0
    tt(S("RM", 16, 24), S("RM", 0, 16, 2), S("RM", 1, 16, 2), A.add)
    for m in range(8):
        lin("v" if MIX else "a", S("SEP", 128 * m, 128 * m + 128), S("O1"), col("RM", 16 + m), 0.0)
    ts(R15, RF, 15.0, None, A.is_equal)
    ts(R16, RF, 16.0, None, A.mult)
    ts(R1, RF, 1.0, None, A.add)
    ts(R1W, R15, -16.0, R1, A.mult, A.add)
    ts(INI, R15, BIGK, KEYMAX - BIGK, A.mult, A.add)
    ts(INX, R15, -BIGK, BIGK - KEYMAX, A.mult, A.add)
    ts(KB, RF, 0.5, 0.25, A.mult, A.add)
    ts(COF, R15, BD, 1280.0 - BD, A.mult, A.add)
    ts(CKA, R15, BD, -BD, A.mult, A.add)
    ts(S("BB", 256, 384), S("T16"), 0.0, CKA, A.mult, A.subtract)
    for t in range(RO):
        ts(col("CF", 17 + t), RF, -191.25 / SC2, (8176.0 - 5 * t) / SC2, A.mult, A.add)
    ts(OFD, R15, -BD, BD + 256.5, A.mult, A.add)
    ts(S("POFF"), S("IOT", 0, 16), R16, None, A.add)
    ts(S("XM", 0, 8), S("IOT", 0, 128, 16), RF, 512.0, A.add, A.add)
    ts(S("XM", 8, 10), S("IOT", 0, 32, 16), RF, 3088.0, A.add, A.add)
    ts(S("XM", 10, 12), S("IOT", 0, 32, 16), RF, NONE + 1.0, A.add, A.add)
    ts(S("DUM"), S("XM"), -1.0 / SC2, CC2 / SC2, A.mult, A.add)
    ms(S("CF", 24, 28), 1.0 / 256)
    for nm, c in (("O256", 256.0), ("ONB", -1024.0), ("OKW", RF), ("O4K", 4096.0), ("ON256", -256.0), ("ON1", -1.0)):
        ts(S(nm), S("QG"), GF, c, A.is_equal, A.mult)
    chain[0] = True
    pick(S("I1"), S("O1"), A.is_equal, 0.0)
    for nm, c in (("IN8", -8192.0), ("IN64", -64.0), ("IN1", -1.0)):
        pick(S(nm), S("I1"), A.not_equal, c)
    chain[0] = False
    ts(S("E1", 0, 128), S("T16", 0, 128), RF, BIGK, A.is_equal, A.mult)
    ts(S("E2", 0, 128), S("T16", 0, 128), R1W, BIGK, A.is_equal, A.mult)
    tt(S("MMN"), S("E1", 0, 128), S("E2", 0, 128), A.subtract)
    tt(S("MMX"), S("E2", 0, 128), S("E1", 0, 128), A.subtract)
    ts(S("E1"), S("T16"), RF, -3 * BD, A.is_equal, A.mult)
    ts(S("E2"), S("T16"), R1, BD, A.is_equal, A.mult)

    tt(S("MD"), S("E1"), S("E2"), A.add)
    boost[0] = 2e6
    both([(S("W", 16, 3088, part=slice(s, 128, 16)), S("PC", 192 * s, 192 * s + 192)) for s in range(2)], "sa", 2200)
    for t in range(RO):
        act(S("LN", 576 * t + 288, 576 * t + 544), IND(S("YW"), S("LOFF", 48 + 16 * t, 64 + 16 * t)), AF.Identity, bias=12.0)
        act(S("LN", 576 * t + 544, 576 * t + 576), S("PC", 5 * t, 384, 12), AF.Identity)
        ts(S("UVO", 64 * t + 32, 64 * t + 64), S("LN", 576 * t + 544, 576 * t + 576), 256.0, None, A.add)
    cp(col("SVC", 0), col("YW", NONE))
    ms(col("YW", NONE), 255.0)
    boost[0] = 0.5e6
    for c in range(8):
        on = GPLAN[2 * c:2 * c + 2]
        for e, a, b in [(on[0], 64 * c, 64 * c + 64)] if on[0] == on[1] else [(on[0], 64 * c, 64 * c + 32), (on[1], 64 * c + 32, 64 * c + 64)]:
            lin(e, S("MM", 16 * a, 16 * b), IND(S("W"), S("NEO", a, b)), 1.0, 0.0)
        pb = S("p%d" % (c // 2), 64 * (c % 2), 64 * (c % 2) + 64)
        mm([(pb, S("IN8"), S("CX", 64 * c, 64 * c + 64), True, False), (pb, S("IN8"), S("CB", 128, 192), False, False)]
           + [(pb, S("BE", 15 - k, 143 - k), S("MM", 1024 * c + k, 1024 * c + 1024, 16), False, k == 15) for k in range(16)])
        if c % 2 and FARE[c // 2] == "a":
            act(S("FAR", 64 * c - 64, 64 * c + 64), S("p%d" % (c // 2), 0, 128), AF.Relu, scale=-1.0 / 8192)
        elif c % 2:
            ts(S("FAR", 64 * c - 64, 64 * c + 64), S("p%d" % (c // 2), 0, 128), -1.0 / 8192, 0.0, A.mult, A.max)
    boost[0] = 0.0
    peers = [T.cores[(rank + 1 + t) % N] for t in range(RO)]
    backs = [T.cores[(rank - 1 - t) % N] for t in range(RO)]
    sent = [0]

    def send_lanes():
        trs, at = [], 0
        for t in range(RO):
            en = topo.engines(core, peers[t])
            k = len(en) // 2 if t == 0 else len(en) // 4
            rid, pid, _s = topo.addr(peers[t])
            trs.append(RemoteDMATransfer(dst_ids=[DstId(rid=rid, pnc=pid)], dma_engine_mask=sum(1 << e for e in en[at:at + k]),
                                         remote_sem=T.sem["ln%d" % t], src=T.LN[:, 576 * t + 288:576 * t + 576], dst=T.LN[:, 576 * t:576 * t + 288]))
            at += k
        sent[0] += at
        return g.remote_dma_fused(trs, local_sem=T.sem.sent)
    js = add("g", send_lanes, [], [S("LN", 576 * t + 288, 576 * t + 576) for t in range(RO)], 5500, "rem", busy=3200)
    iota(S("RST", 0, 4 * L), [[0, L // 4], [-16384, 16]], 16384, 0)
    for x in range(1, 4):
        dma("s", S("RST", 4 * L * x, 4 * L * x + 4 * L), S("RST", 0, 4 * L), 2500)
    dma("g", S("THI", part=slice(0, 1)), T.th[:], 2500, True)
    dma("g", S("ENR", 16, 3088), T.y0[:], 9000)
    iota(S("BBI"), [[0, 4], [1, 2], [2, 16]], 0, 0)
    for t in range(RO):
        iota(S("LID", 256 * t, 256 * t + 256), [[12, 16], [192, 16]], 5 * t - 3071, 0)
        for r in range(16 if t < RO - 1 else 0):
            c = min(16, max(0, -((192 * r + 5 * t - CUT) // 12)))
            if c:
                iota(S("LID", 256 * t + r, 256 * t + 16 * c, 16), [[24, c]], 2 * (192 * r + 5 * t) + LOW - NONE, 0)
    pick(S("IBG"), S("I1"), A.not_equal, 16777216.0)
    ts(S("AX", 0, 128), S("QG"), GF, -CEN / 32, A.is_equal, A.mult)
    pick(S("AX", 128, 256), S("AX", 0, 128), A.is_gt, 0.0)
    pick(S("TRI"), S("AX", 128, 256), A.not_equal, CEN / 64)
    ts(S("TRN"), S("TRI"), -1.0, None, A.mult)
    spread(S("IF"), S("I1"))
    iota(S("CB", 0, 128), [[0, 128]], int(CEN) // 64, 0)
    iota(S("C3"), [[0, 64]], 3071, 0)
    iota(S("ENR", 0, 16), [[0, 16]], 0, 0)
    iota(S("ENR", 3088, 3136), [[0, 48]], 0, 0)
    iota(S("NOUT", 512, 640), [[0, 128]], 0, 0)
    chain[0] = False
    ts(S("BB", 0, 128), S("BBI"), 1.0 / 128, None, A.mult)
    ts(S("BB", 128, 256), S("BBI"), 1.0 / 128, 0.125, A.mult, A.add)
    for t in range(RO):
        ne_t = len(topo.engines(backs[t], core))
        j = add("x", None, [S("LN", 576 * t, 576 * t + 288)], [], 0, "arr", "ln%d" % t, ne_t // 2 if t == 0 else ne_t // 4)
        ops[j]["soft"].add(js)
        ts(S("UVO", 64 * t, 64 * t + 32), S("LN", 576 * t + 256, 576 * t + 288), 256.0, None, A.add)
    def own_ends(t, pb):
        mm([(S(pb, 256 * s + r, 256 * s + 256, 16), S("SEL", 128 * s, 128 * s + 128), S("W", 16 + 192 * r + 5 * t, 208 + 192 * r, 12), True, True)
            for s in range(2) for r in range(16)])
        act(S("UV", 512 * t, 512 * t + 512), S(pb), AF.Identity)
    own_ends(0, "p6")
    cp(S("THF", part=slice(0, 1)), S("THI", part=slice(0, 1)))
    add("g", lambda: g.partition_broadcast(T.THB[:, :], T.THF[0:1, :], 128), [S("THB")], [S("THF")], 200)
    ts(S("AC", 8, 16), S("IOT", 0, 8), GF, None, A.is_equal)
    tt(S("THF"), S("AC", 8, 16), S("THB"), A.mult)
    red(col("AC", 0), S("THF"), A.add)
    ts(col("AC", 1), col("AC", 0), -256.0, CEN + 0.5, A.mult, A.add)
    cp(S("EBF"), S("EB"))
    dma("s", S("ENR", 16, 3088, part=slice(0, 128, 16)), S("EBF"), 2500)
    ring = {"d": 0, "w": 0}

    def write(to, frm, pairs, cost):
        k = ring["w"]
        ring["w"] += 1
        rid, pid, _s = topo.addr(to)
        en = topo.engines(core, to)
        cuts = [0, len(en)] if len(pairs) == 1 else [0, len(en) // 2, 3 * len(en) // 4, len(en)]

        def send():
            return g.remote_dma_fused([RemoteDMATransfer(dst_ids=[DstId(rid=rid, pnc=pid)], dma_engine_mask=sum(1 << e for e in en[a:b]), remote_sem=T.sem["in%d" % k],
                                                         srcs=[x["ap"] for x in srcs], dsts=[land["ap"]], alu_op=3 if len(srcs) > 1 else 0)
                                       for (land, srcs), a, b in zip(pairs, cuts, cuts[1:])], local_sem=T.sem["out%d" % k])
        jj = add("g", send, [], [x for _l, srcs in pairs for x in srcs], RLAT + cost, "rem", "out%d" % k, len(en), busy=1200)
        jd = add("d", None, [], [], RLAT - 1200 + cost, "way", busy=cost)
        ja = add("x", None, [land for land, _x in pairs], [], 0, "arr", "in%d" % k, len(topo.engines(frm, core)))
        ops[jd]["soft"].add(jj)
        ops[ja]["soft"].add(jd)

    for t in range(RO):
        lastr = t == RO - 1
        dbank = {}
        trb = 16 * 544 * (t % 2)
        runs = [[0, 256]] if t else [list(x) for x in FIRST]
        for j, (lo, hi) in enumerate(CH):
            if j not in CLIP[t] and lo >= 256:
                if runs[-1][1] == lo + 32:
                    runs[-1][1] = hi + 32
                else:
                    runs.append([lo + 32, hi + 32])
        for a, b in runs:
            for k in range(16):
                o, src = S("TR", trb + 16 * a + k, trb + 16 * b, 16), S("LN", 576 * t + a, 576 * t + b)
                on = SPE[k] if a > 256 and t else "g"
                if on == "g":
                    spread(o, src)
                else:
                    lin(on, o, src, 1.0, 0.0)

        def pre(kind, lo, hi):
            side, a, b = lo // 256, (lo % 256) // 16, (hi - 1) % 256 // 16 + 1
            uo = S("UVO", 64 * t + 32 * side + a, 64 * t + 32 * side + b)
            vo = S("UVO", 64 * t + 32 * side + 16 + a, 64 * t + 32 * side + 16 + b)
            on = (PENG if t else PENG0)[PRE.index((lo, hi))]
            if kind == "P":
                lin(on[0], S("SS", lo, hi), IND(S("FAR"), uo), -1.0, 300.0)
                lin(on[1], S("X1", lo, hi), IND(S("FAR"), vo), -64.0, 300.0 * 64)
            elif kind == "Q":
                lin(on[2], S("X2", lo, hi), IND(S("NE"), vo), -1.0 / 256, 1.0 / 256)
            else:
                ts(S("AO", lo, hi), IND(S("NE"), uo), float(NONE), None, A.add)

        def after_sum(j, lo, hi, kb):
            if lo < 256:
                a, b = 4096 * t + 16 * lo, 4096 * t + 16 * hi
                return write(backs[t], peers[t], [(S("RI", a, b), [S("TR", trb + 16 * lo, trb + 16 * hi), S("MM", 16 * lo, 16 * hi)])], FOLD * (hi - lo))
            a, b = lo - 256, hi - 256
            scan(S("SC", a, b), S("MMN", 0, b - a), kb, col("SC", a - 1) if a % 128 else INI, A.add, A.min)
            scan(S("SC", 256 + a, 256 + b), S("MMX", 0, b - a), kb, col("SC", 255 + a) if a % 128 else INX, A.add, A.max)
            act(S("SG", a, b), kb, AF.Sign, bias=col("AC", 1 if t == 0 else 3 + t))
            if b % 128 == 0:
                chain[0] = False
                h = a // 128
                ce, cd = col("SC", b - 1), col("SC", 255 + b)
                ts(col("Q", h), col("CF", 24), ce, -0.25 - 0.5 * h, A.mult, A.add)
                ts(S("Q", 4 + 4 * h, 8 + 4 * h), S("CF", 24, 28), cd, -0.25 - 0.5 * h, A.mult, A.add)
                ts(col("OFF", h), col("Q", h), -256.0, ce, A.mult, A.add)
                ts(S("OFF", 2 + h, 10, 2), S("Q", 4 + 4 * h, 8 + 4 * h), -256.0, cd, A.mult, A.add)
                chain[0] = CHAINED

        def step(tok):
            kind, j = tok[0], int(tok[1])
            lo, hi = CH[j]
            w = hi - lo
            nm, nb, ab = 512 // w, w // 32, 16 * (lo % 256)
            bk = int(tok[2]) if len(tok) > 2 else 0
            at = lo if lo < 256 else lo + 32
            top = S("LN", 576 * t + at, 576 * t + at + w)
            kb = S("p%d" % (5 + j % 2), 0, w)
            if kind == "U":
                ri = 4096 * t + 16 * (lo - 256)
                mm([(kb, S("I1"), S("JJ", lo - 256, hi - 256), True, False)] + [(kb, S("O4K"), top, False, False)] * (1 if j in CLIP[t] else 2) + [
                    (kb, S("IN64"), S("CB", 0, w), False, False)] + [(kb, S("ON256"), S("RI", ri + k, ri + 16 * w, 16), False, False) for k in range(16)])
            least = S("MN", 16 * lo + 15, 16 * hi, 16)
            if kind == "D":
                pb = dbank[j, bk] = "p%d" % (ring["d"] % ND)
                ring["d"] += 1
                it = []
                for x in range(nm):
                    m, o = nm * bk + x, S(pb, x, 512, nm)
                    it.append((o, S("IN64"), S("SS", lo, hi), True, False))
                    if lo < MIX:
                        it += [(o, S("SEL", 128 * m, 128 * m + 128), S(nm_, lo, hi), False, nm_ == "X2") for nm_ in ("X1", "X2")]
                    else:
                        it.append((o, S("SEP", 128 * (m // 2), 128 * (m // 2) + 128), S("XA", 512 * (m % 2) + lo, 512 * (m % 2) + hi), False, True))
                mm(it)
            elif kind == "A":
                act(S("AB", 16 * lo + bk, 16 * hi, nb), S(dbank[j, bk]), AF.Abs)
            elif kind == "S":
                scan(S("MN", 16 * lo, 16 * hi), S("RST", 0, 16 * w), S("AB", 16 * lo, 16 * hi), 0.0, A.max, A.min)
            elif kind == "C":
                ts(S("CO", lo, hi), least, -256.0, NONE + 1.0, A.mult, A.add)
            elif kind == "N":
                act(S("PEN", lo - 256, hi - 256), least, AF.Relu, bias=33554432.0, scale=-1048576.0)
            elif kind == "F":
                tt(S("F2", lo - 256, hi - 256), S("SS", lo, hi), S("UV", 512 * t + lo, 512 * t + hi), A.is_equal)
            elif kind == "K":
                after_sum(j, lo, hi, kb)
            elif kind == "E":
                act(S("K2", lo - 256, hi - 256), S("p7", lo - 256, hi - 256), AF.Identity, KB, 1.0 / 1024)
            elif kind == "Y":
                a = lo + 32 * bk
                b = a + 32 * int(tok[4])
                o, src = S("YA", 16 * a, 16 * b), IND(S("YW"), S("AO", a, b))
                lin(tok[3], o, src, 1.0, 0.0)
            elif kind == "X":
                tt(S("MM", 16 * lo, 16 * hi), IND(S("YW"), S("CO", lo, hi)), S("YA", 16 * lo, 16 * hi), A.max)
            elif kind in "MRU" and j in CLIP[t]:
                for b in range(nb if kind != "M" else 0):
                    r0 = ab + 512 * b
                    if kind == "R":
                        pb = "p%d" % (ring["d"] % ND)
                        ring["d"] += 1
                        mm([it for x in range(nm) for it in ((S(pb, w * x, w * x + w), S("I1"), top, True, False),
                                                            (S(pb, w * x, w * x + w), S("IN1"), S("MM", 16 * lo + nm * b + x, 16 * hi, 16), False, True))])
                        act(S("RR", r0, r0 + 512), S(pb), AF.Relu)
                    else:
                        mm([(kb, S("O256"), S("RR", r0 + w * x, r0 + w * x + w), False, b == nb - 1 and x == nm - 1) for x in range(nm)])
            elif kind == "M":
                tt(S("MM", 16 * lo, 16 * hi, 16), S("MM", 16 * lo, 16 * hi, 16), top, A.min)
            elif kind == "R":
                scan(S("RR", ab, ab + 16 * w), S("TR", trb + 16 * at, trb + 16 * (at + w)), S("MM", 16 * lo, 16 * hi), 0.0, A.max, A.min)
            elif kind == "U":
                mm([(kb, S("ON256"), S("RR", ab + k, ab + 16 * w, 16), False, k == 15) for k in range(16)])
            elif kind == "T":
                a, b = lo - 256, hi - 256
                pb = S("p7", a, b)
                mm([(pb, S("BE", 15 - k, 143 - k), S("YA", 16 * lo + k, 16 * hi, 16), k == 0, False) for k in range(16)]
                   + [(pb, S("IBG"), S("F2", a, b), False, False), (pb, S("I1"), S("PEN", a, b), False, True)])

        for lo, hi in PRE:
            for kind in "PQO":
                pre(kind, lo, hi)
            for odd in range(2 if lo >= MIX else 0):
                both([(S("XA", 512 * odd + lo, 512 * odd + hi, part=slice(x, 128, 2)), S(nm_, lo, hi, part=slice(odd, 128, 2)))
                      for x, nm_ in enumerate(("X1", "X2"))], "ss", 2600)
        for tok in PLAN.split():
            step(tok)
        if lastr:
            act(S("p0"), S("NE", 0, 512), AF.Identity, bias=2047.5, scale=0.5)
            act(S("NOUT", 0, 512), S("NE", 0, 512), AF.Identity, bias=3071.0)
            tt(S("NOUT", 0, 512), S("NOUT", 0, 512), S("p0"), A.max)
            dma("s", S("W", 16 + CUT, 3088), S("YW", CUT + HIGH, NONE + 1), 4000)
            cp(S("W", 16, 16 + CUT), S("YW", LOW, CUT + HIGH, 2))
            act(col("W", 3087), col("SVC", 0), AF.Identity)
        if not lastr:
            own_ends(t + 1, "p0")
        eo, do = S("OFF", 0, 2), S("OFF", 2, 4)
        uw, vw = S("UV", 512 * t, 512 * t + 256), S("UV", 512 * t + 256, 512 * t + 512)
        lin("v", S("KE"), IND(S("K2"), eo), 1.0, 0.0)
        tr(S("TT"), S("KE"))
        scan(S("MV"), S("RST", 0, 32), S("TT"), 0.0, A.max, A.min)
        for x in range(2):
            ts(S("EQ", 16 * x, 16 * x + 16), S("TT", 16 * x, 16 * x + 16), col("MV", 16 * x + 15), None, A.is_equal)
        tr(S("SL"), S("EQ"))
        act(S("VP", 0, 32), IND(vw, eo), AF.Identity)
        act(S("VP", 32, 64), IND(uw, do), AF.Identity)
        act(S("VP", 64, 96), IND(vw, do), AF.Identity)
        act(S("PS"), IND(S("JJ"), eo), AF.Identity, scale=16.0)
        act(S("YE"), IND(S("LN", 576 * t + 288, 576 * t + 544), eo), AF.Identity, bias=-12.0)
        tt(S("SX"), IND(S("SS", 256, 512), eo), S("SL"), A.mult)
        act(S("DD"), IND(S("LID", 256 * t, 256 * t + 256), S("OFF", 2, 10)), AF.Identity)
        mm([(S("p7", 0, 128), S("I1"), S("BB", 0, 128), True, False), (S("p7", 32, 128), S("I1"), S("VP"), False, False)])
        mm([(S("p1", 0, 128), S("I1"), S("BB", 128, 256), True, False), (S("p1", 0, 128), S("I1"), S("BB", 256, 384), False, False),
            (S("p1", 32, 128), S("I1"), S("VP"), False, False)])
        for pb in ("p7", "p1"):
            mm([(S(pb, 32 * x, 32 * x + 32), S("ONB"), S("SL"), False, False) for x in range(4)] + [(S(pb, 0, 32), S("O1"), S("SX"), False, True)])
        mm([(S("p3", 0, 32), S("I1"), S("PS"), True, False), (S("p3", 0, 32), S("OKW"), S("SL"), False, True)])
        scan(S("WR", 0, 128), S("MD", 0, 128), S("p7", 0, 128), 0.0, A.add, A.max)
        scan(S("WR", 128, 160), S("MD", 0, 32), S("p3", 0, 32), 0.0, A.add, A.max)
        ts(S("NO", 0, 8), S("WR", 15, 128, 16), COF, 511.0, A.add, A.min)
        for h in range(2):
            for x in range(4):
                act(S("AX", 512 * h + 128 * x, 512 * h + 128 * x + 128), S("p1", 0, 128), AF.Abs, bias=col("WR", 32 * x + 16 * h + 15), scale=-1.0)
            scan(S("CM", 256 * h, 256 * h + 256), S("AX", 512 * h, 512 * h + 256), S("AX", 512 * h + 256, 512 * h + 512), 1.0, A.min, A.min)
        mm([(S("p0", 0, 32), S("I1"), S("VP", 0, 32), True, False), (S("p0", 0, 32), S("O1"), S("SX"), False, True),
            (S("p0", 32, 64), S("IN1"), S("VP", 0, 32), True, False), (S("p0", 32, 64), S("O1"), S("SX"), False, True)])
        ts(S("EM"), IND(S("NE"), S("NO", 0, 4)), 0.0, None, A.is_equal)
        lin(CNE, S("CN"), IND(S("NOUT" if lastr else "NE"), S("NO", 0, 8)), 1.0, -3071.0 if lastr else 0.0)
        mm([(S("p7", 0, 64), S("O1"), S("EM"), True, False), (S("p7", 0, 32), S("O256"), S("SL"), False, False),
            (S("p7", 32, 64), S("O256"), S("SL"), False, True)])
        mm([(S("p2", 0, 64), S("I1"), S("CB", 0, 64), True, False), (S("p2", 0, 64), S("IF"), S("DD", 0, 64), False, False),
            (S("p2", 0, 64), S("TRN"), S("EM"), False, True)])
        if not lastr:
            mm([(S("p5", 0, 64), S("IN1"), S("CB", 0, 64), True, False), (S("p5", 0, 64), S("I1"), S("CB", 128, 192), False, False),
                (S("p5", 0, 32), S("IN1"), S("VP", 0, 32), False, False), (S("p5", 32, 64), S("ON1"), S("SX"), False, False),
                (S("p5", 0, 64), S("TRI"), S("EM"), False, True)])
        scan(S("W2"), S("MD", 0, 64), S("p7", 0, 64), 0.0, A.add, A.max)
        ts(S("OK", 0, 4), S("W2", 15, 64, 16), OFD, 8192.0 / SC2, A.is_ge, A.mult)
        ts(S("XF", 0, 8), S("NO", 0, 8), -1.0 / SC2, 8192.0 / SC2, A.mult, A.add)
        ts(S("XF", 8, 10), do, -0.75 / SC2, col("CF", 17 + t), A.mult, A.add)
        if not lastr:
            act(S("XF", 12, 14), S("XF", 8, 10), AF.Identity, bias=-8176.0 / SC2, scale=2.0)
            act(S("XF", 14, 16), S("XF", 8, 10), AF.Identity, bias=-1024.0 / SC2)
            tt(S("XF", 10, 12), S("XF", 12, 14), S("XF", 14, 16), A.max)
        for h in range(2):
            ts(S("XP", h, 12, 2), S("XF", h, 12, 2), col("OK", h), col("OK", 2 + h), A.min, A.min)
            ts(S("XM", h, 12, 2), S("XP", h, 12, 2), (CC2 - 8192.0) / SC2, col("CM", 256 * h + 255), A.add, A.min)
        tt(S("XN"), S("XM"), S("DUM"), A.max)
        ts(S("SO"), S("XN"), -SC2, CC2, A.mult, A.add)
        tt(S("KP"), S("CN") if lastr else IND(S("NE"), S("NO", 0, 8)), S("DD"), A.not_equal)
        act(S("LH", 0, 32), S("p0", 0, 32), AF.Identity, bias=512.5 * 512, scale=512.5)
        act(S("LH", 32, 64), S("p0", 32, 64), AF.Abs, scale=511.5)
        if not lastr:
            act(S("CR"), IND(S("FAR"), S("NO", 0, 8)), AF.Identity)
            tt(S("N1", 0, 64), S("CN", 0, 64), S("p2", 0, 64), A.min)
            tt(S("N2", 0, 64), S("CR", 0, 64), S("p5", 0, 64), A.max)
            tt(IND(S("FAR"), S("SO", 4, 8)), S("CR", 64, 128), S("KP", 64, 128), A.mult)
            tt(IND(S("NE"), S("SO", 4, 8)), S("CN", 64, 128), S("KP", 64, 128), A.mult)
            tt(IND(S("FAR"), S("SO", 0, 4)), S("N2", 0, 64), S("KP", 0, 64), A.mult)
            tt(IND(S("NE"), S("SO", 0, 4)), S("N1", 0, 64), S("KP", 0, 64), A.mult)
        else:
            tt(S("N1"), S("CN"), S("KP"), A.mult)
            tt(S("N2", 0, 64), S("N1", 0, 64), S("p2", 0, 64), A.min)
            tt(IND(S("NOUT"), S("SO", 4, 8)), S("N1", 64, 128), S("C3"), A.add)
            tt(IND(S("NOUT"), S("SO", 0, 4)), S("N2", 0, 64), S("C3"), A.add)
        mm([(S("p4", 0, 256), S("I1"), S("LN", 576 * t + 288, 576 * t + 544), True, False), (S("p4", 0, 256), S("I1"), S("SG"), False, True)])
        act(S("T2", 0, 256), S("p4", 0, 256), AF.Relu, bias=-12.0)
        act(S("T2", 256, 512), IND(S("T2", 0, 256), S("POFF")), AF.Relu, bias=63.0, scale=-1.0)
        low = -((5 * t - CUT) // 12)
        if lastr:
            act(S("W", 16 + 5 * t, 3088, 12), S("T2", 256, 512), AF.Identity, bias=63.0, scale=-1.0)
        else:
            act(S("YW", LOW + 10 * t, CUT + HIGH, 24), S("T2", 256, 256 + low), AF.Identity, bias=63.0, scale=-1.0)
            act(S("YW", HIGH + 5 * t + 12 * low, NONE + 1, 12), S("T2", 256 + low, 512), AF.Identity, bias=63.0, scale=-1.0)
        ts(S("NO", 8, 10), S("WR", 143, 160, 16), CKA, None, A.add)
        tt(S("YS"), IND(S("YA", 4096, 8192), S("NO", 8, 10)), S("YE"), A.add)
        ts(S("YI"), S("YS"), 0.5, -0.25, A.mult, A.add)
        cp(IND(S("W"), S("SO", 8, 10)) if lastr else IND(S("YW"), S("SO", 10, 12)), S("YI"))
        tt(IND(S("ENR"), S("SO", 8, 10)), S("LH", 0, 32), S("LH", 32, 64), A.subtract)
        if not lastr:
            ts(S("GO", 2 * t, 2 * t + 2), S("XN", 8, 10), (CC2 - 3087.5) / SC2, None, A.is_gt)
            mm([(S("p6", 0, 1), S("O1"), col("GO", x), x == 0, x == 2 * t + 1) for x in range(2 * t + 2)])
            cp(col("AI", 2 * t), S("p6", 0, 1))
            ts(col("AI", 2 * t + 1), col("AI", 2 * t), 31, None, A.bitwise_and)
            ts(col("AC", 4 + t), col("AI", 2 * t + 1), -2048.0, col("AC", 1), A.mult, A.add)
    dma("s", T.y1[:, 0:1536], S("W", 16, 1552), 4500)
    dma("a", T.y1[:, 1536:3072], S("W", 1552, 3088), 4500)
    dma("a", T.ne1[:], S("NOUT", 0, 512), 2500)
    dma("s", T.ends1[:], S("ENR", 16, 3088, part=slice(0, 128, 16)), 2500)

    n = len(ops)
    if "start" not in ORDER:
        ORDER["start"] = arrange(ops)
    start, where = ORDER["start"]
    for o, e in zip(ops, where):
        if e != o["eng"]:
            o["eng"], o["fn"], o["cost"] = o["alt"]
    order = sorted(range(n), key=lambda i: (start[i], i))
    done_at = [start[i] + ops[i]["cost"] for i in range(n)]
    queue = {"v": g.vector, "a": g.scalar, "p": g.tensor, "g": g, "s": g.sync}
    needed = [False] * n
    for o in ops:
        for j in o["hard"]:
            needed[j] = True
    count = {"sv": 0, "sa": 0, "sp": 0, "sg": 0}
    known = {e: {} for e in queue}
    clock = [None] * n
    for i in order:
        o = ops[i]
        e = o["eng"]
        if e in "xd":
            clock[i] = {o["sem"]: o["val"]}
            continue
        kn = known[e]
        want = {}
        for j in o["hard"]:
            p = ops[j]
            if kn.get(p["sem"], 0) < p["val"] and want.get(p["sem"], (0, 0))[0] < p["val"]:
                want[p["sem"]] = (p["val"], j)
        for sem, (v, j) in sorted(want.items(), key=lambda x: -done_at[x[1][1]]):
            if kn.get(sem, 0) < v:
                queue[e].wait_ge(T.sem[sem], v)
                for s2, v2 in clock[j].items():
                    if kn.get(s2, 0) < v2:
                        kn[s2] = v2
        ins = o["fn"]()
        clock[i] = dict(kn)
        if o["kind"] == "dma":
            ins.then_inc(T.sem[o["sem"]], 16)
            clock[i][o["sem"]] = 16
        elif o["kind"] == "rem" and o["sem"]:
            clock[i][o["sem"]] = o["val"]
        elif o["kind"] == "c" and needed[i]:
            o["sem"] = "s" + e
            count[o["sem"]] += 1
            o["val"] = count[o["sem"]]
            ins.then_inc(T.sem[o["sem"]], 1)
            clock[i][o["sem"]] = o["val"]
    for sem, v in count.items():
        if v:
            g.wait_ge(T.sem[sem], v)
    g.wait_ge(T.sem.sent, sent[0])
    for o in ops:
        if o["kind"] in ("dma", "arr", "rem") and o["sem"]:
            g.wait_ge(T.sem[o["sem"]], o["val"])
    return ops
